import numpy as np, ml_dtypes
CORES = [9,25,41,57]
N = 4
BF = ml_dtypes.bfloat16
V, CAP, LB, RO = 3072, 256, 3, 3
L = N * V
PL = (np.arange(N)[:, None] * V + np.arange(V)).reshape(N, 1, 1, V)
def draw(rng, size):
    s = (N, 8, 16, V)
    t = PL + 1 + (size * rng.random(s) * rng.random(s)).astype(np.int64)
    t = np.where(t > L, np.minimum(PL + 1 + ((L - PL) * rng.random(s)).astype(np.int64), L), t); z = rng.random(s)
    return np.where(z < 0.12, 0, np.where(z < 0.121, L, t))
def sizes(rng):
    a = np.array([V >> 6, V >> 5, V >> 4, V >> 3, V >> 3, V >> 2, V >> 1, 2 * V])[rng.permutation(8)]
    return (a[:, None] * np.exp2(2 * rng.random((8, 16)) - 1)).reshape(1, 8, 16, 1)
def perms(rng):
    return np.argsort(rng.random((N, 8, 16, LB)), axis=2)
def pack(t, rt):
    return {"ends": np.ascontiguousarray(t.reshape(N, 128, V)).astype(np.int32), "rights": np.ascontiguousarray(rt.reshape(N, 128, LB)).astype(np.int32)}
def setup_inputs(rng):
    return pack(draw(rng, sizes(rng)), perms(rng))
def setup_inputs_room(rng):
    t = draw(rng, np.full((1, 8, 16, 1), V >> 4)); p = np.arange(V)
    for r in range(N):
        for g in range(8):
            for b in range(LB):
                v = np.where((p == V - 1) | (rng.random(V) < 0.3), 0, r * V + p + 1 + ((V - 1 - p) * rng.random(V)).astype(np.int64))
                o = rng.permutation(V); k = 0
                for q in range(r + 1, N):
                    n = int(rng.choice(np.array([0, 1, CAP - 1, CAP, CAP + 1, 2 * CAP])))
                    if r == 0 and q == 1 and b == 0: n = (CAP, CAP + 1, 2 * CAP, CAP - 1, 1, 0, CAP, CAP + 1)[g]
                    x = rng.integers(0, V, n)
                    if n > 1: x[0] = 0; x[n - 1] = V - 1
                    v[o[k:k + n]] = q * V + x; k += n
                t[r, g, b] = v
    return pack(t, perms(rng))
def setup_inputs_alike(rng):
    t = draw(rng, sizes(rng)); p = PL.reshape(-1)
    for g in (0, 2, 4, 6):
        s = np.array([V, 1, 16, V // 4] * 4)
        if g: s = s[rng.permutation(16)]
        t[:, g] = np.minimum((PL[:, 0] // s[None, :, None] + 1) * s[None, :, None], L)
    for g in (1, 3):
        for a in range(16):
            cut = np.append(np.sort(rng.integers(1, L, 40)), L)
            t[:, g, a] = cut[np.searchsorted(cut, p, side="right")].reshape(N, V)
    rt = rng.integers(0, 16, (N, 8, 16, LB)); rt[:, 0] = np.arange(LB); rt[:, 2] = rng.choice(np.array([0, 15]), (N, 16, LB))
    return pack(t, rt)
def setup_inputs_fails(rng):
    t = draw(rng, sizes(rng)); rt = perms(rng); q = 1 + rng.permutation(7); h = V // 2; e = (N - 1) * V
    t[rng.integers(0, N), :, :LB] = 0
    t[:, 0, :LB] = 0; t[:, q[0], :LB] = 0; t[:, q[1], :LB] = L
    t[:, q[2]] = np.where(rng.random((N, 1, V)) < 0.6, 0, t[:, q[2]]); t[:, q[3], LB:] = 0
    b = int(rng.integers(0, LB))
    t[:, q[4], b] = np.where(rng.random((N, V)) < 0.1, L, 0); rt[:, q[4], b] = rng.integers(LB, 16, (N, LB))
    for s in (q[5], q[6]):
        t[:N - 1, s, :LB] = 0; t[N - 1, s, :, :h] = 0; t[N - 1, s, 0, :h] = e + h + rng.integers(0, h, h)
        for r in range(N - 1):
            o = rng.permutation(V)[:CAP]; t[r, s, 0, o] = e + rng.integers(0, h, CAP)
        rt[:N - 1, s, :, 0] = rng.integers(1, 15, (N - 1, 16))
    t[N - 1, q[6], 15, :h] = L; rt[:N - 1, q[6], 0, 0] = 15
    return pack(t, rt)
def setup_inputs_far(rng):
    t = draw(rng, np.full((1, 8, 16, 1), 8 * L))
    t[:, :, :LB] = np.where(rng.random((N, 8, LB, V)) < 0.85, 0, t[:, :, :LB])
    for r in range(N - 1):
        o = rng.permutation(8)
        for q in range(r + 1, N):
            b = int(rng.integers(1, LB)); v = np.where(rng.random(V) < 0.04, L, q * V + rng.integers(0, V, V))
            t[r, o[q], b] = v; t[r, o[q], 0] = np.where(rng.random(V) < 0.04, v, t[r, o[q], 0])
    t[:, :, :LB, 0] = L - 1; t[:, :, :LB, V - 1] = ((np.arange(N) + 1) * V)[:, None, None]
    return pack(t, perms(rng))
def setup_inputs_spread(rng):
    u = rng.random((N, 8, 16, V)) * np.sqrt(rng.random((N, 8, 1, V)))
    t = np.minimum(PL + np.maximum(np.exp2(np.log2(L - PL) * u).astype(np.int64), 1), L)
    t = np.where(rng.random(t.shape) < rng.random((N, 8, 1, 1)) * 0.3, 0, t)
    return pack(t, rng.integers(0, 16, (N, 8, 16, LB)))
def check_inputs(d):
    bad = []; a = np.asarray(d["ends"]).astype(np.int64); b = np.asarray(d["rights"])
    if not np.all((a == 0) | ((a > PL.reshape(N, 1, V)) & (a <= L))): bad.append("range of ends")
    if np.min(b) < 0 or np.max(b) > 15: bad.append("range of rights")
    return bad
def reference(ends, rights):
    m = np.ascontiguousarray(ends.astype(np.int64).reshape(N, 8, 16, V).transpose(1, 2, 0, 3)).reshape(8, 16, L)
    rt = rights.astype(np.int64).reshape(N, 8, 16, LB).transpose(1, 2, 0, 3)
    own = (np.arange(L) // V)[None, :]
    for rnd in range(RO):
        new = m
        for b in range(LB):
            t = m[:, b]; good = (t > 0) & (t < L); to = np.where(good, t // V, N)
            for q in range(1, N):
                far = (to == q) & (own < q)
                h = far.reshape(8, N, V).astype(np.int64); before = np.add.accumulate(h, axis=2) - h
                good = good & ~(far & (before.reshape(8, L) >= CAP))
            c = np.take_along_axis(m, np.where(good, t, 0)[:, None, :], 2)
            c = np.where(good[:, None, :], c, 0)
            c = np.take_along_axis(c.reshape(8, 16, N, V), rt[:, :, :, b:b + 1], 1).reshape(8, 16, L)
            new = np.maximum(new, c)
        m = new
    return {"y": np.ascontiguousarray(m.reshape(8, 16, N, V).transpose(2, 0, 1, 3)).reshape(N, 128, V).astype(np.float32)}

@@ -1,0 +1,552 @@
+import math
+import numpy as np
+from concourse.bass import DstId, RemoteDMATransfer
+from concourse.mybir import AluOpType as AL, ActivationFunctionType as AF
+
+V, CAP, LB, RO, NR = 3072, 256, 3, 3, 4
+ALPHA = math.log(2.0) / 98.0
+PHASE = 0.00196
+MID = 6144
+KI = 1.0 / ALPHA
+C0 = MID - (PHASE - 0.0000192) * KI
+Z0 = 16
+WW = Z0 + NR * V + 16
+NL = LB * V // 16
+CHK = [[0, 512, 1536, 3072], [0, 1536, 3072], [0, 1536, 3072]]
+STAGES = [(0, 512), (512, 1792), (1792, 3072)]
+START_VIA = [1, 1, 1]
+START_FUSED = True
+GW = 512
+PARTS = [(x, x + GW) for x in range(0, V, GW)]
+LAST = PARTS[:-1] + [(2560, 2816), (2816, 3072)]
+PIECES = [(0, 1024), (1024, 2048), (2048, 2560), (2560, 2816), (2816, 3072)]
+END_VIA = [3, 3, 3, 3, None]
+DVE_GATHER = [{(0, 1), (2, 1), (4, 1)}, {(0, 1), (2, 1), (4, 1)}, {(0, 1), (6, 1)}]
+PE_TAIL = True
+EARLY = True
+NG = 8
+LAG = 1024
+TRIES, MOVES = 150, 3500
+NS, NP = len(STAGES), len(PIECES)
+EW = V + 32
+
+SB = lambda n, dt: ("sbuf", [128, n], dt)
+PS = lambda n: ("psum", [128, n], "float32")
+F32, B16, I32, U16 = "float32", "bfloat16", "int32", "uint16"
+SCRATCH = {
+    "raw": SB(V, I32), "rawf": SB(V, F32), "rti": SB(8, I32), "enc": SB(EW, B16), "land": SB(EW, B16), "rt2": SB(16, B16),
+    "w0": SB(WW, B16), "w1": SB(WW, B16), "gt": SB(NG * GW, B16), "off": SB(2 * NL, U16), "lt": ("sbuf", [128, LB * 3, 128], F32),
+    "cls": SB(NL, B16), "hh": SB(3 * NL, B16), "rl": SB(2 * NL, B16), "ee": SB(208, B16), "u16": SB(V, U16),
+    "land16": SB(V, U16), "yf": SB(V, F32), "ones": SB(768, B16), "c256": SB(128, F32), "fio": SB(128, F32), "col": SB(8, F32),
+    "colb": SB(8, B16), "pint": SB(8, I32), "sel": SB(48, B16), "jw": SB(232, B16), "blw": SB(224, B16), "bc": SB(768, B16),
+    "f1": SB(128, B16), "negi": SB(224, B16), "idf": SB(128, F32), "qq": SB(520, B16), "pt": SB(384, B16), "pm": SB(384, B16),
+    "pa": PS(1024), "pb": PS(1024), "q0": PS(512), "q1": PS(512), "qz": PS(1024),
+}
+PSUM = ("pa", "pb", "q0", "q1", "qz")
+SEMAPHORES = (["cp", "cv", "ca", "ct", "sent"] + ["d%d" % i for i in range(44)]
+              + ["as%d" % i for i in range(4 * NS)] + ["ae%d" % i for i in range(4 * NP)]
+              + ["hs%d" % i for i in range(NS)] + ["he%d" % i for i in range(NP)])
+
+CY, PCY, GA = 0.00083 * 1.2, 0.00042 * 1.2, 1.56
+LAT, DLAT, DBW, RLAT, RBW, RCALL, ROW = 0.12, 1.9, 300e3, 2.5, 60e3, 0.7, 0.03
+CASES = [(1.0, 1.0, 1.0), (0.75, 1.0, 0.8), (1.25, 1.0, 1.0), (1.0, 1.5, 1.3)]
+
+
+def stage_cols(h, dd):
+    x0, x1 = STAGES[h]
+    w = (x1 - x0) // 4
+    c = dd * (w + 8) if h == 0 else x0 + 32 + dd * w
+    return c, c + w, c + w + (LB if h == 0 else 0)
+
+
+def piece_cols(pi, dd):
+    x0, x1 = PIECES[pi]
+    w = (x1 - x0) // 4
+    return x0 + dd * w, x0 + (dd + 1) * w
+
+
+def helper_of(core, topo):
+    return [c for c in topo.cores_of(core) if topo.die(c) != topo.die(core)][0]
+
+
+def helper_program(g, core, owner, T, topo):
+    k = T.rank_of(owner)
+    far = set(topo.engines(owner, T.cores[(k + 1) % NR]))
+    nin = len([e for e in topo.engines(owner, core) if e not in far])
+    jobs = [("hs%d" % h, "as%d" % (4 * h + dd), dd, "enc", "land", stage_cols(h, dd)[0], stage_cols(h, dd)[2])
+            for h, dd in enumerate(START_VIA) if dd]
+    jobs += [("he%d" % pi, "ae%d" % (4 * pi + dd), dd, "u16", "land16") + piece_cols(pi, dd) for pi, dd in enumerate(END_VIA) if dd]
+    n = 0
+    for hs, arr, dd, src, dst, c0, c1 in jobs:
+        to = T.cores[(k + dd) % NR]
+        g.wait_ge(T.sem[hs], nin)
+        g.remote_dma(T[dst][:, c0:c1], T[src][:, c0:c1], T.sem[arr], T.sem.sent, topo.addr(to)[1], topo.addr(to)[0], topo.mask(core, to))
+        n += len(topo.engines(core, to))
+    if n:
+        g.wait_ge(T.sem.sent, n)
+
+
+def build_ops(core, K, T, topo):
+    ops, sends, nsem, item = [], [], [0], [0]
+
+    def R(name, c0, c1, p0=0, p1=128):
+        return (name, p0, p1, c0, c1)
+
+    def AP(r):
+        return T[r[0]][r[1]:r[2], r[3]:r[4]] if isinstance(r, tuple) else r
+
+    def add(eng, fn, rd, wr, dur, kind="c", **kw):
+        o = dict(eng=eng, fn=fn, rd=[r for r in rd if isinstance(r, tuple)], wr=wr, dur=dur, kind=kind, n=len(ops), after=[], cls=-1)
+        o.update(kw)
+        ops.append(o)
+        return o
+
+    def newsem():
+        nsem[0] += 1
+        return "d%d" % (nsem[0] - 1)
+
+    def wd(r):
+        return r[4] - r[3]
+
+    def vec(fn, rd, wr, cyc):
+        return add("v", fn, rd, wr, max(64, cyc) * CY + 0.04)
+
+    def act(out, src, func, bias=0.0, scale=1.0):
+        return add("a", lambda q: q.activation(AP(out), AP(src), func, bias=AP(bias), scale=scale), [src, bias], [out], max(64, wd(src)) * CY + 0.06)
+
+    def memset(r, val):
+        return vec(lambda q: q.memset(AP(r), val), [], [r], wd(r) // 2)
+
+    def ts(out, src, s1, s2, o0, o1=None, half=False):
+        def fn(q):
+            if o1 is None:
+                return q.tensor_scalar(AP(out), AP(src), AP(s1), None, o0)
+            return q.tensor_scalar(AP(out), AP(src), AP(s1), AP(s2), o0, o1)
+        return vec(fn, [src, s1, s2], [out], wd(src) // 2 if half else wd(src))
+
+    def tt(out, a, b, op):
+        return vec(lambda q: q.tensor_tensor(AP(out), AP(a), AP(b), op), [a, b], [out], wd(a) * (1 if a[0] in PSUM else 2))
+
+    def cp(out, src):
+        return vec(lambda q: q.tensor_copy(AP(out), AP(src)), [src], [out], wd(src))
+
+    def mm(items, rd=(), wr=None, cyc=None):
+        def fn(q):
+            return [q.matmul(AP(o), AP(l), AP(r), st, sp) for o, l, r, st, sp in items][-1]
+        return add("t", fn, list(set([x for it in items for x in it[1:3] if isinstance(x, tuple)])) + list(rd),
+                   wr or list(set(it[0] for it in items)), (cyc or sum(max(64, wd(it[0])) for it in items)) * PCY + 0.05, cls=1)
+
+    def select(out, src, pat, op, fill, base, cm):
+        return add("p", lambda q: q.affine_select(AP(out), AP(src), pat, op, fill, base, cm), [src], [out], 0.17 + 2 * wd(out) * CY)
+
+    def dma(eng, out, src, nbytes, sem):
+        return add(eng, lambda q: q.dma_start(AP(out), AP(src)), [src], [out] if isinstance(out, tuple) else [], 0.1, kind="d", sem=sem, nbytes=nbytes)
+
+    hel = helper_of(core, topo)
+    far = topo.engines(core, T.cores[(K + 1) % NR])
+    near = [e for e in topo.engines(core, hel) if e not in set(far)]
+
+    def exchange(via, cols, srcn, dstn, arr, hsem, fused):
+        direct = [dd for dd in (1, 2, 3) if dd != via]
+        h = len(far) // (2 if via else 4)
+        share = ([far[:h], far[h:]] if via else [far[:2 * h], far[2 * h:3 * h], far[3 * h:]]) if fused else [far] * 3
+        xs = []
+        for dd in ([via] if via else []) + direct:
+            to = hel if dd == via else T.cores[(K + dd) % NR]
+            engs = near if dd == via else share[direct.index(dd)]
+            xs.append(dict(dd=dd, rid=topo.addr(to)[0], pid=topo.addr(to)[1], mask=sum(1 << e for e in engs), n=len(engs), src=R(srcn, *cols(dd)),
+                           dst=R(srcn if dd == via else dstn, *cols(dd)), sem=T.sem[hsem if dd == via else arr(dd)]))
+        for call in ([xs] if fused else [[x] for x in xs]):
+            def fn(q, call=call):
+                if len(call) == 1:
+                    x = call[0]
+                    return q.remote_dma(AP(x["dst"]), AP(x["src"]), x["sem"], T.sem.sent, x["pid"], x["rid"], x["mask"])
+                return q.remote_dma_fused([RemoteDMATransfer(dst_ids=[DstId(rid=x["rid"], pnc=x["pid"])], dma_engine_mask=x["mask"], remote_sem=x["sem"],
+                                                             src=AP(x["src"]), dst=AP(x["dst"])) for x in call], local_sem=T.sem.sent)
+            o = add("p", fn, [x["src"] for x in call], [], RCALL, kind="r", cnt=sum(x["n"] for x in call))
+            o["after"] += sends[-1:]
+            sends.append(o)
+            for x in call:
+                v = x["dd"] == via
+                a = add("x%d" % v, None, [], [R(dstn, *cols(x["dd"]))], 256 * wd(x["src"]) / RBW, kind="x", sem=arr(x["dd"]),
+                        cnt=len(far) if v else x["n"], lat=(RLAT + ROW * 128 / x["n"]) * (2 if v else 1))
+                a["after"].append(o)
+
+    col = lambda j, p0=0, p1=128: R("col", j, j + 1, p0, p1)
+    ones, fio, negi, w = R("ones", 0, 768), R("fio", 0, 128), R("negi", 0, 128), ("w0", "w1")
+    pi0, pi1, pi2, c16b = R("pint", 0, 1), R("pint", 1, 2), R("pint", 2, 3), R("colb", 0, 1)
+    memset(ones, 1.0)
+    add("p", lambda q: q.iota(AP(pi0), [[1, 1]], 0, 1), [], [pi0], 0.14)
+    add("p", lambda q: q.iota(AP(fio), [[1, 128]], 0, 0, allow_small_or_imprecise_dtypes=True), [], [fio], 0.4)
+    select(R("sel", 0, 24), R("ones", 0, 24), [[-32, 4], [-1, 3], [-16, 2]], AL.is_equal, 0.0, 0, 1)
+    select(R("sel", 24, 48), R("ones", 0, 24), [[-1, 3], [-32, 4], [-16, 2]], AL.is_equal, 0.0, 0, 1)
+    bl = R("blw", 96, 224)
+    select(bl, R("ones", 0, 128), [[1, 128]], AL.is_gt, 0.0, 0, -1)
+    select(bl, bl, [[-16, 8], [0, 16]], AL.is_ge, 0.0, 0, 1)
+    select(bl, bl, [[1, 128]], AL.not_equal, 32.0, 0, -1)
+    select(R("bc", 0, 768), ones, [[1, 6], [16, 8], [0, 16]], AL.is_equal, 0.0, 0, -1)
+    select(R("qq", 0, 516), R("ones", 0, 516), [[1, 516]], AL.is_equal, 0.0, -4, -4)
+    cp(col(0), pi0)
+    ts(pi1, pi0, 112, None, AL.bitwise_and)
+    ts(pi2, pi0, 96, None, AL.bitwise_and)
+    cp(col(2), pi1)
+    cp(c16b, pi1)
+    ts(col(5), col(0), 96.0, -96.0, AL.is_ge, AL.mult)
+    tt(col(1), col(0), col(5), AL.add)
+    ts(col(3), pi2, -1.0 / 32, 127.5 + (C0 + 0.5) / V, AL.mult, AL.add)
+    memset(col(3, 96, 128), -1000.0)
+    ts(col(4), pi2, -V / 32.0, C0 + Z0, AL.mult, AL.add)
+    for r in (R("jw", 0, 104), R("blw", 0, 96), R("negi", 128, 224), R("ee", 0, 16), R("w0", 0, Z0), R("w1", 0, Z0)):
+        memset(r, 0.0)
+    ts(R("jw", 104, 232), fio, col(2), None, AL.is_equal)
+    ts(R("f1", 0, 128), fio, col(1), -128.0, AL.is_equal, AL.mult)
+    ts(negi, fio, col(0), -128.0, AL.is_equal, AL.mult)
+    ts(R("idf", 0, 128), fio, col(0), None, AL.is_equal)
+    memset(R("c256", 0, 128), float(CAP))
+    for nm in w:
+        for r in range(NR):
+            memset(R(nm, Z0 + (NR - r) * V, Z0 + (NR - r) * V + 16, 32 * r, 32 * r + 32), 0.0)
+
+    rti = R("rti", 0, LB)
+    dma("a", rti, T.rights[:, :], 2000, newsem())
+    tiles = [(h, dd) for h in range(NS) for dd in ([START_VIA[h]] if START_VIA[h] else []) + [d for d in (1, 2, 3) if d != START_VIA[h]]]
+    tiles = tiles[:6] + [(0, 0)] + tiles[6:] + [(h, 0) for h in range(1, NS)]
+    exps, line = [], []
+    for u, (h, dd) in enumerate(tiles):
+        (x0, x1), d, (c0, c1, c2) = STAGES[h], (K + dd) % NR, stage_cols(h, dd)
+        a = x0 + dd * (c1 - c0)
+        raw, rf = R("raw", a, a + c1 - c0), R("rawf", a, a + c1 - c0)
+        line.append((dma("s" if u % 2 == 0 or u > 5 else "a", raw, T.ends[32 * d:32 * d + 32, x0:x1], 512 * wd(raw), newsem()),
+                     ts(rf, raw, float(MID), None, AL.subtract), act(R("enc", c0, c1), rf, AF.Exp, PHASE, ALPHA)))
+        exps.append(line[-1][2])
+        for z, back in ((0, 2), (1, 1), (2, 1)):
+            if u >= back:
+                line[-1][z]["behind"] = [line[-1 - back][z]]
+        if h == 0:
+            cp(R("enc", c1, c2), rti)
+    exps[0]["dur"] += 1.3
+    for h in range(NS):
+        exchange(START_VIA[h], lambda dd: stage_cols(h, dd)[0::2], "enc", "land", lambda dd: "as%d" % (4 * h + dd), "hs%d" % h, START_FUSED)
+    s_cur, s_own, s_blk, s_rt = [newsem() for _ in STAGES], newsem(), newsem(), newsem()
+    for h, dd in tiles:
+        (x0, x1), r, (c0, c1, c2), nm = STAGES[h], (K - dd) % NR, stage_cols(h, dd), "land" if dd else "enc"
+        for j in range(r + 1):
+            dma("a" if dd and h == NS - 1 and j % 2 else "s", R("w0", Z0 + j * V + x0, Z0 + j * V + x1, 32 * (r - j), 32 * (r - j) + 32),
+                R(nm, c0, c1), 256 * (c1 - c0), s_blk if j else s_cur[h] if dd or h else s_own)
+        if h == 0:
+            dma("s", R("rt2", 0, LB, 32 * r, 32 * r + 32), R(nm, c1, c2, 32 * K, 32 * K + 32), 1000, s_rt)
+    for b in range(LB):
+        ts(R("pt", 128 * b, 128 * b + 128), fio, c16b, R("rt2", b, b + 1), AL.subtract, AL.is_equal)
+    mm([(R("pa", 128 * b, 128 * b + 128), R("pt", 128 * b, 128 * b + 128), negi, True, True) for b in range(LB)])
+    act(R("pm", 0, 384), R("pa", 0, 384), AF.Copy, scale=-1.0 / 128)
+
+    def lists(rnd, k):
+        e0, CC = CHK[rnd][k] // 16, (CHK[rnd][k + 1] - CHK[rnd][k]) // 16
+        wn, c0, LC, n3 = w[rnd % 2], Z0 + 16 * e0, 16 * CC, LB * CC
+        t0, t1 = LB * e0, LB * e0 + n3
+        X, CS, Z = R("q1", 0, n3), R("q0", 0, CC), R("qz", 512 - n3, 512 + n3)
+
+        def turn(bank, p0, p1, so):
+            it = [(T[bank][0:CC, i:384:16], T[wn][p0:p1, c0 + i:c0 + LC:16], R("sel", so, so + 24, p0, p1), True, True) for i in range(16)]
+            mm(it, [R(wn, c0, c0 + LC, p0, p1)], [R(bank, 0, 384)], 16 * min(64, CC))
+
+        def ln(bank, r0, r1):
+            return add("a", lambda q: q.activation(T.lt[0:CC, LB * k:LB * k + LB, 32 * r0:32 * r1], T[bank][0:CC, 96 * r0:96 * r1], AF.Ln),
+                       [R(bank, 96 * r0, 96 * r1)], [R("lt", 384 * k + 96 * r0, 384 * k + 96 * r1)], 96 * (r1 - r0) * CY + 0.06)
+
+        def back(b, start):
+            return (R("q1", b * CC, (b + 1) * CC), T.lt[0:CC, LB * k + b, :], R("idf", 0, CC, 0, CC), start, True)
+        if rnd == 0 and k == 0 and EARLY:
+            turn("qz", 32 * K, 32 * K + 32, 0)
+            o = ln("qz", K, K + 1)
+            o["after"] += exps
+            o["dur"] += 1.5
+            turn("q0", 0, 128, 0)
+            for r in range(NR):
+                if r != K:
+                    ln("q0", r, r + 1)["after"].append(o)
+        else:
+            turn("q0", 0, 128, 24)
+            o = ln("q0", 0, NR)
+            if rnd == 0:
+                o["after"] += exps
+                o["dur"] += 1.5 if k == 0 else 0.0
+        if k == 0:
+            cp(R(wn, Z0 - 1, Z0, 0, 32), R(wn, Z0, Z0 + 1, 0, 32))
+            memset(R(wn, Z0, Z0 + 1, 0, 32), 0.0)
+        lt, cl, hb = R("lt", 384 * k, 384 * k + 384), R("cls", t0, t1), 3 * t0
+        mm([back(b, True) for b in range(LB)], [lt], None, 12 * max(64, CC))
+        act(cl, X, AF.Identity, col(3), KI / V)
+        for j in range(3):
+            ts(R("hh", hb + j * n3, hb + (j + 1) * n3), cl, 129.0 + j, None, AL.is_equal, half=True)
+        hj = lambda j, b: R("hh", hb + j * n3 + b * CC, hb + j * n3 + (b + 1) * CC)
+        it = [(CS, R("jw", c - 2 * b, c - 2 * b + 128), hj(j, b), False, False) for b in range(LB) for c, j in ((104, 0), (8, 2), (103, 1))]
+        mm([it[0][:3] + (True, False)] + it[1:-1] + [it[-1][:3] + (False, True)])
+        eo, ini, ex = R("ee", e0 + 1, e0 + CC + 1), R("ee", e0, e0 + 1), R("ee", e0, e0 + CC)
+        vec(lambda q: q.tensor_tensor_scan(AP(eo), AP(CS), T.c256[:, 0:CC], AP(ini), AL.add, AL.min), [ini, CS, R("c256", 0, CC)], [eo], CC)
+        it = []
+        for b in range(LB):
+            z1, z2 = R("qz", 512 - n3 + b * CC, 512 - n3 + (b + 1) * CC), R("qz", 512 + b * CC, 512 + (b + 1) * CC)
+            it += [(z1, bl, hj(0, b), True, False), (z1, R("blw", 0, 128), hj(2, b), False, False), (z1, R("bc", 256 * b, 256 * b + 128), ex, False, True),
+                   (z2, bl, hj(1, b), True, False), (z2, R("bc", 256 * b + 128, 256 * b + 256), ex, False, True)]
+        mm(it)
+        act(R("rl", 2 * t0, 2 * t1), Z, AF.Relu, -(CAP + 31.0))
+        it = []
+        for b in range(LB):
+            f, a = R("q1", b * CC, (b + 1) * CC), 2 * t0 + b * CC
+            it += [(f, R("f1", 0, 128), R("rl", a, a + CC), True, False), (f, negi, R("rl", a + n3, a + n3 + CC), False, False), back(b, False)]
+        mm(it, [lt], None, 18 * max(64, CC))
+        ts(R("off", (rnd % 2) * NL + t0, (rnd % 2) * NL + t1), X, KI, col(4), AL.mult, AL.add)
+
+    for k in range(len(CHK[0]) - 1):
+        lists(0, k)
+    s_y, done = newsem(), []
+
+    def finish(pi):
+        x0, x1 = PIECES[pi]
+        wq, wn = (x1 - x0) // 4, w[RO % 2]
+        for half, dds in enumerate(((2, 3), (0, 1)) if wq > 128 else ((0, 1, 2, 3),)):
+            (bank, z0), l0, l1 = (("q0", 0), ("q1", 0), ("qz", 0), ("qz", 512))[2 * (pi % 2) + half], x0 + dds[0] * wq, x0 + (dds[-1] + 1) * wq
+            mm([(R(bank, z0 + z * wq, z0 + (z + 1) * wq), R("qq", 128 * ((K + dd) % NR) + 4 - u, 128 * ((K + dd) % NR) + 132 - u),
+                 R(wn, Z0 + x0 + u * wq, Z0 + x0 + (u + 1) * wq), u == 0, u == 3) for z, dd in enumerate(dds) for u in range(4)])
+            done.append((x1, act(R("rawf", l0, l1), R(bank, z0, z0 + l1 - l0), AF.Ln), ts(R("u16", l0, l1), R("rawf", l0, l1), KI, C0, AL.mult, AL.add)))
+        exchange(END_VIA[pi], lambda dd: piece_cols(pi, dd), "u16", "land16", lambda dd: "ae%d" % (4 * pi + dd), "he%d" % pi, True)
+        for dd in range(NR):
+            yf, src = R("yf", *piece_cols(pi, dd)), (K - dd) % NR
+            cp(yf, R("land16" if dd else "u16", yf[3], yf[4]))
+            dma("a" if pi >= NP - 2 and dd % 2 else "s", T.y[32 * src:32 * src + 32, x0:x1], yf, 512 * wq, s_y)
+
+    for rnd in range(RO):
+        ws, wt, last = w[rnd % 2], w[(rnd + 1) % 2], rnd == RO - 1
+        parts = LAST if last else PARTS
+        for pi, (x0, x1) in enumerate(parts):
+            k, n = max(z for z, x in enumerate(CHK[rnd]) if x <= x0), x1 - x0
+            ca, cb = CHK[rnd][k], CHK[rnd][k + 1]
+            dst, old = R(wt, Z0 + x0, Z0 + x1), [d for d in done if d[0] + LAG <= x0]
+            for b in range(LB):
+                g0, ps, pz = (item[0] % NG) * GW, PSUM[item[0] % 2], 512 * (item[0] // 2 % 2)
+                item[0] += 1
+                o0 = (rnd % 2) * NL + (LB * ca + b * (cb - ca) + x0 - ca) // 16
+                gt, of, win = R("gt", g0, g0 + n), R("off", o0, o0 + n // 16), R(ws, 0, WW)
+                if (pi, b) in DVE_GATHER[rnd]:
+                    vec(lambda q, gt=gt, win=win, of=of: q.tensor_copy(AP(gt), AP(win).indirect(AP(of))), [win, of], [gt], n * GA)["cls"] = 0
+                else:
+                    add("a", lambda q, gt=gt, win=win, of=of: q.activation(AP(gt), AP(win).indirect(AP(of)), AF.Copy),
+                        [win, of], [gt], n * GA * CY + 0.065, cls=0, behind=[d[1] for d in old])
+                mm([(R(ps, pz, pz + n), R("pm", 128 * b, 128 * b + 128), gt, True, True)])
+                tt(dst, R(ps, pz, pz + n), R(ws, dst[3], dst[4]) if b == 0 else dst, AL.max)["behind"] = [d[2] for d in old]
+                if b == 0 and x0 == 0:
+                    p0 = R(wt, Z0, Z0 + 1, 0, 32)
+                    tt(p0, p0, R(ws, Z0 - 1, Z0, 0, 32), AL.max)
+            if last:
+                for z in range(NP):
+                    if PIECES[z][1] == x1:
+                        finish(z)
+                continue
+            if PE_TAIL and pi == len(parts) - 1:
+                oth = PSUM[item[0] % 2]
+                for j, z in ((1, R(oth, 0, n)), (2, R(oth, 512, 512 + n)), (3, R(ps, 512 - pz, 512 - pz + n))):
+                    mm([(z, R("negi", 32 * j, 32 * j + 128), dst, True, True)])
+                    to = R(wt, dst[3] + j * V, dst[4] + j * V)
+                    if j == 2:
+                        ts(to, z, -1.0 / 128, None, AL.mult)
+                    else:
+                        act(to, z, AF.Copy, scale=-1.0 / 128)
+            else:
+                sr = newsem()
+                for j in range(1, NR):
+                    dma("s", R(wt, dst[3] + j * V, dst[4] + j * V, 0, 128 - 32 * j), R(wt, dst[3], dst[4], 32 * j, 128), (128 - 32 * j) * n * 2, sr)
+            if x1 in CHK[rnd + 1]:
+                lists(rnd + 1, CHK[rnd + 1].index(x1) - 1)
+    return ops
+
+
+def depends(ops):
+    hist, groups, lastt = {}, {}, {}
+    for o in ops:
+        deps = set()
+        mine = [(r, False) for r in o["rd"]] + [(r, True) for r in o["wr"]]
+        for r, wr in mine:
+            for q, qw, a in hist.get(r[0], ()):
+                if r[0] in PSUM and a["eng"] != o["eng"]:
+                    hit = q[3] // 512 <= (r[4] - 1) // 512 and r[3] // 512 <= (q[4] - 1) // 512
+                else:
+                    hit = (wr or qw) and q[1] < r[2] and r[1] < q[2] and q[3] < r[4] and r[3] < q[4] and not a["eng"] == o["eng"] == "t"
+                if hit:
+                    deps.add(a["n"])
+        for r, wr in mine:
+            hist.setdefault(r[0], []).append((r, wr, o))
+        o["deps"] = deps
+        if o["kind"] == "d":
+            groups.setdefault(o["sem"], []).append(o["n"])
+    for o in ops:
+        for d in list(o["deps"]):
+            if ops[d]["kind"] == "d":
+                o["deps"].update(groups[ops[d]["sem"]])
+        o["order"] = o["deps"] | set(a["n"] for a in o["after"])
+        if o["eng"] == "t":
+            for bk in set((r[0], r[3] // 512) for r in o["wr"]):
+                if bk in lastt:
+                    o["order"].add(lastt[bk])
+                lastt[bk] = o["n"]
+    return groups
+
+
+def schedule(ops):
+    n = len(ops)
+    pred = [sorted(o["order"] | set(a["n"] for a in o.get("behind", ()))) for o in ops]
+    hard = [sorted(o["order"]) for o in ops]
+    succ = [[] for _ in ops]
+    for i in range(n):
+        for d in pred[i]:
+            succ[d].append(i)
+    isd = [o["kind"] == "d" for o in ops]
+    res = ["dma" if isd[i] else ops[i]["eng"] for i in range(n)]
+    dur = [ops[i]["nbytes"] / DBW + 0.05 if isd[i] else ops[i]["dur"] for i in range(n)]
+    pre = [DLAT + LAT if isd[i] else ops[i].get("lat", LAT) for i in range(n)]
+
+    def sgs(key, fwd):
+        before, after = (pred, succ) if fwd else (succ, pred)
+        left = [len(b) for b in before]
+        ready = [i for i in range(n) if not left[i]]
+        st, busy = [0.0] * n, {}
+        while ready:
+            i = min(ready, key=key.get)
+            ready.remove(i)
+            t = max([st[d] + (0.01 - (pre[i] if fwd else dur[i]) if isd[i] and isd[d] else dur[d] + (0.0 if fwd else pre[d]))
+                     for d in before[i]] + [0.0]) + (pre[i] if fwd else 0.0)
+            line, z = busy.setdefault(res[i], []), 0
+            for a, b in line:
+                if b > t:
+                    if a >= t + dur[i] - 1e-9:
+                        break
+                    t = b
+                z += 1
+            line.insert(z, (t, t + dur[i]))
+            st[i] = t
+            for s in after[i]:
+                left[s] -= 1
+                if not left[s]:
+                    ready.append(s)
+        return st
+
+    def replay(seq, f):
+        free, fin, dfree, lastq = {}, [0.0] * n, 0.0, {}
+        for i in seq:
+            o, t, by = ops[i], 0.0, None
+            for d in hard[i]:
+                if fin[d] > t:
+                    t, by = fin[d], d
+            t += o["lat"] * f[2] if "lat" in o else LAT
+            o["byq"] = free.get(o["eng"], 0.0) > t
+            if o["byq"]:
+                t, by = free[o["eng"]], lastq[o["eng"]]
+            o["by"], lastq[o["eng"]] = by, i
+            free[o["eng"]] = fin[i] = t + o["dur"] * (f[o["cls"]] if o["cls"] >= 0 else f[2] if o["kind"] == "x" else 1.0)
+            if isd[i]:
+                dfree = fin[i] = max(fin[i] + DLAT * f[2], dfree) + dur[i] * f[2]
+            o["st"], o["fin"] = t, fin[i]
+        return max(fin)
+
+    def cost(seq):
+        return sum(replay(seq, f) for f in CASES) / len(CASES)
+
+    rng = np.random.default_rng(1)
+    best, key = None, dict((i, float(i)) for i in range(n))
+    for trial in range(TRIES):
+        st = sgs(key, True)
+        if trial % 4 == 2:
+            for fwd in (False, True):
+                st = sgs(dict((i, -(st[i] + dur[i])) for i in range(n)), fwd)
+        seq = sorted(range(n), key=lambda i: (st[i] - (DLAT if isd[i] else 0.0), i))
+        span = cost(seq)
+        if best is None or span < best[0]:
+            best = (span, seq, st)
+        amp, mid, wid = (1.0, 3.0, 6.0)[int(rng.integers(3))], best[0] * rng.random(), (1.5, 4.0)[int(rng.integers(2))]
+        key = dict((i, s + (amp * (rng.random() - 0.5) if abs(s - mid) < wid and rng.random() < 0.4 else 0.0)) for i, s in enumerate(best[2]))
+    cur, crit = best[:2], None
+    for trial in range(MOVES):
+        seq = cur[1]
+        if crit is None:
+            replay(seq, CASES[int(rng.integers(len(CASES)))])
+            crit, j = [], max(range(n), key=lambda z: ops[z]["fin"])
+            while j is not None:
+                if ops[j]["byq"]:
+                    crit += [(j, -1), (ops[j]["by"], 1)]
+                j = ops[j]["by"]
+        if crit and rng.random() < 0.7:
+            i, step = crit[int(rng.integers(len(crit)))]
+            p = seq.index(i)
+        else:
+            p, step = int(rng.integers(n)), (1 if rng.random() < 0.5 else -1)
+            i = seq[p]
+        stop, z, to, hops = set(succ[i] if step > 0 else pred[i]), p + step, None, int(rng.integers(1, 4))
+        while 0 <= z < n and seq[z] not in stop and hops:
+            if ops[seq[z]]["eng"] == ops[i]["eng"]:
+                to, hops = z, hops - 1
+            z += step
+        if to is None:
+            continue
+        new = seq[:p] + seq[p + 1:]
+        new.insert(to, i)
+        span = cost(new)
+        if span <= cur[0] + 0.12 * (1.0 - trial / MOVES):
+            new.sort(key=lambda j: ops[j]["st"])
+            cur, crit = (span, new), None
+            if span < best[0]:
+                best = cur
+    replay(best[1], CASES[0])
+    return best[1]
+
+
+def emit(g, T, ops, seq, groups):
+    queue = {"p": g, "v": g.vector, "a": g.scalar, "t": g.tensor, "s": g.sync}
+    need = set(d for o in ops for d in o["deps"])
+    known = dict((e, {}) for e in queue)
+    total = {}
+    for i in seq:
+        o = ops[i]
+        if o["kind"] == "x":
+            o["tok"], o["vc"] = (o["sem"], o["cnt"]), {}
+            total[o["sem"]] = o["cnt"]
+            continue
+        q, kn, toks = queue[o["eng"]], known[o["eng"]], {}
+        for d in o["deps"]:
+            s, c = ops[d]["tok"]
+            if c > toks.get(s, (0, 0))[0]:
+                toks[s] = (c, d)
+        for s, (c, d) in sorted(toks.items(), key=lambda kv: -ops[kv[1][1]]["fin"]):
+            if kn.get(s, 0) < c:
+                q.wait_ge(T.sem[s], c)
+                kn[s] = c
+                for m in (groups[s] if ops[d]["kind"] == "d" else [d]):
+                    for s2, c2 in ops[m]["vc"].items():
+                        kn[s2] = max(kn.get(s2, 0), c2)
+        ins = o["fn"](q)
+        o["vc"] = dict(kn)
+        if o["kind"] == "d":
+            ins.then_inc(T.sem[o["sem"]], 16)
+            total[o["sem"]] = 16 * len(groups[o["sem"]])
+            o["tok"] = (o["sem"], total[o["sem"]])
+        elif o["kind"] == "r":
+            total["sent"] = total.get("sent", 0) + o["cnt"]
+        elif i in need:
+            s = "c" + o["eng"]
+            total[s] = total.get(s, 0) + 1
+            ins.then_inc(T.sem[s], 1)
+            o["tok"] = (s, total[s])
+    for s, c in total.items():
+        if max(kn.get(s, 0) for kn in known.values()) < c:
+            g.wait_ge(T.sem[s], c)
+
+
+def rank_program(g, core, T, topo):
+    rank = T.rank_of(core)
+    if rank is None:
+        for owner in T.cores:
+            if helper_of(owner, topo) == core:
+                helper_program(g, core, owner, T, topo)
+        return
+    ops = build_ops(core, rank, T, topo)
+    groups = depends(ops)
+    emit(g, T, ops, schedule(ops), groups)

@@ -1,89 +1,105 @@
 import math
 import numpy as np
 from concourse.bass import DstId, RemoteDMATransfer
-from concourse.mybir import AluOpType as AL, ActivationFunctionType as AF
+from concourse.mybir import AluOpType as AL, ActivationFunctionType as AF, AxisListType as AX
 
 V, CAP, LB, RO, NR = 3072, 256, 3, 3, 4
 ALPHA = math.log(2.0) / 98.0
 PHASE = 0.00196
 MID = 6144
 KI = 1.0 / ALPHA
-C0 = MID - (PHASE - 0.0000192) * KI
-Z0 = 16
-WW = Z0 + NR * V + 16
-NL = LB * V // 16
-CHK = [[0, 512, 1536, 3072], [0, 1536, 3072], [0, 1536, 3072]]
-STAGES = [(0, 512), (512, 1792), (1792, 3072)]
-START_VIA = [1, 1, 1]
-START_FUSED = True
-GW = 512
-PARTS = [(x, x + GW) for x in range(0, V, GW)]
-LAST = PARTS[:-1] + [(2560, 2816), (2816, 3072)]
-PIECES = [(0, 1024), (1024, 2048), (2048, 2560), (2560, 2816), (2816, 3072)]
-END_VIA = [3, 3, 3, 3, None]
-DVE_GATHER = [{(0, 1), (2, 1), (4, 1)}, {(0, 1), (2, 1), (4, 1)}, {(0, 1), (6, 1)}]
-PE_TAIL = True
-EARLY = True
-NG = 8
-LAG = 1024
-TRIES, MOVES = 150, 3500
-NS, NP = len(STAGES), len(PIECES)
-EW = V + 32
+LNS = math.exp(0.0000192 - PHASE)
+ROUND = 12582912.0
+Q = V // 4
+CC = Q // 16
+NL = LB * CC
+GAP = 3 * Q + 16
+OWN = [16 + k * (V + GAP) for k in range(NR + 1)]
+BEG = [0] + [c - GAP for c in OWN[1:]]
+WW = OWN[NR] + 16
+CB, BIG = 130.0, 32768.0
+START = [[(0, Q)], [(0, Q)], [(0, Q // 2), (Q // 2, Q)], [(0, Q // 2), (Q // 2, Q)]]
+START_VIA = [[[1]], [[1]], [[1], [2]], [[1], [2]]]
+START_AFTER = [2, 3, None, None]
+BATCH = [[[3], [2], [1], [0]], [[3, 2], [1], [0]], [[3, 2], [1], [0]]]
+CUTS = [[0, Q], [0, Q], [0, 384, Q], [0, 384, 640, Q]]
+END_VIA = [1, 1, 0]
+DVE_GATHER = [320] * 12
+ORDER = 1
+ON_ACT = ""
+STAGGER = True
+DVE_B = 1
+DECODE = [2, 2, 1]
+NG = 6
 
 SB = lambda n, dt: ("sbuf", [128, n], dt)
 PS = lambda n: ("psum", [128, n], "float32")
 F32, B16, I32, U16 = "float32", "bfloat16", "int32", "uint16"
 SCRATCH = {
-    "raw": SB(V, I32), "rawf": SB(V, F32), "rti": SB(8, I32), "enc": SB(EW, B16), "land": SB(EW, B16), "rt2": SB(16, B16),
-    "w0": SB(WW, B16), "w1": SB(WW, B16), "gt": SB(NG * GW, B16), "off": SB(2 * NL, U16), "lt": ("sbuf", [128, LB * 3, 128], F32),
-    "cls": SB(NL, B16), "hh": SB(3 * NL, B16), "rl": SB(2 * NL, B16), "ee": SB(208, B16), "u16": SB(V, U16),
-    "land16": SB(V, U16), "yf": SB(V, F32), "ones": SB(768, B16), "c256": SB(128, F32), "fio": SB(128, F32), "col": SB(8, F32),
-    "colb": SB(8, B16), "pint": SB(8, I32), "sel": SB(48, B16), "jw": SB(232, B16), "blw": SB(224, B16), "bc": SB(768, B16),
-    "f1": SB(128, B16), "negi": SB(224, B16), "idf": SB(128, F32), "qq": SB(520, B16), "pt": SB(384, B16), "pm": SB(384, B16),
-    "pa": PS(1024), "pb": PS(1024), "q0": PS(512), "q1": PS(512), "qz": PS(1024),
+    "raw": SB(V, I32), "rawf": SB(V, F32), "rta": SB(16, I32), "rtb": SB(16, B16), "rtc": SB(16, F32), "enc": SB(V, B16), "land": SB(V, B16),
+    "w0": SB(WW, B16), "w1": SB(WW, B16), "w2": SB(WW, B16), "res": SB(V, B16), "gt": SB(NG * Q, B16), "off": SB(RO * NR * NL, U16),
+    "lt": ("sbuf", [128, 3 * LB, 128], F32), "cls": SB(3 * NL, B16), "hh": SB(9 * NL, B16), "rl": SB(6 * NL, B16), "fl": ("sbuf", [128, LB, 128], B16), "ee": SB(6 * CC, B16),
+    "xa": SB(NL, F32), "yf": SB(V, F32), "ones": SB(384, B16), "c256": SB(2 * CC, F32), "fio": SB(144, B16), "col": SB(8, F32),
+    "pint": SB(8, I32), "sel": SB(24, B16), "rep": SB(128, B16), "jw": SB(240, B16), "jc": SB(144, B16), "bl": SB(128, B16), "bc": SB(9 * 128, B16),
+    "negi": SB(128, B16), "gapi": SB(128, B16), "kid": SB(128, F32), "pt": SB(768, B16), "pm": SB(NR * 384, B16),
+    "pa": PS(1024), "pb": PS(1024), "pc": PS(1024), "q0": PS(512), "q1": PS(512),
 }
-PSUM = ("pa", "pb", "q0", "q1", "qz")
-SEMAPHORES = (["cp", "cv", "ca", "ct", "sent"] + ["d%d" % i for i in range(44)]
-              + ["as%d" % i for i in range(4 * NS)] + ["ae%d" % i for i in range(4 * NP)]
-              + ["hs%d" % i for i in range(NS)] + ["he%d" % i for i in range(NP)])
+PSUM = ("pa", "pb", "pc", "q0", "q1")
+SEMAPHORES = (["cp", "cv", "ca", "ct", "sent", "ar"] + ["d%d" % i for i in range(40)]
+              + ["as%d" % i for i in range(8)] + ["ae%d" % i for i in range(8)] + ["h%d" % i for i in range(8)])
 
 CY, PCY, GA = 0.00083 * 1.2, 0.00042 * 1.2, 1.56
-LAT, DLAT, DBW, RLAT, RBW, RCALL, ROW = 0.12, 1.9, 300e3, 2.5, 60e3, 0.7, 0.03
-CASES = [(1.0, 1.0, 1.0), (0.75, 1.0, 0.8), (1.25, 1.0, 1.0), (1.0, 1.5, 1.3)]
+LAT, DLAT, DBW, RLAT, RCALL = 0.12, 1.9, 300e3, 4.5, 0.7
+ARRIVE = [[19.0], [16.0], [11.5, 13.5], [9.0, 11.0]]
+BEAT, HOP, LOOK, TAIL, AHEAD = 1.4, 0.2, 0.1, 6.0, {"a": 5.0, "v": 5.0, "t": 1.0}
 
 
-def stage_cols(h, dd):
-    x0, x1 = STAGES[h]
-    w = (x1 - x0) // 4
-    c = dd * (w + 8) if h == 0 else x0 + 32 + dd * w
-    return c, c + w, c + w + (LB if h == 0 else 0)
+def last_round(K):
+    if ORDER:
+        return [k for k in range(NR - 1, -1, -1) if k != K] + [K]
+    return [k for k in range(NR - 1, -1, -1) if k not in (K, NR - 1 - K)] + [NR - 1 - K, K]
 
 
-def piece_cols(pi, dd):
-    x0, x1 = PIECES[pi]
-    w = (x1 - x0) // 4
-    return x0 + dd * w, x0 + (dd + 1) * w
+def end_pieces(i):
+    return [(0, Q // 2, END_VIA[i]), (Q // 2, Q, 0)]
 
 
-def helper_of(core, topo):
-    return [c for c in topo.cores_of(core) if topo.die(c) != topo.die(core)][0]
+def helpers_of(core, topo):
+    return [c for c in topo.cores_of(core) if topo.die(c) != topo.die(core)]
 
 
-def helper_program(g, core, owner, T, topo):
-    k = T.rank_of(owner)
-    far = set(topo.engines(owner, T.cores[(k + 1) % NR]))
-    nin = len([e for e in topo.engines(owner, core) if e not in far])
-    jobs = [("hs%d" % h, "as%d" % (4 * h + dd), dd, "enc", "land", stage_cols(h, dd)[0], stage_cols(h, dd)[2])
-            for h, dd in enumerate(START_VIA) if dd]
-    jobs += [("he%d" % pi, "ae%d" % (4 * pi + dd), dd, "u16", "land16") + piece_cols(pi, dd) for pi, dd in enumerate(END_VIA) if dd]
-    n = 0
-    for hs, arr, dd, src, dst, c0, c1 in jobs:
-        to = T.cores[(k + dd) % NR]
-        g.wait_ge(T.sem[hs], nin)
-        g.remote_dma(T[dst][:, c0:c1], T[src][:, c0:c1], T.sem[arr], T.sem.sent, topo.addr(to)[1], topo.addr(to)[0], topo.mask(core, to))
-        n += len(topo.engines(core, to))
+def hand_ons(K):
+    jobs = []
+    for h, (x0, x1) in enumerate(START[K]):
+        for z, dd in enumerate(START_VIA[K][h]):
+            jobs.append((z, (K + dd) % NR, "as%d" % (2 * K + h), "enc", dd * Q + x0, dd * Q + x1, "w0", OWN[K] + x0))
+    for i, k in enumerate(last_round(K)[:-1]):
+        for h, (x0, x1, via) in enumerate(end_pieces(i)):
+            if via:
+                jobs.append((0, k, "ae%d" % (2 * K + h), "res", k * Q + x0, k * Q + x1, "land", K * Q + x0))
+    return [(j[0], "h%d" % n) + j[1:] for n, j in enumerate(jobs)]
+
+
+def helper_program(g, core, owner, z, T, topo):
+    K, n = T.rank_of(owner), 0
+    far = set(topo.engines(owner, T.cores[(K + 1) % NR]))
+    near = len([e for e in topo.engines(owner, core) if e not in far])
+    for hz, hs, k, arr, src, c0, c1, dst, d0 in hand_ons(K):
+        if hz == z:
+            to = T.cores[k]
+            h = int(arr[2:]) % 2
+            g.wait_ge(T.sem[hs], near // (len(START_VIA[K][h]) if src == "enc" else 1))
+            g.remote_dma(T[dst][:, d0:d0 + c1 - c0], T[src][:, c0:c1], T.sem[arr], T.sem.sent, topo.addr(to)[1], topo.addr(to)[0], topo.mask(core, to))
+            n += len(topo.engines(core, to))
     if n:
         g.wait_ge(T.sem.sent, n)
+
+
+def start_engines(r, h, nfar):
+    via = START_VIA[r][h]
+    direct = [dd for dd in (1, 2, 3) if dd not in via]
+    share = {1: [nfar], 2: [nfar // 2] * 2, 3: [nfar // 2, nfar // 4, nfar // 4]}[len(direct)]
+    return dict([(dd, nfar) for dd in via] + list(zip(direct, share)))
 
 
 def build_ops(core, K, T, topo):
@@ -136,228 +152,287 @@ def build_ops(core, K, T, topo):
         return add("t", fn, list(set([x for it in items for x in it[1:3] if isinstance(x, tuple)])) + list(rd),
                    wr or list(set(it[0] for it in items)), (cyc or sum(max(64, wd(it[0])) for it in items)) * PCY + 0.05, cls=1)
 
+    def group(out, terms):
+        return [(out, l, r, z == 0, z == len(terms) - 1) for z, (l, r) in enumerate(terms)]
+
     def select(out, src, pat, op, fill, base, cm):
         return add("p", lambda q: q.affine_select(AP(out), AP(src), pat, op, fill, base, cm), [src], [out], 0.17 + 2 * wd(out) * CY)
 
     def dma(eng, out, src, nbytes, sem):
         return add(eng, lambda q: q.dma_start(AP(out), AP(src)), [src], [out] if isinstance(out, tuple) else [], 0.1, kind="d", sem=sem, nbytes=nbytes)
 
-    hel = helper_of(core, topo)
+    hel = helpers_of(core, topo)
     far = topo.engines(core, T.cores[(K + 1) % NR])
-    near = [e for e in topo.engines(core, hel) if e not in set(far)]
+    near = [e for e in topo.engines(core, hel[0]) if e not in set(far)]
+    jobs = hand_ons(K)
 
-    def exchange(via, cols, srcn, dstn, arr, hsem, fused):
-        direct = [dd for dd in (1, 2, 3) if dd != via]
-        h = len(far) // (2 if via else 4)
-        share = ([far[:h], far[h:]] if via else [far[:2 * h], far[2 * h:3 * h], far[3 * h:]]) if fused else [far] * 3
-        xs = []
-        for dd in ([via] if via else []) + direct:
-            to = hel if dd == via else T.cores[(K + dd) % NR]
-            engs = near if dd == via else share[direct.index(dd)]
-            xs.append(dict(dd=dd, rid=topo.addr(to)[0], pid=topo.addr(to)[1], mask=sum(1 << e for e in engs), n=len(engs), src=R(srcn, *cols(dd)),
-                           dst=R(srcn if dd == via else dstn, *cols(dd)), sem=T.sem[hsem if dd == via else arr(dd)]))
-        for call in ([xs] if fused else [[x] for x in xs]):
-            def fn(q, call=call):
-                if len(call) == 1:
-                    x = call[0]
-                    return q.remote_dma(AP(x["dst"]), AP(x["src"]), x["sem"], T.sem.sent, x["pid"], x["rid"], x["mask"])
-                return q.remote_dma_fused([RemoteDMATransfer(dst_ids=[DstId(rid=x["rid"], pnc=x["pid"])], dma_engine_mask=x["mask"], remote_sem=x["sem"],
-                                                             src=AP(x["src"]), dst=AP(x["dst"])) for x in call], local_sem=T.sem.sent)
-            o = add("p", fn, [x["src"] for x in call], [], RCALL, kind="r", cnt=sum(x["n"] for x in call))
-            o["after"] += sends[-1:]
-            sends.append(o)
-            for x in call:
-                v = x["dd"] == via
-                a = add("x%d" % v, None, [], [R(dstn, *cols(x["dd"]))], 256 * wd(x["src"]) / RBW, kind="x", sem=arr(x["dd"]),
-                        cnt=len(far) if v else x["n"], lat=(RLAT + ROW * 128 / x["n"]) * (2 if v else 1))
-                a["after"].append(o)
+    def send(xs, wait=()):
+        def fn(q):
+            return q.remote_dma_fused([RemoteDMATransfer(dst_ids=[DstId(rid=topo.addr(c)[0], pnc=topo.addr(c)[1]) for c in to],
+                                                         dma_engine_mask=sum(1 << e for e in engs), remote_sem=T.sem[sem],
+                                                         srcs=[AP(src)], dsts=[AP(dst)] * len(to)) for to, engs, sem, src, dst in xs], local_sem=T.sem.sent)
+        o = add("p", fn, [x[3] for x in xs] + list(wait), [], RCALL, kind="r", cnt=sum(len(x[1]) for x in xs))
+        o["after"] += sends[-1:]
+        sends.append(o)
+        return o
+
+    def arrival(dst, sem, cnt, after, lat, tmin=0.0):
+        o = add("x" + sem, None, [], [dst], 0.01, kind="x", sem=sem, cnt=cnt, lat=lat, tmin=tmin)
+        o["after"] += after
+
+    def to_helper(src, engs):
+        hz, hs = [j[:2] for j in jobs if (j[4], j[5]) == (src[0], src[3])][0]
+        return ([hel[hz]], engs, hs, src, src)
+
+    others = [(K + dd) % NR for dd in (1, 2, 3)]
+    mine = R("rta", LB * K, LB * K + LB)
+    dma("s", mine, T.rights[:, :], 2000, newsem())
+    first = send([([T.cores[k] for k in others], far, "ar", mine, mine)])
+    first["due"] = -60.0
 
     col = lambda j, p0=0, p1=128: R("col", j, j + 1, p0, p1)
-    ones, fio, negi, w = R("ones", 0, 768), R("fio", 0, 128), R("negi", 0, 128), ("w0", "w1")
-    pi0, pi1, pi2, c16b = R("pint", 0, 1), R("pint", 1, 2), R("pint", 2, 3), R("colb", 0, 1)
-    memset(ones, 1.0)
+    ones, fio, negi, gapi, kid, w = R("ones", 0, 128), R("fio", 0, 128), R("negi", 0, 128), R("gapi", 0, 128), R("kid", 0, 128), ("w0", "w1", "w2")
+    pi0, pi1, pi2 = R("pint", 0, 1), R("pint", 1, 2), R("pint", 2, 3)
+    memset(R("ones", 0, 384), 0.0)
+    act(R("ones", 0, 384), R("ones", 0, 384), AF.Exp)["dur"] += 1.3
     add("p", lambda q: q.iota(AP(pi0), [[1, 1]], 0, 1), [], [pi0], 0.14)
-    add("p", lambda q: q.iota(AP(fio), [[1, 128]], 0, 0, allow_small_or_imprecise_dtypes=True), [], [fio], 0.4)
-    select(R("sel", 0, 24), R("ones", 0, 24), [[-32, 4], [-1, 3], [-16, 2]], AL.is_equal, 0.0, 0, 1)
-    select(R("sel", 24, 48), R("ones", 0, 24), [[-1, 3], [-32, 4], [-16, 2]], AL.is_equal, 0.0, 0, 1)
-    bl = R("blw", 96, 224)
-    select(bl, R("ones", 0, 128), [[1, 128]], AL.is_gt, 0.0, 0, -1)
-    select(bl, bl, [[-16, 8], [0, 16]], AL.is_ge, 0.0, 0, 1)
-    select(bl, bl, [[1, 128]], AL.not_equal, 32.0, 0, -1)
-    select(R("bc", 0, 768), ones, [[1, 6], [16, 8], [0, 16]], AL.is_equal, 0.0, 0, -1)
-    select(R("qq", 0, 516), R("ones", 0, 516), [[1, 516]], AL.is_equal, 0.0, -4, -4)
+    add("p", lambda q: q.iota(T.fio[:, :], [[1, 144]], 0, 0, allow_small_or_imprecise_dtypes=True), [], [R("fio", 0, 144)], 0.4)
+    select(R("rep", 0, 128), ones, [[0, 4], [-1, 32]], AL.is_equal, 0.0, -32 * K, 1)
+    select(R("sel", 0, 24), R("ones", 0, 24), [[-1, 3], [-16, 8]], AL.is_equal, 0.0, 0, 1)
     cp(col(0), pi0)
     ts(pi1, pi0, 112, None, AL.bitwise_and)
     ts(pi2, pi0, 96, None, AL.bitwise_and)
-    cp(col(2), pi1)
-    cp(c16b, pi1)
-    ts(col(5), col(0), 96.0, -96.0, AL.is_ge, AL.mult)
-    tt(col(1), col(0), col(5), AL.add)
-    ts(col(3), pi2, -1.0 / 32, 127.5 + (C0 + 0.5) / V, AL.mult, AL.add)
-    memset(col(3, 96, 128), -1000.0)
-    ts(col(4), pi2, -V / 32.0, C0 + Z0, AL.mult, AL.add)
-    for r in (R("jw", 0, 104), R("blw", 0, 96), R("negi", 128, 224), R("ee", 0, 16), R("w0", 0, Z0), R("w1", 0, Z0)):
-        memset(r, 0.0)
-    ts(R("jw", 104, 232), fio, col(2), None, AL.is_equal)
-    ts(R("f1", 0, 128), fio, col(1), -128.0, AL.is_equal, AL.mult)
-    ts(negi, fio, col(0), -128.0, AL.is_equal, AL.mult)
-    ts(R("idf", 0, 128), fio, col(0), None, AL.is_equal)
-    memset(R("c256", 0, 128), float(CAP))
+    cp(col(1), pi1)
+    for k in range(NR):
+        ts(col(2 + k), pi2, -Q / 32.0, MID + 16 - BEG[k] + (k * GAP if k == NR - 1 else -CB * GAP), AL.mult, AL.add)
+    ts(col(6), pi2, -Q / 32.0, float(MID - 3 * V), AL.mult, AL.add)
+    ts(negi, fio, col(0), -BIG, AL.is_equal, AL.mult, half=True)
+    ts(kid, fio, col(0), KI, AL.is_equal, AL.mult)
+    ts(gapi, fio, col(0), float(GAP), AL.is_equal, AL.mult, half=True)
+    memset(R("jw", 0, 96), 0.0)
+    ts(R("jw", 96, 240), R("fio", 0, 144), col(1), 16.0, AL.subtract, AL.is_equal, half=True)
+    tt(R("jc", 0, 144), R("jw", 64, 208), R("jw", 32, 176), AL.add)
+    tt(R("jc", 0, 144), R("jc", 0, 144), R("jw", 0, 144), AL.add)
+    memset(R("c256", 0, 2 * CC), float(CAP))
+    vec(lambda q: q.memset(T.fl[:, :, :], 0.0), [], [R("fl", 0, 384)], 192)
     for nm in w:
-        for r in range(NR):
-            memset(R(nm, Z0 + (NR - r) * V, Z0 + (NR - r) * V + 16, 32 * r, 32 * r + 32), 0.0)
+        zs = [R(nm, c, c + 1) for c in BEG[1:NR]]
+        vec(lambda q, nm=nm: q.memset(T[nm][:, BEG[1]:BEG[NR - 1] + 1:V + GAP], 0.0), [], zs, 64)
+        memset(R(nm, 0, 1), 0.0)
+        for u in range(4):
+            c = OWN[NR - 1] + V - Q * u
+            vec(lambda q, nm=nm, c=c, u=u: q.memset(T[nm][32 * u:32 * u + 32, c:c + GAP + 1:GAP], 0.0), [],
+                [R(nm, c + z, c + z + 1, 32 * u, 32 * u + 32) for z in (0, GAP)], 64)
+    bl = R("bl", 0, 128)
+    select(bl, ones, [[1, 128]], AL.is_gt, 0.0, 0, -1)
+    select(bl, bl, [[-16, 8], [0, 16]], AL.is_ge, 0.0, 0, 1)
+    select(bl, bl, [[1, 128]], AL.not_equal, 32.0, 0, -1)
+    for z in (1, 2, 3):
+        select(R("bc", 384 * z - 384, 384 * z), R("ones", 0, 384), [[1, 3], [16, 8], [0, 16]], AL.is_equal, 0.0, 3 * z - 3, -1)
 
-    rti = R("rti", 0, LB)
-    dma("a", rti, T.rights[:, :], 2000, newsem())
-    tiles = [(h, dd) for h in range(NS) for dd in ([START_VIA[h]] if START_VIA[h] else []) + [d for d in (1, 2, 3) if d != START_VIA[h]]]
-    tiles = tiles[:6] + [(0, 0)] + tiles[6:] + [(h, 0) for h in range(1, NS)]
-    exps, line = [], []
-    for u, (h, dd) in enumerate(tiles):
-        (x0, x1), d, (c0, c1, c2) = STAGES[h], (K + dd) % NR, stage_cols(h, dd)
-        a = x0 + dd * (c1 - c0)
-        raw, rf = R("raw", a, a + c1 - c0), R("rawf", a, a + c1 - c0)
-        line.append((dma("s" if u % 2 == 0 or u > 5 else "a", raw, T.ends[32 * d:32 * d + 32, x0:x1], 512 * wd(raw), newsem()),
-                     ts(rf, raw, float(MID), None, AL.subtract), act(R("enc", c0, c1), rf, AF.Exp, PHASE, ALPHA)))
-        exps.append(line[-1][2])
-        for z, back in ((0, 2), (1, 1), (2, 1)):
-            if u >= back:
-                line[-1][z]["behind"] = [line[-1 - back][z]]
-        if h == 0:
-            cp(R("enc", c1, c2), rti)
-    exps[0]["dur"] += 1.3
-    for h in range(NS):
-        exchange(START_VIA[h], lambda dd: stage_cols(h, dd)[0::2], "enc", "land", lambda dd: "as%d" % (4 * h + dd), "hs%d" % h, START_FUSED)
-    s_cur, s_own, s_blk, s_rt = [newsem() for _ in STAGES], newsem(), newsem(), newsem()
-    for h, dd in tiles:
-        (x0, x1), r, (c0, c1, c2), nm = STAGES[h], (K - dd) % NR, stage_cols(h, dd), "land" if dd else "enc"
-        for j in range(r + 1):
-            dma("a" if dd and h == NS - 1 and j % 2 else "s", R("w0", Z0 + j * V + x0, Z0 + j * V + x1, 32 * (r - j), 32 * (r - j) + 32),
-                R(nm, c0, c1), 256 * (c1 - c0), s_blk if j else s_cur[h] if dd or h else s_own)
-        if h == 0:
-            dma("s", R("rt2", 0, LB, 32 * r, 32 * r + 32), R(nm, c1, c2, 32 * K, 32 * K + 32), 1000, s_rt)
-    for b in range(LB):
-        ts(R("pt", 128 * b, 128 * b + 128), fio, c16b, R("rt2", b, b + 1), AL.subtract, AL.is_equal)
-    mm([(R("pa", 128 * b, 128 * b + 128), R("pt", 128 * b, 128 * b + 128), negi, True, True) for b in range(LB)])
-    act(R("pm", 0, 384), R("pa", 0, 384), AF.Copy, scale=-1.0 / 128)
+    exps, u = [], 0
+    for h, (x0, x1) in enumerate(START[K]):
+        via, eng = START_VIA[K][h], start_engines(K, h, len(far))
+        for dd in via + [d for d in (1, 2, 3) if d not in via]:
+            exps.append((h, dd))
+    exps += [(h, 0) for h in range(len(START[K]))]
+    line = []
+    for z, (h, dd) in enumerate(exps):
+        (x0, x1), d, sem = START[K][h], (K + dd) % NR, newsem()
+        raw, rf = R("raw", dd * Q + x0, dd * Q + x1), R("rawf", dd * Q + x0, dd * Q + x1)
+        ld = [dma("sa"[u % 2] if z < 3 else "s", R("raw", raw[3], raw[4], 32 * u, 32 * u + 32), T.ends[32 * d:32 * d + 32, u * Q + x0:u * Q + x1], 128 * wd(raw), sem)
+              for u in range(4)]
+        line.append((ld[0], ld[1], ts(rf, raw, float(MID), None, AL.subtract),
+                     act(R("enc", raw[3], raw[4]) if dd else R("w0", OWN[K] + x0, OWN[K] + x1), rf, AF.Exp, PHASE, ALPHA)))
+        for y in range(4):
+            if z:
+                line[-1][y]["behind"] = [line[-2][y]]
+    exps = [l[3] for l in line]
+    tile = lambda r, h: R("w0", OWN[r] + START[r][h][0], OWN[r] + START[r][h][1])
 
-    def lists(rnd, k):
-        e0, CC = CHK[rnd][k] // 16, (CHK[rnd][k + 1] - CHK[rnd][k]) // 16
-        wn, c0, LC, n3 = w[rnd % 2], Z0 + 16 * e0, 16 * CC, LB * CC
-        t0, t1 = LB * e0, LB * e0 + n3
-        X, CS, Z = R("q1", 0, n3), R("q0", 0, CC), R("qz", 512 - n3, 512 + n3)
-
-        def turn(bank, p0, p1, so):
-            it = [(T[bank][0:CC, i:384:16], T[wn][p0:p1, c0 + i:c0 + LC:16], R("sel", so, so + 24, p0, p1), True, True) for i in range(16)]
-            mm(it, [R(wn, c0, c0 + LC, p0, p1)], [R(bank, 0, 384)], 16 * min(64, CC))
-
-        def ln(bank, r0, r1):
-            return add("a", lambda q: q.activation(T.lt[0:CC, LB * k:LB * k + LB, 32 * r0:32 * r1], T[bank][0:CC, 96 * r0:96 * r1], AF.Ln),
-                       [R(bank, 96 * r0, 96 * r1)], [R("lt", 384 * k + 96 * r0, 384 * k + 96 * r1)], 96 * (r1 - r0) * CY + 0.06)
-
-        def back(b, start):
-            return (R("q1", b * CC, (b + 1) * CC), T.lt[0:CC, LB * k + b, :], R("idf", 0, CC, 0, CC), start, True)
-        if rnd == 0 and k == 0 and EARLY:
-            turn("qz", 32 * K, 32 * K + 32, 0)
-            o = ln("qz", K, K + 1)
-            o["after"] += exps
-            o["dur"] += 1.5
-            turn("q0", 0, 128, 0)
-            for r in range(NR):
-                if r != K:
-                    ln("q0", r, r + 1)["after"].append(o)
-        else:
-            turn("q0", 0, 128, 24)
-            o = ln("q0", 0, NR)
-            if rnd == 0:
-                o["after"] += exps
-                o["dur"] += 1.5 if k == 0 else 0.0
-        if k == 0:
-            cp(R(wn, Z0 - 1, Z0, 0, 32), R(wn, Z0, Z0 + 1, 0, 32))
-            memset(R(wn, Z0, Z0 + 1, 0, 32), 0.0)
-        lt, cl, hb = R("lt", 384 * k, 384 * k + 384), R("cls", t0, t1), 3 * t0
-        mm([back(b, True) for b in range(LB)], [lt], None, 12 * max(64, CC))
-        act(cl, X, AF.Identity, col(3), KI / V)
-        for j in range(3):
-            ts(R("hh", hb + j * n3, hb + (j + 1) * n3), cl, 129.0 + j, None, AL.is_equal, half=True)
-        hj = lambda j, b: R("hh", hb + j * n3 + b * CC, hb + j * n3 + (b + 1) * CC)
-        it = [(CS, R("jw", c - 2 * b, c - 2 * b + 128), hj(j, b), False, False) for b in range(LB) for c, j in ((104, 0), (8, 2), (103, 1))]
-        mm([it[0][:3] + (True, False)] + it[1:-1] + [it[-1][:3] + (False, True)])
-        eo, ini, ex = R("ee", e0 + 1, e0 + CC + 1), R("ee", e0, e0 + 1), R("ee", e0, e0 + CC)
-        vec(lambda q: q.tensor_tensor_scan(AP(eo), AP(CS), T.c256[:, 0:CC], AP(ini), AL.add, AL.min), [ini, CS, R("c256", 0, CC)], [eo], CC)
-        it = []
-        for b in range(LB):
-            z1, z2 = R("qz", 512 - n3 + b * CC, 512 - n3 + (b + 1) * CC), R("qz", 512 + b * CC, 512 + (b + 1) * CC)
-            it += [(z1, bl, hj(0, b), True, False), (z1, R("blw", 0, 128), hj(2, b), False, False), (z1, R("bc", 256 * b, 256 * b + 128), ex, False, True),
-                   (z2, bl, hj(1, b), True, False), (z2, R("bc", 256 * b + 128, 256 * b + 256), ex, False, True)]
-        mm(it)
-        act(R("rl", 2 * t0, 2 * t1), Z, AF.Relu, -(CAP + 31.0))
-        it = []
-        for b in range(LB):
-            f, a = R("q1", b * CC, (b + 1) * CC), 2 * t0 + b * CC
-            it += [(f, R("f1", 0, 128), R("rl", a, a + CC), True, False), (f, negi, R("rl", a + n3, a + n3 + CC), False, False), back(b, False)]
-        mm(it, [lt], None, 18 * max(64, CC))
-        ts(R("off", (rnd % 2) * NL + t0, (rnd % 2) * NL + t1), X, KI, col(4), AL.mult, AL.add)
-
-    for k in range(len(CHK[0]) - 1):
-        lists(0, k)
-    s_y, done = newsem(), []
-
-    def finish(pi):
-        x0, x1 = PIECES[pi]
-        wq, wn = (x1 - x0) // 4, w[RO % 2]
-        for half, dds in enumerate(((2, 3), (0, 1)) if wq > 128 else ((0, 1, 2, 3),)):
-            (bank, z0), l0, l1 = (("q0", 0), ("q1", 0), ("qz", 0), ("qz", 512))[2 * (pi % 2) + half], x0 + dds[0] * wq, x0 + (dds[-1] + 1) * wq
-            mm([(R(bank, z0 + z * wq, z0 + (z + 1) * wq), R("qq", 128 * ((K + dd) % NR) + 4 - u, 128 * ((K + dd) % NR) + 132 - u),
-                 R(wn, Z0 + x0 + u * wq, Z0 + x0 + (u + 1) * wq), u == 0, u == 3) for z, dd in enumerate(dds) for u in range(4)])
-            done.append((x1, act(R("rawf", l0, l1), R(bank, z0, z0 + l1 - l0), AF.Ln), ts(R("u16", l0, l1), R("rawf", l0, l1), KI, C0, AL.mult, AL.add)))
-        exchange(END_VIA[pi], lambda dd: piece_cols(pi, dd), "u16", "land16", lambda dd: "ae%d" % (4 * pi + dd), "he%d" % pi, True)
-        for dd in range(NR):
-            yf, src = R("yf", *piece_cols(pi, dd)), (K - dd) % NR
-            cp(yf, R("land16" if dd else "u16", yf[3], yf[4]))
-            dma("a" if pi >= NP - 2 and dd % 2 else "s", T.y[32 * src:32 * src + 32, x0:x1], yf, 512 * wq, s_y)
-
-    for rnd in range(RO):
-        ws, wt, last = w[rnd % 2], w[(rnd + 1) % 2], rnd == RO - 1
-        parts = LAST if last else PARTS
-        for pi, (x0, x1) in enumerate(parts):
-            k, n = max(z for z, x in enumerate(CHK[rnd]) if x <= x0), x1 - x0
-            ca, cb = CHK[rnd][k], CHK[rnd][k + 1]
-            dst, old = R(wt, Z0 + x0, Z0 + x1), [d for d in done if d[0] + LAG <= x0]
-            for b in range(LB):
-                g0, ps, pz = (item[0] % NG) * GW, PSUM[item[0] % 2], 512 * (item[0] // 2 % 2)
-                item[0] += 1
-                o0 = (rnd % 2) * NL + (LB * ca + b * (cb - ca) + x0 - ca) // 16
-                gt, of, win = R("gt", g0, g0 + n), R("off", o0, o0 + n // 16), R(ws, 0, WW)
-                if (pi, b) in DVE_GATHER[rnd]:
-                    vec(lambda q, gt=gt, win=win, of=of: q.tensor_copy(AP(gt), AP(win).indirect(AP(of))), [win, of], [gt], n * GA)["cls"] = 0
-                else:
-                    add("a", lambda q, gt=gt, win=win, of=of: q.activation(AP(gt), AP(win).indirect(AP(of)), AF.Copy),
-                        [win, of], [gt], n * GA * CY + 0.065, cls=0, behind=[d[1] for d in old])
-                mm([(R(ps, pz, pz + n), R("pm", 128 * b, 128 * b + 128), gt, True, True)])
-                tt(dst, R(ps, pz, pz + n), R(ws, dst[3], dst[4]) if b == 0 else dst, AL.max)["behind"] = [d[2] for d in old]
-                if b == 0 and x0 == 0:
-                    p0 = R(wt, Z0, Z0 + 1, 0, 32)
-                    tt(p0, p0, R(ws, Z0 - 1, Z0, 0, 32), AL.max)
-            if last:
-                for z in range(NP):
-                    if PIECES[z][1] == x1:
-                        finish(z)
-                continue
-            if PE_TAIL and pi == len(parts) - 1:
-                oth = PSUM[item[0] % 2]
-                for j, z in ((1, R(oth, 0, n)), (2, R(oth, 512, 512 + n)), (3, R(ps, 512 - pz, 512 - pz + n))):
-                    mm([(z, R("negi", 32 * j, 32 * j + 128), dst, True, True)])
-                    to = R(wt, dst[3] + j * V, dst[4] + j * V)
-                    if j == 2:
-                        ts(to, z, -1.0 / 128, None, AL.mult)
-                    else:
-                        act(to, z, AF.Copy, scale=-1.0 / 128)
+    def arrive(r, after):
+        for h in range(len(START[r])):
+            arrival(tile(r, h), "as%d" % (2 * r + h), start_engines(r, h, len(far))[(K - r) % NR], after, 0.1, ARRIVE[r][h])
+    for r in range(K + 1, NR):
+        arrive(r, [first])
+    for h, (x0, x1) in enumerate(START[K]):
+        via, eng, xs, e0 = START_VIA[K][h], start_engines(K, h, len(far)), [], 0
+        for dd in (1, 2, 3):
+            src = R("enc", dd * Q + x0, dd * Q + x1)
+            if dd in via:
+                n = len(near) // len(via)
+                xs.append(to_helper(src, near[via.index(dd) * n:via.index(dd) * n + n]))
             else:
-                sr = newsem()
-                for j in range(1, NR):
-                    dma("s", R(wt, dst[3] + j * V, dst[4] + j * V, 0, 128 - 32 * j), R(wt, dst[3], dst[4], 32 * j, 128), (128 - 32 * j) * n * 2, sr)
-            if x1 in CHK[rnd + 1]:
-                lists(rnd + 1, CHK[rnd + 1].index(x1) - 1)
+                xs.append(([T.cores[(K + dd) % NR]], far[e0:e0 + eng[dd]], "as%d" % (2 * K + h), src, tile(K, h)))
+                e0 += eng[dd]
+        send(xs, [tile(START_AFTER[K], 0)] if START_AFTER[K] else [])["due"] = -40.0 + h
+    for r in range(K):
+        arrive(r, sends[-1:])
+
+    arrival(R("rta", 0, LB * NR), "ar", 3 * len(far), [first], RLAT)
+    cp(R("rtb", 0, 12), R("rta", 0, 12))
+    mm([(R("pa", 0, 12), R("rep", 0, 128), R("rtb", 0, 12), True, True)])
+    cp(R("rtc", 0, 12), R("pa", 0, 12))
+    for r in range(NR - 1, -1, -1):
+        z, bank = 384 * (r % 2), 512 * (r % 2)
+        for b in range(LB):
+            ts(R("pt", z + 128 * b, z + 128 * b + 128), fio, col(1), R("rtc", LB * r + b, LB * r + b + 1), AL.subtract, AL.is_equal, half=True)
+        mm([(R("pa", bank + 128 * b, bank + 128 * b + 128), R("pt", z + 128 * b, z + 128 * b + 128), negi, True, True) for b in range(LB)])
+        act(R("pm", 384 * r, 384 * r + 384), R("pa", bank, bank + 384), AF.Copy, scale=-1.0 / BIG)
+
+    def spread(wn, k, apart):
+        sem, c = newsem(), OWN[k]
+        for j in (1, 2, 3):
+            dma("s", R(wn, c + j * Q, c + j * Q + Q, 0, 128 - 32 * j), R(wn, c, c + Q, 32 * j, 128), (128 - 32 * j) * Q * 2, sem)
+        if k:
+            sem = newsem() if apart else sem
+            for j in (1, 2, 3):
+                dma("s", R(wn, c - j * Q, c - j * Q + Q, 32 * j, 128), R(wn, c, c + Q, 0, 128 - 32 * j), (128 - 32 * j) * Q * 2, sem)
+
+    nlist, lns = [0, 0], []
+
+    def lists(rnd, ks):
+        wn, par, quick, n0 = w[rnd], nlist[0] % 3, rnd == 0 and ks == [NR - 1], len(ops)
+        nlist[0] += 1
+        banks = ["pc"] if quick else [PSUM[3 + (nlist[1] + h) % 2] for h in range(len(ks))]
+        nlist[1] += 0 if quick else len(ks)
+        tb, np_ = banks[0], 64 * len(ks) - 16
+        if len(ks) > 1:
+            mm([(R(tb, 0, 384, 32, 64), R("ones", 0, 32), R("ones", 0, 384), True, True)])
+        for h, k in enumerate(ks):
+            c0 = OWN[k]
+            for i0 in (0, 8):
+                mm([(T[tb][64 * h:64 * h + CC, i:384:16], T[wn][:, c0 + i:c0 + Q:16], R("sel", 0, 24), True, True) for i in range(i0, i0 + 8)],
+                   [R(wn, c0, c0 + Q)], [R(tb, 0, 384, 64 * h, 64 * h + CC)], 8 * CC)
+        lt = R("lt", 384 * par, 384 * par + 384)
+        o = add("a", lambda q: q.activation(T.lt[0:np_, LB * par:LB * par + LB, :], T[tb][0:np_, 0:384], AF.Ln, scale=LNS), [R(tb, 0, 384)], [lt], 384 * CY + 0.06)
+        if not lns:
+            o["dur"] += 1.5
+        o["after"] += exps
+        lns.append(o)
+        X = lambda h, b: R(banks[h], b * CC, (b + 1) * CC)
+        back = lambda h, b: (T.lt[0:np_, LB * par + b, :], R("kid", 64 * h, 64 * h + CC, 0, np_))
+        for h in range(len(ks)):
+            for b in range(LB):
+                mm([(X(h, b),) + back(h, b) + (True, True)], [lt], None, 256)
+        for h, k in enumerate(ks):
+            xb = banks[h]
+            off, xh = R("off", (rnd * NR + k) * NL, (rnd * NR + k + 1) * NL), R(xb, 0, NL)
+            if quick:
+                act(R("xa", 0, NL), xh, AF.Abs)
+                ts(off, R("xa", 0, NL), col(6), None, AL.add)
+                continue
+            if k < NR - 1:
+                cb, hb, rb, eb = k * NL, 3 * k * NL, 3 * (k % 2) * NL, 2 * k * CC
+                if "c" in ON_ACT:
+                    act(R("cls", cb, cb + NL), xh, AF.Identity, CB - 0.5 + (MID + 0.5) / V, 1.0 / V)
+                else:
+                    ts(R("cls", cb, cb + NL), xh, 1.0 / V, CB - 0.5 + (MID + 0.5) / V, AL.mult, AL.add)
+                for qq in range(k + 1, NR):
+                    ts(R("hh", hb + (qq - 1) * NL, hb + qq * NL), R("cls", cb, cb + NL), CB + qq, None, AL.is_equal, half=True)
+                if k == 0:
+                    vec(lambda q, h=h: q.tensor_scalar(T.fl[64 * h:64 * h + CC, :, 0:32], T.lt[64 * h:64 * h + CC, LB * par:LB * par + LB, 0:32], (0.5 - MID) / KI, None, AL.is_lt),
+                        [lt], [R("fl", 0, 384)], 96)
+                slots = [(qq, b) for qq in range(k + 1, NR) for b in range(LB)]
+                hq = lambda qq, b: R("hh", hb + (qq - 1) * NL + b * CC, hb + (qq - 1) * NL + (b + 1) * CC)
+                mm(group(R(xb, 400, 400 + CC), [(R("jc", 16 - z, 144 - z), hq(*s)) for z, s in enumerate(slots)]))
+                mm(group(R(xb, 400 + CC, 400 + 2 * CC), [(R("jw", 112 - z, 240 - z), hq(*s)) for z, s in enumerate(slots)]))
+                cs, eo, ex = R(xb, 400, 399 + 2 * CC), R("ee", eb, eb + 2 * CC - 1), R("ee", eb + CC - 1, eb + 2 * CC - 1)
+                vec(lambda q, eo=eo, cs=cs: q.tensor_tensor_scan(AP(eo), AP(cs), T.c256[:, 0:2 * CC - 1], 0.0, AL.add, AL.min), [cs, R("c256", 0, 2 * CC)], [eo], 2 * CC)
+                for z0 in range(0, len(slots), LB):
+                    mm([m for z in range(z0, z0 + LB) for m in group(R(xb, z * CC, (z + 1) * CC), [(bl, hq(*slots[z])), (R("bc", 128 * z, 128 * z + 128), ex)])])
+                if "r" in ON_ACT:
+                    act(R("rl", rb, rb + len(slots) * CC), R(xb, 0, len(slots) * CC), AF.Relu, -(CAP + 31.0))
+                else:
+                    ts(R("rl", rb, rb + len(slots) * CC), R(xb, 0, len(slots) * CC), CAP + 32.0, None, AL.is_ge)
+                for b in range(LB):
+                    terms = [(gapi, R("cls", cb + b * CC, cb + (b + 1) * CC)), back(h, b)]
+                    terms += [(negi, R("rl", rb + z * CC, rb + (z + 1) * CC)) for z, s in enumerate(slots) if s[1] == b]
+                    if k == 0:
+                        terms.append((T.fl[0:np_, b, :], R("negi", 64 * h, 64 * h + CC, 0, np_)))
+                    mm(group(X(h, b), terms), [lt, R("fl", 0, 384)], None, 64 * (len(terms) + 3))
+            ts(off, xh, col(2 + k), None, AL.add)
+        for o in ops[n0:]:
+            o["chain"] = True
+
+    for k in range(NR - 1, -1, -1):
+        spread("w0", k, k == NR - 1)
+    for ks in sorted(BATCH[0], key=lambda ks: K not in ks or K == NR - 1):
+        lists(0, ks)
+    s_y, nd = newsem(), [0]
+
+    def decode(src, r, x0, x1):
+        a, e = r * Q + x0, r * Q + x1
+        bank, z0 = PSUM[3 + nd[0] % 2], 0
+        nd[0] += 1
+        act(R("rawf", a, e), R(src, a, e), AF.Ln, scale=LNS)
+        mm([(R(bank, z0, z0 + e - a), kid, R("rawf", a, e), True, True)], cyc=4 * (e - a))
+        ts(R("yf", a, e), R(bank, z0, z0 + e - a), ROUND + MID, ROUND, AL.add, AL.subtract)
+        for u in range(4):
+            dma("s", T.y[32 * r:32 * r + 32, u * Q + x0:u * Q + x1], R("yf", a, e, 32 * u, 32 * u + 32), 128 * (e - a), s_y)
+
+    steps = [(rnd, k) for rnd in range(RO - 1) for k in range(NR - 1, -1, -1)] + [(RO - 1, k) for k in last_round(K)]
+
+    def grow(si, x0, x1, b):
+        (rnd, k), n = steps[si], x1 - x0
+        ws = w[rnd]
+        win = R(ws, OWN[k] if si == 0 else BEG[k], OWN[k] + V + 16 if k == NR - 1 else WW)
+        dst = R("res", k * Q + x0, k * Q + x1) if rnd == RO - 1 else R(w[rnd + 1], OWN[k] + x0, OWN[k] + x1)
+        g0, ps = (item[0] % NG) * Q, PSUM[item[0] % 3]
+        item[0] += 1
+        nv = DVE_GATHER[si] * n // Q // 32 * 32 if b == DVE_B else 0
+        for y0, y1, e in ((0, nv, "v"), (nv, n, "a")):
+            if y1 > y0:
+                o0 = (rnd * NR + k) * NL + b * CC + (x0 + y0) // 16
+                gt, of = R("gt", g0 + y0, g0 + y1), R("off", o0, o0 + (y1 - y0) // 16)
+                if e == "v":
+                    vec(lambda q, gt=gt, of=of: q.tensor_copy(AP(gt), AP(win).indirect(AP(of))), [win, of], [gt], (y1 - y0) * GA)["cls"] = 0
+                else:
+                    add("a", lambda q, gt=gt, of=of: q.activation(AP(gt), AP(win).indirect(AP(of)), AF.Copy),
+                        [win, of], [gt], (y1 - y0) * GA * CY + 0.065, cls=0)
+        mm([(R(ps, y, min(n, y + 512)), R("pm", 384 * k + 128 * b, 384 * k + 128 * b + 128), R("gt", g0 + y, g0 + min(n, y + 512)), True, True)
+            for y in range(0, n, 512)])
+        tt(dst, R(ps, 0, n), R(ws, OWN[k] + x0, OWN[k] + x1) if b == 0 else dst, AL.max)["beat"] = n / Q
+
+    def done(si, x0, x1):
+        (rnd, k), i = steps[si], si - (RO - 1) * NR
+        if rnd < RO - 1:
+            spread(w[rnd + 1], k, False)
+            for ks in BATCH[rnd + 1]:
+                if ks[-1] == k:
+                    lists(rnd + 1, ks)
+        elif k == K:
+            decode("res", K, x0, x1)
+        elif x1 == Q:
+            xs = [to_helper(R("res", k * Q + x0, k * Q + x1), near) if via else
+                  ([T.cores[k]], far, "ae%d" % (2 * K + h), R("res", k * Q + x0, k * Q + x1), R("land", K * Q + x0, K * Q + x1))
+                  for h, (x0, x1, via) in enumerate(end_pieces(i))]
+            calls = [send(xs)] * 2 if END_VIA[i] else [send([x]) for x in xs]
+            for r in others:
+                if last_round(r)[i] == K:
+                    for h, (x0, x1, via) in enumerate(end_pieces(i)):
+                        arrival(R("land", r * Q + x0, r * Q + x1), "ae%d" % (2 * r + h), len(far), [calls[h]], RLAT * (1.7 if via else 1.0))
+                        late.append(("land", r, x0, x1))
+
+    cuts = lambda si: CUTS[si - (RO - 1) * NR] if si >= (RO - 1) * NR else [0, Q]
+    pieces, late = [(si, x0, x1) for si in range(len(steps)) for x0, x1 in zip(cuts(si), cuts(si)[1:])], []
+    for z, p in enumerate(pieces):
+        if STAGGER:
+            grow(*p, 0)
+        if z:
+            grow(*pieces[z - 1], 2)
+            done(*pieces[z - 1])
+        if not STAGGER:
+            grow(*p, 0)
+        grow(*p, 1)
+        if p[0] == len(steps) - 1:
+            for d in late[:DECODE[z - len(pieces)]]:
+                decode(*d)
+            late = late[DECODE[z - len(pieces)]:]
+    grow(*pieces[-1], 2)
+    done(*pieces[-1])
+    for d in late:
+        decode(*d)
     return ops
 
 
@@ -385,7 +460,7 @@ def depends(ops):
                 o["deps"].update(groups[ops[d]["sem"]])
         o["order"] = o["deps"] | set(a["n"] for a in o["after"])
         if o["eng"] == "t":
-            for bk in set((r[0], r[3] // 512) for r in o["wr"]):
+            for bk in set((r[0], z) for r in o["wr"] for z in (r[3] // 512, (r[4] - 1) // 512)):
                 if bk in lastt:
                     o["order"].add(lastt[bk])
                 lastt[bk] = o["n"]
@@ -394,109 +469,54 @@ def depends(ops):
 
 def schedule(ops):
     n = len(ops)
-    pred = [sorted(o["order"] | set(a["n"] for a in o.get("behind", ()))) for o in ops]
-    hard = [sorted(o["order"]) for o in ops]
+    pred = [o["order"] | set(a["n"] for a in o.get("behind", ())) for o in ops]
     succ = [[] for _ in ops]
     for i in range(n):
         for d in pred[i]:
             succ[d].append(i)
-    isd = [o["kind"] == "d" for o in ops]
-    res = ["dma" if isd[i] else ops[i]["eng"] for i in range(n)]
-    dur = [ops[i]["nbytes"] / DBW + 0.05 if isd[i] else ops[i]["dur"] for i in range(n)]
-    pre = [DLAT + LAT if isd[i] else ops[i].get("lat", LAT) for i in range(n)]
+    left = [len(p) for p in pred]
+    line = [i for i in range(n) if not left[i]]
+    for i in line:
+        for s in succ[i]:
+            left[s] -= 1
+            if not left[s]:
+                line.append(s)
+    t, due = 0.0, [0.0] * n
+    for o in ops:
+        if "beat" in o:
+            t += o["beat"] * BEAT
+            o["due"] = t
+    for i in reversed(line):
+        o = ops[i]
+        e = min([due[s] - ops[s].get("lat", HOP if ops[s]["eng"] != o["eng"] else 0.0) for s in succ[i]] + [o.get("due", t + TAIL)])
+        due[i] = e - o["dur"] - (DLAT + o["nbytes"] / DBW if o["kind"] == "d" else 0.0)
+    for i in range(n):
+        due[i] -= AHEAD[ops[i]["eng"]] if ops[i].get("chain") else 0.0
+    left, ready, free, dfree, seq = [len(p) for p in pred], {}, {}, 0.0, []
 
-    def sgs(key, fwd):
-        before, after = (pred, succ) if fwd else (succ, pred)
-        left = [len(b) for b in before]
-        ready = [i for i in range(n) if not left[i]]
-        st, busy = [0.0] * n, {}
-        while ready:
-            i = min(ready, key=key.get)
-            ready.remove(i)
-            t = max([st[d] + (0.01 - (pre[i] if fwd else dur[i]) if isd[i] and isd[d] else dur[d] + (0.0 if fwd else pre[d]))
-                     for d in before[i]] + [0.0]) + (pre[i] if fwd else 0.0)
-            line, z = busy.setdefault(res[i], []), 0
-            for a, b in line:
-                if b > t:
-                    if a >= t + dur[i] - 1e-9:
-                        break
-                    t = b
-                z += 1
-            line.insert(z, (t, t + dur[i]))
-            st[i] = t
-            for s in after[i]:
-                left[s] -= 1
-                if not left[s]:
-                    ready.append(s)
-        return st
-
-    def replay(seq, f):
-        free, fin, dfree, lastq = {}, [0.0] * n, 0.0, {}
-        for i in seq:
-            o, t, by = ops[i], 0.0, None
-            for d in hard[i]:
-                if fin[d] > t:
-                    t, by = fin[d], d
-            t += o["lat"] * f[2] if "lat" in o else LAT
-            o["byq"] = free.get(o["eng"], 0.0) > t
-            if o["byq"]:
-                t, by = free[o["eng"]], lastq[o["eng"]]
-            o["by"], lastq[o["eng"]] = by, i
-            free[o["eng"]] = fin[i] = t + o["dur"] * (f[o["cls"]] if o["cls"] >= 0 else f[2] if o["kind"] == "x" else 1.0)
-            if isd[i]:
-                dfree = fin[i] = max(fin[i] + DLAT * f[2], dfree) + dur[i] * f[2]
-            o["st"], o["fin"] = t, fin[i]
-        return max(fin)
-
-    def cost(seq):
-        return sum(replay(seq, f) for f in CASES) / len(CASES)
-
-    rng = np.random.default_rng(1)
-    best, key = None, dict((i, float(i)) for i in range(n))
-    for trial in range(TRIES):
-        st = sgs(key, True)
-        if trial % 4 == 2:
-            for fwd in (False, True):
-                st = sgs(dict((i, -(st[i] + dur[i])) for i in range(n)), fwd)
-        seq = sorted(range(n), key=lambda i: (st[i] - (DLAT if isd[i] else 0.0), i))
-        span = cost(seq)
-        if best is None or span < best[0]:
-            best = (span, seq, st)
-        amp, mid, wid = (1.0, 3.0, 6.0)[int(rng.integers(3))], best[0] * rng.random(), (1.5, 4.0)[int(rng.integers(2))]
-        key = dict((i, s + (amp * (rng.random() - 0.5) if abs(s - mid) < wid and rng.random() < 0.4 else 0.0)) for i, s in enumerate(best[2]))
-    cur, crit = best[:2], None
-    for trial in range(MOVES):
-        seq = cur[1]
-        if crit is None:
-            replay(seq, CASES[int(rng.integers(len(CASES)))])
-            crit, j = [], max(range(n), key=lambda z: ops[z]["fin"])
-            while j is not None:
-                if ops[j]["byq"]:
-                    crit += [(j, -1), (ops[j]["by"], 1)]
-                j = ops[j]["by"]
-        if crit and rng.random() < 0.7:
-            i, step = crit[int(rng.integers(len(crit)))]
-            p = seq.index(i)
-        else:
-            p, step = int(rng.integers(n)), (1 if rng.random() < 0.5 else -1)
-            i = seq[p]
-        stop, z, to, hops = set(succ[i] if step > 0 else pred[i]), p + step, None, int(rng.integers(1, 4))
-        while 0 <= z < n and seq[z] not in stop and hops:
-            if ops[seq[z]]["eng"] == ops[i]["eng"]:
-                to, hops = z, hops - 1
-            z += step
-        if to is None:
-            continue
-        new = seq[:p] + seq[p + 1:]
-        new.insert(to, i)
-        span = cost(new)
-        if span <= cur[0] + 0.12 * (1.0 - trial / MOVES):
-            new.sort(key=lambda j: ops[j]["st"])
-            cur, crit = (span, new), None
-            if span < best[0]:
-                best = cur
-    replay(best[1], CASES[0])
-    return best[1]
+    def release(i):
+        o = ops[i]
+        ready[i] = max([o.get("tmin", 0.0)] + [ops[d]["fin"] + o.get("lat", LAT if d in o["deps"] else 0.0) if d in o["order"] else ops[d]["st"]
+                                              for d in pred[i]])
+    for i in range(n):
+        if not left[i]:
+            release(i)
+    while ready:
+        can = dict((i, max(t, free.get(ops[i]["eng"], 0.0))) for i, t in ready.items())
+        i0 = min(can, key=can.get)
+        i = min((j for j in can if ops[j]["eng"] == ops[i0]["eng"] and can[j] <= can[i0] + LOOK), key=lambda j: due[j])
+        o = ops[i]
+        del ready[i]
+        seq.append(i)
+        o["st"] = can[i]
+        free[o["eng"]] = o["fin"] = can[i] + o["dur"]
+        if o["kind"] == "d":
+            dfree = o["fin"] = max(o["fin"] + DLAT, dfree) + o["nbytes"] / DBW + 0.05
+        for s in succ[i]:
+            left[s] -= 1
+            if not left[s]:
+                release(s)
+    return seq
 
 
 def emit(g, T, ops, seq, groups):
@@ -544,8 +564,8 @@ def rank_program(g, core, T, topo):
     rank = T.rank_of(core)
     if rank is None:
         for owner in T.cores:
-            if helper_of(owner, topo) == core:
-                helper_program(g, core, owner, T, topo)
+            if core in helpers_of(owner, topo):
+                helper_program(g, core, owner, helpers_of(owner, topo).index(core), T, topo)
         return
     ops = build_ops(core, rank, T, topo)
     groups = depends(ops)

@@ -21,15 +21,22 @@ CB, BIG = 130.0, 32768.0
 START = [[(0, Q)], [(0, Q)], [(0, Q // 2), (Q // 2, Q)], [(0, Q // 2), (Q // 2, Q)]]
 START_VIA = [[[1]], [[1]], [[1], [2]], [[1], [2]]]
 START_AFTER = [2, 3, None, None]
-BATCH = [[[3], [2], [1], [0]], [[3, 2], [1], [0]], [[3, 2], [1], [0]]]
-CUTS = [[0, Q], [0, Q], [0, 384, Q], [0, 384, 640, Q]]
-END_VIA = [1, 1, 0]
-DVE_GATHER = [320] * 12
-ORDER = 1
+BATCH = [[[3], [2], [1], [0]], [[3], [2], [1], [0]], [[3], [2], [1], [0]]]
+CUTS = [0, 384, 640, Q]
+END_VIA = True
+DVE_GATHER = [320, 320, 320]
+ORDER = 0
 ON_ACT = ""
-STAGGER = True
+STAGGER = False
+REOPEN = True
+MIX = "pa"
 DVE_B = 1
-DECODE = [2, 2, 1]
+LOADS_A = 3
+PERMS = 2
+NSLOT, SPLIT, NLT = 3, 384, 4
+LAG = 900
+DIRECT = 256
+DBEAT = 0.4
 NG = 6
 
 SB = lambda n, dt: ("sbuf", [128, n], dt)
@@ -38,30 +45,31 @@ F32, B16, I32, U16 = "float32", "bfloat16", "int32", "uint16"
 SCRATCH = {
     "raw": SB(V, I32), "rawf": SB(V, F32), "rta": SB(16, I32), "rtb": SB(16, B16), "rtc": SB(16, F32), "enc": SB(V, B16), "land": SB(V, B16),
     "w0": SB(WW, B16), "w1": SB(WW, B16), "w2": SB(WW, B16), "res": SB(V, B16), "gt": SB(NG * Q, B16), "off": SB(RO * NR * NL, U16),
-    "lt": ("sbuf", [128, 3 * LB, 128], F32), "cls": SB(3 * NL, B16), "hh": SB(9 * NL, B16), "rl": SB(6 * NL, B16), "fl": ("sbuf", [128, LB, 128], B16), "ee": SB(6 * CC, B16),
-    "xa": SB(NL, F32), "yf": SB(V, F32), "ones": SB(384, B16), "c256": SB(2 * CC, F32), "fio": SB(144, B16), "col": SB(8, F32),
+    "lt": ("sbuf", [128, NLT * LB, 128], F32), "cls": SB(3 * NL, B16), "hh": SB(9 * NL, B16), "rl": SB(6 * NL, B16), "fl": ("sbuf", [128, LB, 128], B16), "ee": SB(6 * CC, B16),
+    "xa": SB(NL, F32), "yf": SB(V, F32), "ones": SB(128, B16), "f16": SB(128, B16), "c256": SB(2 * CC, F32), "fio": SB(144, B16), "col": SB(8, F32),
     "pint": SB(8, I32), "sel": SB(24, B16), "rep": SB(128, B16), "jw": SB(240, B16), "jc": SB(144, B16), "bl": SB(128, B16), "bc": SB(9 * 128, B16),
-    "negi": SB(128, B16), "gapi": SB(128, B16), "kid": SB(128, F32), "pt": SB(768, B16), "pm": SB(NR * 384, B16),
-    "pa": PS(1024), "pb": PS(1024), "pc": PS(1024), "q0": PS(512), "q1": PS(512),
+    "negi": SB(224, B16), "gapi": SB(128, B16), "kid": SB(128, F32), "pt": SB(NR * 384, B16), "pm": SB(NR * 384, B16),
 }
-PSUM = ("pa", "pb", "pc", "q0", "q1")
+PSUM = ["p%d" % i for i in range(8)]
+SCRATCH.update((p, PS(512)) for p in PSUM)
 SEMAPHORES = (["cp", "cv", "ca", "ct", "sent", "ar"] + ["d%d" % i for i in range(40)]
               + ["as%d" % i for i in range(8)] + ["ae%d" % i for i in range(8)] + ["h%d" % i for i in range(8)])
 
 CY, PCY, GA = 0.00083 * 1.2, 0.00042 * 1.2, 1.56
 LAT, DLAT, DBW, RLAT, RCALL = 0.12, 1.9, 300e3, 4.5, 0.7
 ARRIVE = [[19.0], [16.0], [11.5, 13.5], [9.0, 11.0]]
-BEAT, HOP, LOOK, TAIL, AHEAD = 1.4, 0.2, 0.1, 6.0, {"a": 5.0, "v": 5.0, "t": 1.0}
+BEAT, HOP, LOOK, TAIL, AHEAD = 1.4, 0.2, 0.05, 6.0, {"a": 10.0, "v": 10.0, "t": 2.0}
 
 
 def last_round(K):
-    if ORDER:
-        return [k for k in range(NR - 1, -1, -1) if k != K] + [K]
-    return [k for k in range(NR - 1, -1, -1) if k not in (K, NR - 1 - K)] + [NR - 1 - K, K]
+    a, b, c = [k for k in range(NR - 1, -1, -1) if k != K]
+    H = Q // 2
+    far = [(a, 0, Q), (b, 0, H), (c, 0, H), (c, H, Q), (b, H, Q)] if ORDER else [(a, 0, Q), (b, 0, Q), (c, 0, H), (c, H, Q)]
+    return far + [(K, x0, x1) for x0, x1 in zip(CUTS, CUTS[1:])]
 
 
-def end_pieces(i):
-    return [(0, Q // 2, END_VIA[i]), (Q // 2, Q, 0)]
+def end_sends(K):
+    return [(i, k, h, h == 0 and END_VIA) for i, (k, x0, x1) in enumerate(last_round(K)) if k != K for h in range(2 * x0 // Q, 2 * x1 // Q)]
 
 
 def helpers_of(core, topo):
@@ -73,10 +81,9 @@ def hand_ons(K):
     for h, (x0, x1) in enumerate(START[K]):
         for z, dd in enumerate(START_VIA[K][h]):
             jobs.append((z, (K + dd) % NR, "as%d" % (2 * K + h), "enc", dd * Q + x0, dd * Q + x1, "w0", OWN[K] + x0))
-    for i, k in enumerate(last_round(K)[:-1]):
-        for h, (x0, x1, via) in enumerate(end_pieces(i)):
-            if via:
-                jobs.append((0, k, "ae%d" % (2 * K + h), "res", k * Q + x0, k * Q + x1, "land", K * Q + x0))
+    for i, k, h, via in end_sends(K):
+        if via:
+            jobs.append((0, k, "ae%d" % (2 * K + h), "res", k * Q + h * Q // 2, k * Q + (h + 1) * Q // 2, "land", K * Q + h * Q // 2))
     return [(j[0], "h%d" % n) + j[1:] for n, j in enumerate(jobs)]
 
 
@@ -103,7 +110,7 @@ def start_engines(r, h, nfar):
 
 
 def build_ops(core, K, T, topo):
-    ops, sends, nsem, item = [], [], [0], [0]
+    ops, sends, nsem, item = [], [], [0], [0, 0, 0]
 
     def R(name, c0, c1, p0=0, p1=128):
         return (name, p0, p1, c0, c1)
@@ -186,17 +193,20 @@ def build_ops(core, K, T, topo):
 
     others = [(K + dd) % NR for dd in (1, 2, 3)]
     mine = R("rta", LB * K, LB * K + LB)
-    dma("s", mine, T.rights[:, :], 2000, newsem())
+    dma("s", mine, T.rights[:, :], 2000, newsem())["due"] = -61.0
     first = send([([T.cores[k] for k in others], far, "ar", mine, mine)])
     first["due"] = -60.0
 
     col = lambda j, p0=0, p1=128: R("col", j, j + 1, p0, p1)
     ones, fio, negi, gapi, kid, w = R("ones", 0, 128), R("fio", 0, 128), R("negi", 0, 128), R("gapi", 0, 128), R("kid", 0, 128), ("w0", "w1", "w2")
     pi0, pi1, pi2 = R("pint", 0, 1), R("pint", 1, 2), R("pint", 2, 3)
-    memset(R("ones", 0, 384), 0.0)
-    act(R("ones", 0, 384), R("ones", 0, 384), AF.Exp)["dur"] += 1.3
+    memset(ones, 1.0)
+    memset(R("c256", 0, 2 * CC), 0.0)
+    o = act(R("c256", 0, 2 * CC), R("c256", 0, 2 * CC), AF.Exp, math.log(CAP))
+    o["dur"], o["due"] = o["dur"] + 1.3, -50.0
     add("p", lambda q: q.iota(AP(pi0), [[1, 1]], 0, 1), [], [pi0], 0.14)
     add("p", lambda q: q.iota(T.fio[:, :], [[1, 144]], 0, 0, allow_small_or_imprecise_dtypes=True), [], [R("fio", 0, 144)], 0.4)
+    add("p", lambda q: q.iota(T.f16[:, :], [[16, 8], [0, 16]], 0, 0, allow_small_or_imprecise_dtypes=True), [], [R("f16", 0, 128)], 0.4)
     select(R("rep", 0, 128), ones, [[0, 4], [-1, 32]], AL.is_equal, 0.0, -32 * K, 1)
     select(R("sel", 0, 24), R("ones", 0, 24), [[-1, 3], [-16, 8]], AL.is_equal, 0.0, 0, 1)
     cp(col(0), pi0)
@@ -207,13 +217,13 @@ def build_ops(core, K, T, topo):
         ts(col(2 + k), pi2, -Q / 32.0, MID + 16 - BEG[k] + (k * GAP if k == NR - 1 else -CB * GAP), AL.mult, AL.add)
     ts(col(6), pi2, -Q / 32.0, float(MID - 3 * V), AL.mult, AL.add)
     ts(negi, fio, col(0), -BIG, AL.is_equal, AL.mult, half=True)
+    memset(R("negi", 128, 224), 0.0)
     ts(kid, fio, col(0), KI, AL.is_equal, AL.mult)
     ts(gapi, fio, col(0), float(GAP), AL.is_equal, AL.mult, half=True)
     memset(R("jw", 0, 96), 0.0)
     ts(R("jw", 96, 240), R("fio", 0, 144), col(1), 16.0, AL.subtract, AL.is_equal, half=True)
     tt(R("jc", 0, 144), R("jw", 64, 208), R("jw", 32, 176), AL.add)
     tt(R("jc", 0, 144), R("jc", 0, 144), R("jw", 0, 144), AL.add)
-    memset(R("c256", 0, 2 * CC), float(CAP))
     vec(lambda q: q.memset(T.fl[:, :, :], 0.0), [], [R("fl", 0, 384)], 192)
     for nm in w:
         zs = [R(nm, c, c + 1) for c in BEG[1:NR]]
@@ -227,27 +237,29 @@ def build_ops(core, K, T, topo):
     select(bl, ones, [[1, 128]], AL.is_gt, 0.0, 0, -1)
     select(bl, bl, [[-16, 8], [0, 16]], AL.is_ge, 0.0, 0, 1)
     select(bl, bl, [[1, 128]], AL.not_equal, 32.0, 0, -1)
-    for z in (1, 2, 3):
-        select(R("bc", 384 * z - 384, 384 * z), R("ones", 0, 384), [[1, 3], [16, 8], [0, 16]], AL.is_equal, 0.0, 3 * z - 3, -1)
+    for z in range(9):
+        ts(R("bc", 128 * z, 128 * z + 128), R("f16", 0, 128), col(0), -float(z), AL.subtract, AL.is_equal, half=True)
 
     exps, u = [], 0
     for h, (x0, x1) in enumerate(START[K]):
         via, eng = START_VIA[K][h], start_engines(K, h, len(far))
         for dd in via + [d for d in (1, 2, 3) if d not in via]:
             exps.append((h, dd))
-    exps += [(h, 0) for h in range(len(START[K]))]
+    own = [(h, 0) for h in range(len(START[K]))]
+    exps = exps + own if K == NR - 1 else own + exps
     line = []
     for z, (h, dd) in enumerate(exps):
         (x0, x1), d, sem = START[K][h], (K + dd) % NR, newsem()
         raw, rf = R("raw", dd * Q + x0, dd * Q + x1), R("rawf", dd * Q + x0, dd * Q + x1)
-        ld = [dma("sa"[u % 2] if z < 3 else "s", R("raw", raw[3], raw[4], 32 * u, 32 * u + 32), T.ends[32 * d:32 * d + 32, u * Q + x0:u * Q + x1], 128 * wd(raw), sem)
+        ld = [dma("sa"[u % 2] if z < LOADS_A else "s", R("raw", raw[3], raw[4], 32 * u, 32 * u + 32), T.ends[32 * d:32 * d + 32, u * Q + x0:u * Q + x1], 128 * wd(raw), sem)
               for u in range(4)]
-        line.append((ld[0], ld[1], ts(rf, raw, float(MID), None, AL.subtract),
+        for u in range(4):
+            ld[u]["due"] = -59.0 + 0.1 * (4 * z + u)
+        line.append((ts(rf, raw, float(MID), None, AL.subtract),
                      act(R("enc", raw[3], raw[4]) if dd else R("w0", OWN[K] + x0, OWN[K] + x1), rf, AF.Exp, PHASE, ALPHA)))
-        for y in range(4):
-            if z:
-                line[-1][y]["behind"] = [line[-2][y]]
-    exps = [l[3] for l in line]
+        for y in range(2):
+            line[-1][y]["due"] = -45.0 + 0.1 * z
+    exps = [l[1] for l in line]
     tile = lambda r, h: R("w0", OWN[r] + START[r][h][0], OWN[r] + START[r][h][1])
 
     def arrive(r, after):
@@ -271,63 +283,98 @@ def build_ops(core, K, T, topo):
 
     arrival(R("rta", 0, LB * NR), "ar", 3 * len(far), [first], RLAT)
     cp(R("rtb", 0, 12), R("rta", 0, 12))
-    mm([(R("pa", 0, 12), R("rep", 0, 128), R("rtb", 0, 12), True, True)])
-    cp(R("rtc", 0, 12), R("pa", 0, 12))
-    for r in range(NR - 1, -1, -1):
-        z, bank = 384 * (r % 2), 512 * (r % 2)
-        for b in range(LB):
-            ts(R("pt", z + 128 * b, z + 128 * b + 128), fio, col(1), R("rtc", LB * r + b, LB * r + b + 1), AL.subtract, AL.is_equal, half=True)
-        mm([(R("pa", bank + 128 * b, bank + 128 * b + 128), R("pt", z + 128 * b, z + 128 * b + 128), negi, True, True) for b in range(LB)])
-        act(R("pm", 384 * r, 384 * r + 384), R("pa", bank, bank + 384), AF.Copy, scale=-1.0 / BIG)
+    def slot():
+        item[1] += 1
+        return PSUM[(item[1] - 1) % NSLOT]
 
-    def spread(wn, k, apart):
-        sem, c = newsem(), OWN[k]
+    def keep():
+        item[2] += 1
+        return PSUM[NSLOT + (item[2] - 1) % (len(PSUM) - NSLOT)]
+    z = R(slot(), 0, 12)
+    mm([(z, R("rep", 0, 128), R("rtb", 0, 12), True, True)])
+    cp(R("rtc", 0, 12), z)
+    for r in range(NR - 1, -1, -1):
+        for b in range(LB):
+            ts(R("pt", 384 * r + 128 * b, 384 * r + 128 * b + 128), fio, col(1), R("rtc", LB * r + b, LB * r + b + 1), AL.subtract, AL.is_equal, half=True)
+
+    def permutation(r, bank, z):
+        mm([(R(bank, z + 128 * b, z + 128 * b + 128), R("pt", 384 * r + 128 * b, 384 * r + 128 * b + 128), negi, True, True) for b in range(LB)])
+        ts(R("pm", 384 * r, 384 * r + 384), R(bank, z, z + 384), -1.0 / BIG, None, AL.mult)
+    for r in range(NR - 1, NR - 1 - PERMS, -1):
+        permutation(r, slot(), 0)
+
+    def spread(wn, k, first=False):
+        sem, c, n = newsem(), OWN[k], Q // 2 if first else Q
         for j in (1, 2, 3):
-            dma("s", R(wn, c + j * Q, c + j * Q + Q, 0, 128 - 32 * j), R(wn, c, c + Q, 32 * j, 128), (128 - 32 * j) * Q * 2, sem)
+            dma("s", R(wn, c + j * Q, c + j * Q + n, 0, 128 - 32 * j), R(wn, c, c + n, 32 * j, 128), (128 - 32 * j) * n * 2, sem)
+        if first:
+            sem = newsem()
+            for j in (1, 2, 3):
+                bank, z = slot(), 0
+                mm([(R(bank, z, z + n), R("negi", 32 * j, 32 * j + 128), R(wn, c + n, c + Q), True, True)])
+                to, z = R(wn, c + j * Q + n, c + j * Q + Q, 0, 128 - 32 * j), R(bank, z, z + n, 0, 128 - 32 * j)
+                if j == 1:
+                    act(to, z, AF.Copy, scale=-1.0 / BIG)
+                else:
+                    ts(to, z, -1.0 / BIG, None, AL.mult)
         if k:
-            sem = newsem() if apart else sem
             for j in (1, 2, 3):
                 dma("s", R(wn, c - j * Q, c - j * Q + Q, 32 * j, 128), R(wn, c, c + Q, 0, 128 - 32 * j), (128 - 32 * j) * Q * 2, sem)
 
     nlist, lns = [0, 0], []
 
+    def ln(out, src, rd, wr):
+        o = add("a", lambda q: q.activation(out, src, AF.Ln, scale=LNS), [rd], [wr], 384 * CY + 0.06)
+        if not lns:
+            o["dur"], o["due"] = o["dur"] + 1.5, -30.0
+        o["after"] += exps + lns[:1]
+        lns.append(o)
+
+    def first_lists(par):
+        n0, c = len(ops), CC // 2
+        for h in range(2):
+            c0, pc, z = OWN[NR - 1] + h * Q // 2, keep(), 0
+            mm([(T[pc][0:c, z + i:z + 384:16], T.w0[:, c0 + i:c0 + Q // 2:16], R("sel", 0, 24), True, True) for i in range(16)],
+               [R("w0", c0, c0 + Q // 2)], [R(pc, z, z + 384)], 16 * c)
+            lt = R("lt", 384 * par, 384 * par + 384, 64 * h, 64 * h + c)
+            ln(T.lt[64 * h:64 * h + c, LB * par:LB * par + LB, :], T[pc][0:c, z:z + 384], R(pc, z, z + 384), lt)
+            mm([(R(pc, z + b * c, z + (b + 1) * c), T.lt[64 * h:64 * h + c, LB * par + b, :], R("kid", 64 * h, 64 * h + c, 64 * h, 64 * h + c), True, True)
+                for b in range(LB)], [lt], None, 256 * LB)
+            xa = R("xa", h * LB * c, (h + 1) * LB * c)
+            act(xa, R(pc, z, z + LB * c), AF.Abs)
+            ts(R("off", (NR - 1) * NL + xa[3], (NR - 1) * NL + xa[4]), xa, col(6), None, AL.add)
+        for o in ops[n0:]:
+            o["chain"] = True
+
     def lists(rnd, ks):
-        wn, par, quick, n0 = w[rnd], nlist[0] % 3, rnd == 0 and ks == [NR - 1], len(ops)
+        wn, par, n0 = w[rnd], nlist[0] % NLT, len(ops)
         nlist[0] += 1
-        banks = ["pc"] if quick else [PSUM[3 + (nlist[1] + h) % 2] for h in range(len(ks))]
-        nlist[1] += 0 if quick else len(ks)
-        tb, np_ = banks[0], 64 * len(ks) - 16
-        if len(ks) > 1:
-            mm([(R(tb, 0, 384, 32, 64), R("ones", 0, 32), R("ones", 0, 384), True, True)])
+        if rnd == 0 and ks == [NR - 1]:
+            return first_lists(par)
+        work = [keep() for k in ks]
+        banks = [keep() if REOPEN and k < NR - 1 else work[h] for h, k in enumerate(ks)]
+        tb, np_ = work[0], 64 * len(ks) - 16
         for h, k in enumerate(ks):
             c0 = OWN[k]
             for i0 in (0, 8):
                 mm([(T[tb][64 * h:64 * h + CC, i:384:16], T[wn][:, c0 + i:c0 + Q:16], R("sel", 0, 24), True, True) for i in range(i0, i0 + 8)],
                    [R(wn, c0, c0 + Q)], [R(tb, 0, 384, 64 * h, 64 * h + CC)], 8 * CC)
         lt = R("lt", 384 * par, 384 * par + 384)
-        o = add("a", lambda q: q.activation(T.lt[0:np_, LB * par:LB * par + LB, :], T[tb][0:np_, 0:384], AF.Ln, scale=LNS), [R(tb, 0, 384)], [lt], 384 * CY + 0.06)
-        if not lns:
-            o["dur"] += 1.5
-        o["after"] += exps
-        lns.append(o)
+        ln(T.lt[0:np_, LB * par:LB * par + LB, :], T[tb][0:np_, 0:384], R(tb, 0, 384), lt)
         X = lambda h, b: R(banks[h], b * CC, (b + 1) * CC)
         back = lambda h, b: (T.lt[0:np_, LB * par + b, :], R("kid", 64 * h, 64 * h + CC, 0, np_))
         for h in range(len(ks)):
             for b in range(LB):
-                mm([(X(h, b),) + back(h, b) + (True, True)], [lt], None, 256)
+                mm([(R(work[h], b * CC, (b + 1) * CC),) + back(h, b) + (True, True)], [lt], None, 256)
         for h, k in enumerate(ks):
-            xb = banks[h]
-            off, xh = R("off", (rnd * NR + k) * NL, (rnd * NR + k + 1) * NL), R(xb, 0, NL)
-            if quick:
-                act(R("xa", 0, NL), xh, AF.Abs)
-                ts(off, R("xa", 0, NL), col(6), None, AL.add)
-                continue
+            xb = work[h]
+            off, xh = R("off", (rnd * NR + k) * NL, (rnd * NR + k + 1) * NL), R(banks[h], 0, NL)
             if k < NR - 1:
                 cb, hb, rb, eb = k * NL, 3 * k * NL, 3 * (k % 2) * NL, 2 * k * CC
                 if "c" in ON_ACT:
                     act(R("cls", cb, cb + NL), xh, AF.Identity, CB - 0.5 + (MID + 0.5) / V, 1.0 / V)
                 else:
-                    ts(R("cls", cb, cb + NL), xh, 1.0 / V, CB - 0.5 + (MID + 0.5) / V, AL.mult, AL.add)
+                    ts(R("cls", cb, cb + NL), R(xb, 0, NL), 1.0 / V, CB - 0.5 + (MID + 0.5) / V, AL.mult, AL.add)
                 for qq in range(k + 1, NR):
                     ts(R("hh", hb + (qq - 1) * NL, hb + qq * NL), R("cls", cb, cb + NL), CB + qq, None, AL.is_equal, half=True)
                 if k == 0:
@@ -339,18 +386,31 @@ def build_ops(core, K, T, topo):
                 mm(group(R(xb, 400 + CC, 400 + 2 * CC), [(R("jw", 112 - z, 240 - z), hq(*s)) for z, s in enumerate(slots)]))
                 cs, eo, ex = R(xb, 400, 399 + 2 * CC), R("ee", eb, eb + 2 * CC - 1), R("ee", eb + CC - 1, eb + 2 * CC - 1)
                 vec(lambda q, eo=eo, cs=cs: q.tensor_tensor_scan(AP(eo), AP(cs), T.c256[:, 0:2 * CC - 1], 0.0, AL.add, AL.min), [cs, R("c256", 0, 2 * CC)], [eo], 2 * CC)
+                if REOPEN:
+                    mm([(xh, gapi, R("cls", cb, cb + NL), True, False)])
+                    for b in range(LB):
+                        mm([(X(h, b),) + back(h, b) + (False, False)], [lt], None, 256)
+                    if k == 0:
+                        mm([(X(h, b), T.fl[0:np_, b, :], R("negi", 64 * h, 64 * h + CC, 0, np_), False, False) for b in range(LB) if k == 0], [R("fl", 0, 384)] * (k == 0))
                 for z0 in range(0, len(slots), LB):
+                    if REOPEN:
+                        a = hq(*slots[z0])[3]
+                        mm([(R(xb, z0 * CC, z0 * CC + NL), bl, R("hh", a, a + NL), True, False)]
+                           + [(R(xb, z * CC, (z + 1) * CC), R("bc", 128 * z, 128 * z + 128), ex, False, z == z0 + LB - 1) for z in range(z0, z0 + LB)])
+                        continue
                     mm([m for z in range(z0, z0 + LB) for m in group(R(xb, z * CC, (z + 1) * CC), [(bl, hq(*slots[z])), (R("bc", 128 * z, 128 * z + 128), ex)])])
                 if "r" in ON_ACT:
                     act(R("rl", rb, rb + len(slots) * CC), R(xb, 0, len(slots) * CC), AF.Relu, -(CAP + 31.0))
                 else:
                     ts(R("rl", rb, rb + len(slots) * CC), R(xb, 0, len(slots) * CC), CAP + 32.0, None, AL.is_ge)
-                for b in range(LB):
+                if REOPEN:
+                    mm([(xh, negi, R("rl", rb + z * NL, rb + (z + 1) * NL), False, z == NR - 2 - k) for z in range(NR - 1 - k)])
+                for b in range(0 if REOPEN else LB):
                     terms = [(gapi, R("cls", cb + b * CC, cb + (b + 1) * CC)), back(h, b)]
                     terms += [(negi, R("rl", rb + z * CC, rb + (z + 1) * CC)) for z, s in enumerate(slots) if s[1] == b]
                     if k == 0:
                         terms.append((T.fl[0:np_, b, :], R("negi", 64 * h, 64 * h + CC, 0, np_)))
-                    mm(group(X(h, b), terms), [lt, R("fl", 0, 384)], None, 64 * (len(terms) + 3))
+                    mm(group(X(h, b), terms), [lt] + [R("fl", 0, 384)] * (k == 0), None, 64 * (len(terms) + 3))
             ts(off, xh, col(2 + k), None, AL.add)
         for o in ops[n0:]:
             o["chain"] = True
@@ -363,60 +423,79 @@ def build_ops(core, K, T, topo):
 
     def decode(src, r, x0, x1):
         a, e = r * Q + x0, r * Q + x1
-        bank, z0 = PSUM[3 + nd[0] % 2], 0
+        way = "v" if e - a <= DIRECT else MIX[nd[0] % len(MIX)] if at[0] >= V else "p"
         nd[0] += 1
+        bank, z0 = keep() if way == "p" else None, 0
         act(R("rawf", a, e), R(src, a, e), AF.Ln, scale=LNS)
-        mm([(R(bank, z0, z0 + e - a), kid, R("rawf", a, e), True, True)], cyc=4 * (e - a))
-        ts(R("yf", a, e), R(bank, z0, z0 + e - a), ROUND + MID, ROUND, AL.add, AL.subtract)
+        if way != "p":
+            if way == "v":
+                ts(R("yf", a, e), R("rawf", a, e), KI, ROUND + MID, AL.mult, AL.add)
+            else:
+                act(R("yf", a, e), R("rawf", a, e), AF.Identity, ROUND + MID, KI)
+            ts(R("yf", a, e), R("yf", a, e), ROUND, None, AL.subtract)
+        else:
+            mm([(R(bank, z0, z0 + e - a), kid, R("rawf", a, e), True, True)], cyc=4 * (e - a))
+            ts(R("yf", a, e), R(bank, z0, z0 + e - a), ROUND + MID, ROUND, AL.add, AL.subtract)
+        ops[-1]["beat"] = DBEAT
         for u in range(4):
             dma("s", T.y[32 * r:32 * r + 32, u * Q + x0:u * Q + x1], R("yf", a, e, 32 * u, 32 * u + 32), 128 * (e - a), s_y)
 
-    steps = [(rnd, k) for rnd in range(RO - 1) for k in range(NR - 1, -1, -1)] + [(RO - 1, k) for k in last_round(K)]
-
-    def grow(si, x0, x1, b):
-        (rnd, k), n = steps[si], x1 - x0
-        ws = w[rnd]
-        win = R(ws, OWN[k] if si == 0 else BEG[k], OWN[k] + V + 16 if k == NR - 1 else WW)
+    def grow(rnd, k, x0, x1, b):
+        ws, n, quick = w[rnd], x1 - x0, rnd == 0 and k == NR - 1
+        win = R(ws, OWN[k] if quick else BEG[k], OWN[k] + V + 16 if k == NR - 1 else WW)
         dst = R("res", k * Q + x0, k * Q + x1) if rnd == RO - 1 else R(w[rnd + 1], OWN[k] + x0, OWN[k] + x1)
-        g0, ps = (item[0] % NG) * Q, PSUM[item[0] % 3]
+        g0 = (item[0] % NG) * Q
         item[0] += 1
-        nv = DVE_GATHER[si] * n // Q // 32 * 32 if b == DVE_B else 0
+        nv = DVE_GATHER[rnd] * n // Q // 32 * 32 if b == DVE_B else 0
         for y0, y1, e in ((0, nv, "v"), (nv, n, "a")):
             if y1 > y0:
-                o0 = (rnd * NR + k) * NL + b * CC + (x0 + y0) // 16
+                o0 = (rnd * NR + k) * NL + ((LB * x0 + b * n + y0) // 16 if quick else b * CC + (x0 + y0) // 16)
                 gt, of = R("gt", g0 + y0, g0 + y1), R("off", o0, o0 + (y1 - y0) // 16)
                 if e == "v":
                     vec(lambda q, gt=gt, of=of: q.tensor_copy(AP(gt), AP(win).indirect(AP(of))), [win, of], [gt], (y1 - y0) * GA)["cls"] = 0
                 else:
                     add("a", lambda q, gt=gt, of=of: q.activation(AP(gt), AP(win).indirect(AP(of)), AF.Copy),
                         [win, of], [gt], (y1 - y0) * GA * CY + 0.065, cls=0)
-        mm([(R(ps, y, min(n, y + 512)), R("pm", 384 * k + 128 * b, 384 * k + 128 * b + 128), R("gt", g0 + y, g0 + min(n, y + 512)), True, True)
-            for y in range(0, n, 512)])
-        tt(dst, R(ps, 0, n), R(ws, OWN[k] + x0, OWN[k] + x1) if b == 0 else dst, AL.max)["beat"] = n / Q
+        for y0, y1 in ((0, n),) if n <= 512 else ((0, SPLIT), (SPLIT, n)):
+            ps, to = R(slot(), 0, y1 - y0), R(dst[0], dst[3] + y0, dst[3] + y1)
+            mm([(ps, R("pm", 384 * k + 128 * b, 384 * k + 128 * b + 128), R("gt", g0 + y0, g0 + y1), True, True)])
+            tt(to, ps, R(ws, OWN[k] + x0 + y0, OWN[k] + x0 + y1) if b == 0 else to, AL.max)["beat"] = (y1 - y0) / Q
 
-    def done(si, x0, x1):
-        (rnd, k), i = steps[si], si - (RO - 1) * NR
+    H, at = Q // 2, [0]
+    coming = sorted((sum(p[2] - p[1] for p in last_round(r)[:i + 1]), via, r, h) for r in others for i, k, h, via in end_sends(r) if k == K)
+    late = []
+
+    def done(rnd, k, x0, x1):
         if rnd < RO - 1:
-            spread(w[rnd + 1], k, False)
-            for ks in BATCH[rnd + 1]:
-                if ks[-1] == k:
-                    lists(rnd + 1, ks)
-        elif k == K:
+            if x1 == Q:
+                spread(w[rnd + 1], k)
+                for ks in BATCH[rnd + 1]:
+                    if ks[-1] == k:
+                        lists(rnd + 1, ks)
+            return
+        at[0] += x1 - x0
+        now = ops[-1]
+        if k != K:
+            xs = [to_helper(R("res", k * Q + h * H, k * Q + h * H + H), near) if via else
+                  ([T.cores[k]], far, "ae%d" % (2 * K + h), R("res", k * Q + h * H, k * Q + h * H + H), R("land", K * Q + h * H, K * Q + h * H + H))
+                  for i, kk, h, via in end_sends(K) if kk == k and x0 <= h * H < x1]
+            for call in [xs] if END_VIA else [[x] for x in xs]:
+                send(call)
+        while coming and coming[0][0] <= at[0]:
+            pos, via, r, h = coming.pop(0)
+            arrival(R("land", r * Q + h * H, r * Q + h * H + H), "ae%d" % (2 * r + h), len(far), [now], RCALL + RLAT * (1.7 if via else 1.0))
+            late.append((pos + LAG * (1.7 if via else 1.0), r, h * H, h * H + H))
+        late.sort()
+        while late and late[0][0] <= at[0]:
+            decode("land", *late.pop(0)[1:])
+        if k == K:
             decode("res", K, x0, x1)
-        elif x1 == Q:
-            xs = [to_helper(R("res", k * Q + x0, k * Q + x1), near) if via else
-                  ([T.cores[k]], far, "ae%d" % (2 * K + h), R("res", k * Q + x0, k * Q + x1), R("land", K * Q + x0, K * Q + x1))
-                  for h, (x0, x1, via) in enumerate(end_pieces(i))]
-            calls = [send(xs)] * 2 if END_VIA[i] else [send([x]) for x in xs]
-            for r in others:
-                if last_round(r)[i] == K:
-                    for h, (x0, x1, via) in enumerate(end_pieces(i)):
-                        arrival(R("land", r * Q + x0, r * Q + x1), "ae%d" % (2 * r + h), len(far), [calls[h]], RLAT * (1.7 if via else 1.0))
-                        late.append(("land", r, x0, x1))
 
-    cuts = lambda si: CUTS[si - (RO - 1) * NR] if si >= (RO - 1) * NR else [0, Q]
-    pieces, late = [(si, x0, x1) for si in range(len(steps)) for x0, x1 in zip(cuts(si), cuts(si)[1:])], []
+    pieces = [(0, NR - 1, 0, H), (0, NR - 1, H, Q)] + [(rnd, k, 0, Q) for rnd in range(RO - 1) for k in range(NR - 1, -1, -1)][1:]
+    pieces += [(RO - 1,) + p for p in last_round(K)]
     for z, p in enumerate(pieces):
+        if p[0] == 0 and 0 < p[1] <= NR - PERMS and p[3] == Q:
+            permutation(p[1] - 1, slot(), 0)
         if STAGGER:
             grow(*p, 0)
         if z:
@@ -425,14 +504,10 @@ def build_ops(core, K, T, topo):
         if not STAGGER:
             grow(*p, 0)
         grow(*p, 1)
-        if p[0] == len(steps) - 1:
-            for d in late[:DECODE[z - len(pieces)]]:
-                decode(*d)
-            late = late[DECODE[z - len(pieces)]:]
     grow(*pieces[-1], 2)
     done(*pieces[-1])
     for d in late:
-        decode(*d)
+        decode("land", *d[1:])
     return ops
 
 
@@ -490,6 +565,8 @@ def schedule(ops):
         o = ops[i]
         e = min([due[s] - ops[s].get("lat", HOP if ops[s]["eng"] != o["eng"] else 0.0) for s in succ[i]] + [o.get("due", t + TAIL)])
         due[i] = e - o["dur"] - (DLAT + o["nbytes"] / DBW if o["kind"] == "d" else 0.0)
+        if o.get("due", 0.0) < 0.0:
+            due[i] = o["due"]
     for i in range(n):
         due[i] -= AHEAD[ops[i]["eng"]] if ops[i].get("chain") else 0.0
     left, ready, free, dfree, seq = [len(p) for p in pred], {}, {}, 0.0, []

@@ -1,7 +1,6 @@
 import math
-import numpy as np
 from concourse.bass import DstId, RemoteDMATransfer
-from concourse.mybir import AluOpType as AL, ActivationFunctionType as AF, AxisListType as AX
+from concourse.mybir import AluOpType as AL, ActivationFunctionType as AF
 
 V, CAP, LB, RO, NR = 3072, 256, 3, 3, 4
 ALPHA = math.log(2.0) / 98.0
@@ -11,6 +10,7 @@ KI = 1.0 / ALPHA
 LNS = math.exp(0.0000192 - PHASE)
 ROUND = 12582912.0
 Q = V // 4
+H = Q // 2
 CC = Q // 16
 NL = LB * CC
 GAP = 3 * Q + 16
@@ -18,58 +18,56 @@ OWN = [16 + k * (V + GAP) for k in range(NR + 1)]
 BEG = [0] + [c - GAP for c in OWN[1:]]
 WW = OWN[NR] + 16
 CB, BIG = 130.0, 32768.0
-START = [[(0, Q)], [(0, Q)], [(0, Q // 2), (Q // 2, Q)], [(0, Q // 2), (Q // 2, Q)]]
-START_VIA = [[[1]], [[1]], [[1], [2]], [[1], [2]]]
-START_AFTER = [2, 3, None, None]
-BATCH = [[[3], [2], [1], [0]], [[3], [2], [1], [0]], [[3], [2], [1], [0]]]
-CUTS = [0, 384, 640, Q]
-END_VIA = True
-DVE_GATHER = [320, 320, 320]
-ORDER = 0
-ON_ACT = ""
-STAGGER = False
-REOPEN = True
-MIX = "pa"
-DVE_B = 1
+START = [[(0, Q)], [(0, Q)], [(0, H), (H, Q)], [(0, H), (H, Q)]]
+CALLS = [[[(dd, 0, int(dd == 1))] for dd in (1, 2, 3)]] * 2 + [[[(dd, h, int(h == 0 and dd < 3))] for h in (0, 1) for dd in (1, 2, 3)]] * 2
+SWEEP = [[3, 2, 1, 0], [3, 2, 0, 1], [3, 2, 1, 0], [3, 2, 0, 1]]
+LAST = [[2, 1, 3], [3, 0, 2], [3, 1, 0], [2, 0, 1]]
+CUTS = [0, 256, 512, Q]
+END_VIA = 1
+DVE_GATHER = [416, 416, 512]
 LOADS_A = 3
-PERMS = 2
-NSLOT, SPLIT, NLT = 3, 384, 4
-LAG = 900
+PERMS = 4
+NSLOT, NLT, NG = 3, 4, 6
+LAG = 1200
 DIRECT = 256
-DBEAT = 0.4
-NG = 6
+ON_ACT = ""
+OWN_LAST = 0
+FIRST, AHEAD0, SPREAD1 = 0.0, 1.0, 3.0
+OWN_LIST = False
+HALVE = False
+PAIR = True
+PKEEP = False
+WHOLE = False
 
 SB = lambda n, dt: ("sbuf", [128, n], dt)
-PS = lambda n: ("psum", [128, n], "float32")
 F32, B16, I32, U16 = "float32", "bfloat16", "int32", "uint16"
 SCRATCH = {
     "raw": SB(V, I32), "rawf": SB(V, F32), "rta": SB(16, I32), "rtb": SB(16, B16), "rtc": SB(16, F32), "enc": SB(V, B16), "land": SB(V, B16),
     "w0": SB(WW, B16), "w1": SB(WW, B16), "w2": SB(WW, B16), "res": SB(V, B16), "gt": SB(NG * Q, B16), "off": SB(RO * NR * NL, U16),
-    "lt": ("sbuf", [128, NLT * LB, 128], F32), "cls": SB(3 * NL, B16), "hh": SB(9 * NL, B16), "rl": SB(6 * NL, B16), "fl": ("sbuf", [128, LB, 128], B16), "ee": SB(6 * CC, B16),
-    "xa": SB(NL, F32), "yf": SB(V, F32), "ones": SB(128, B16), "f16": SB(128, B16), "c256": SB(2 * CC, F32), "fio": SB(144, B16), "col": SB(8, F32),
-    "pint": SB(8, I32), "sel": SB(24, B16), "rep": SB(128, B16), "jw": SB(240, B16), "jc": SB(144, B16), "bl": SB(128, B16), "bc": SB(9 * 128, B16),
-    "negi": SB(224, B16), "gapi": SB(128, B16), "kid": SB(128, F32), "pt": SB(NR * 384, B16), "pm": SB(NR * 384, B16),
+    "lt": SB(384, F32), "lc": SB(NLT * 384, B16), "lv": SB(2 * NLT * NL, F32), "cls": SB(3 * NL, B16), "hh": SB(9 * NL, B16),
+    "rl": SB(8 * NL, B16), "ee": SB(6 * CC, B16), "xa": SB(NL, F32), "yf": SB(V, F32), "ones": SB(128, B16), "f16": SB(128, B16),
+    "c256": SB(2 * CC, F32), "fio": SB(144, B16), "col": SB(8, F32), "pint": SB(8, I32), "sel": SB(24, B16), "rep": SB(128, B16),
+    "jw": SB(240, B16), "jc": SB(144, B16), "bl": SB(128, B16), "bc": SB(9 * 128, B16), "negi": SB(224, B16), "gapi": SB(128, B16),
+    "kid": SB(128, F32), "pt": SB(NR * 384, B16), "pm": SB(NR * 384, B16),
 }
 PSUM = ["p%d" % i for i in range(8)]
-SCRATCH.update((p, PS(512)) for p in PSUM)
+SCRATCH.update((p, ("psum", [128, 512], F32)) for p in PSUM)
 SEMAPHORES = (["cp", "cv", "ca", "ct", "sent", "ar"] + ["d%d" % i for i in range(40)]
               + ["as%d" % i for i in range(8)] + ["ae%d" % i for i in range(8)] + ["h%d" % i for i in range(8)])
 
-CY, PCY, GA = 0.00083 * 1.2, 0.00042 * 1.2, 1.56
-LAT, DLAT, DBW, RLAT, RCALL = 0.12, 1.9, 300e3, 4.5, 0.7
-ARRIVE = [[19.0], [16.0], [11.5, 13.5], [9.0, 11.0]]
-BEAT, HOP, LOOK, TAIL, AHEAD = 1.4, 0.2, 0.05, 6.0, {"a": 10.0, "v": 10.0, "t": 2.0}
+CY, PCY, GA = 0.00083 * 1.2, 0.00042 * 1.2, 1.75
+LAT, DLAT, DBW, RLAT, RCALL, RVIA = 0.25, 1.9, 300e3, 4.5, 0.7, 1.7
+ARRIVE, RELAY = [[14.0], [14.0], [11.0, 13.0], [10.0, 12.0]], 1.5
+BEAT, DBEAT, HOP, LOOK, TAIL, AHEAD = 1.4, 0.2, 0.3, 0.1, 6.0, {"a": 1.5, "v": 1.5, "t": 1.5}
 
 
 def last_round(K):
-    a, b, c = [k for k in range(NR - 1, -1, -1) if k != K]
-    H = Q // 2
-    far = [(a, 0, Q), (b, 0, H), (c, 0, H), (c, H, Q), (b, H, Q)] if ORDER else [(a, 0, Q), (b, 0, Q), (c, 0, H), (c, H, Q)]
-    return far + [(K, x0, x1) for x0, x1 in zip(CUTS, CUTS[1:])]
+    a, b, c = LAST[K]
+    return [(a, 0, Q), (b, 0, H), (b, H, Q), (c, 0, H), (c, H, Q)] + [(K, x0, x1) for x0, x1 in zip(CUTS, CUTS[1:])]
 
 
 def end_sends(K):
-    return [(i, k, h, h == 0 and END_VIA) for i, (k, x0, x1) in enumerate(last_round(K)) if k != K for h in range(2 * x0 // Q, 2 * x1 // Q)]
+    return [(i, k, h, h == 0 and i < END_VIA) for i, (k, x0, x1) in enumerate(last_round(K)) if k != K for h in range(x0 // H, x1 // H)]
 
 
 def helpers_of(core, topo):
@@ -78,12 +76,14 @@ def helpers_of(core, topo):
 
 def hand_ons(K):
     jobs = []
-    for h, (x0, x1) in enumerate(START[K]):
-        for z, dd in enumerate(START_VIA[K][h]):
-            jobs.append((z, (K + dd) % NR, "as%d" % (2 * K + h), "enc", dd * Q + x0, dd * Q + x1, "w0", OWN[K] + x0))
+    for call in CALLS[K]:
+        via = [c for c in call if c[2]]
+        for dd, h, z in via:
+            x0, x1 = START[K][h]
+            jobs.append((z - 1, len(via), (K + dd) % NR, "as%d" % (2 * K + h), "enc", dd * Q + x0, dd * Q + x1, "w0", OWN[K] + x0))
     for i, k, h, via in end_sends(K):
         if via:
-            jobs.append((0, k, "ae%d" % (2 * K + h), "res", k * Q + h * Q // 2, k * Q + (h + 1) * Q // 2, "land", K * Q + h * Q // 2))
+            jobs.append((0, 1, k, "ae%d" % (2 * K + h), "res", k * Q + h * H, k * Q + h * H + H, "land", K * Q + h * H))
     return [(j[0], "h%d" % n) + j[1:] for n, j in enumerate(jobs)]
 
 
@@ -91,26 +91,31 @@ def helper_program(g, core, owner, z, T, topo):
     K, n = T.rank_of(owner), 0
     far = set(topo.engines(owner, T.cores[(K + 1) % NR]))
     near = len([e for e in topo.engines(owner, core) if e not in far])
-    for hz, hs, k, arr, src, c0, c1, dst, d0 in hand_ons(K):
+    for hz, hs, share, k, arr, src, c0, c1, dst, d0 in hand_ons(K):
         if hz == z:
             to = T.cores[k]
-            h = int(arr[2:]) % 2
-            g.wait_ge(T.sem[hs], near // (len(START_VIA[K][h]) if src == "enc" else 1))
+            g.wait_ge(T.sem[hs], near // share)
             g.remote_dma(T[dst][:, d0:d0 + c1 - c0], T[src][:, c0:c1], T.sem[arr], T.sem.sent, topo.addr(to)[1], topo.addr(to)[0], topo.mask(core, to))
             n += len(topo.engines(core, to))
     if n:
         g.wait_ge(T.sem.sent, n)
 
 
-def start_engines(r, h, nfar):
-    via = START_VIA[r][h]
-    direct = [dd for dd in (1, 2, 3) if dd not in via]
-    share = {1: [nfar], 2: [nfar // 2] * 2, 3: [nfar // 2, nfar // 4, nfar // 4]}[len(direct)]
-    return dict([(dd, nfar) for dd in via] + list(zip(direct, share)))
+def start_engines(r, dd, h, nfar):
+    call = [c for c in CALLS[r] if (dd, h, 0) in c]
+    return nfar // len([x for x in call[0] if not x[2]]) if call else nfar
 
 
 def build_ops(core, K, T, topo):
-    ops, sends, nsem, item = [], [], [0], [0, 0, 0]
+    ops, sends, count = [], [], {}
+
+    def turn(name, n):
+        count[name] = count.get(name, -1) + 1
+        return count[name] % n
+
+    newsem = lambda: "d%d" % turn("sem", 40)
+    slot = lambda: PSUM[turn("slot", NSLOT)]
+    keep = lambda: PSUM[NSLOT + turn("keep", len(PSUM) - NSLOT)]
 
     def R(name, c0, c1, p0=0, p1=128):
         return (name, p0, p1, c0, c1)
@@ -123,10 +128,6 @@ def build_ops(core, K, T, topo):
         o.update(kw)
         ops.append(o)
         return o
-
-    def newsem():
-        nsem[0] += 1
-        return "d%d" % (nsem[0] - 1)
 
     def wd(r):
         return r[4] - r[3]
@@ -162,6 +163,9 @@ def build_ops(core, K, T, topo):
     def group(out, terms):
         return [(out, l, r, z == 0, z == len(terms) - 1) for z, (l, r) in enumerate(terms)]
 
+    def iota(out, ap, pat):
+        return add("p", lambda q: q.iota(ap, pat, 0, 0, allow_small_or_imprecise_dtypes=True), [], out, 0.13 + 2 * sum(wd(r) for r in out) * CY)
+
     def select(out, src, pat, op, fill, base, cm):
         return add("p", lambda q: q.affine_select(AP(out), AP(src), pat, op, fill, base, cm), [src], [out], 0.17 + 2 * wd(out) * CY)
 
@@ -173,12 +177,12 @@ def build_ops(core, K, T, topo):
     near = [e for e in topo.engines(core, hel[0]) if e not in set(far)]
     jobs = hand_ons(K)
 
-    def send(xs, wait=()):
+    def send(xs):
         def fn(q):
             return q.remote_dma_fused([RemoteDMATransfer(dst_ids=[DstId(rid=topo.addr(c)[0], pnc=topo.addr(c)[1]) for c in to],
                                                          dma_engine_mask=sum(1 << e for e in engs), remote_sem=T.sem[sem],
                                                          srcs=[AP(src)], dsts=[AP(dst)] * len(to)) for to, engs, sem, src, dst in xs], local_sem=T.sem.sent)
-        o = add("p", fn, [x[3] for x in xs] + list(wait), [], RCALL, kind="r", cnt=sum(len(x[1]) for x in xs))
+        o = add("p", fn, [x[3] for x in xs], [], RCALL, kind="r", cnt=sum(len(x[1]) for x in xs))
         o["after"] += sends[-1:]
         sends.append(o)
         return o
@@ -188,7 +192,7 @@ def build_ops(core, K, T, topo):
         o["after"] += after
 
     def to_helper(src, engs):
-        hz, hs = [j[:2] for j in jobs if (j[4], j[5]) == (src[0], src[3])][0]
+        hz, hs = [j[:2] for j in jobs if (j[5], j[6]) == (src[0], src[3])][0]
         return ([hel[hz]], engs, hs, src, src)
 
     others = [(K + dd) % NR for dd in (1, 2, 3)]
@@ -197,16 +201,16 @@ def build_ops(core, K, T, topo):
     first = send([([T.cores[k] for k in others], far, "ar", mine, mine)])
     first["due"] = -60.0
 
-    col = lambda j, p0=0, p1=128: R("col", j, j + 1, p0, p1)
+    col = lambda j: R("col", j, j + 1)
     ones, fio, negi, gapi, kid, w = R("ones", 0, 128), R("fio", 0, 128), R("negi", 0, 128), R("gapi", 0, 128), R("kid", 0, 128), ("w0", "w1", "w2")
-    pi0, pi1, pi2 = R("pint", 0, 1), R("pint", 1, 2), R("pint", 2, 3)
+    pi0, pi1, pi2, c256 = R("pint", 0, 1), R("pint", 1, 2), R("pint", 2, 3), R("c256", 0, 2 * CC)
     memset(ones, 1.0)
-    memset(R("c256", 0, 2 * CC), 0.0)
-    o = act(R("c256", 0, 2 * CC), R("c256", 0, 2 * CC), AF.Exp, math.log(CAP))
+    memset(c256, 0.0)
+    o = act(c256, c256, AF.Exp, math.log(CAP))
     o["dur"], o["due"] = o["dur"] + 1.3, -50.0
     add("p", lambda q: q.iota(AP(pi0), [[1, 1]], 0, 1), [], [pi0], 0.14)
-    add("p", lambda q: q.iota(T.fio[:, :], [[1, 144]], 0, 0, allow_small_or_imprecise_dtypes=True), [], [R("fio", 0, 144)], 0.4)
-    add("p", lambda q: q.iota(T.f16[:, :], [[16, 8], [0, 16]], 0, 0, allow_small_or_imprecise_dtypes=True), [], [R("f16", 0, 128)], 0.4)
+    iota([R("fio", 0, 144)], T.fio[:, :], [[1, 144]])
+    iota([R("f16", 0, 128)], T.f16[:, :], [[16, 8], [0, 16]])
     select(R("rep", 0, 128), ones, [[0, 4], [-1, 32]], AL.is_equal, 0.0, -32 * K, 1)
     select(R("sel", 0, 24), R("ones", 0, 24), [[-1, 3], [-16, 8]], AL.is_equal, 0.0, 0, 1)
     cp(col(0), pi0)
@@ -224,15 +228,13 @@ def build_ops(core, K, T, topo):
     ts(R("jw", 96, 240), R("fio", 0, 144), col(1), 16.0, AL.subtract, AL.is_equal, half=True)
     tt(R("jc", 0, 144), R("jw", 64, 208), R("jw", 32, 176), AL.add)
     tt(R("jc", 0, 144), R("jc", 0, 144), R("jw", 0, 144), AL.add)
-    vec(lambda q: q.memset(T.fl[:, :, :], 0.0), [], [R("fl", 0, 384)], 192)
     for nm in w:
-        zs = [R(nm, c, c + 1) for c in BEG[1:NR]]
-        vec(lambda q, nm=nm: q.memset(T[nm][:, BEG[1]:BEG[NR - 1] + 1:V + GAP], 0.0), [], zs, 64)
-        memset(R(nm, 0, 1), 0.0)
-        for u in range(4):
-            c = OWN[NR - 1] + V - Q * u
-            vec(lambda q, nm=nm, c=c, u=u: q.memset(T[nm][32 * u:32 * u + 32, c:c + GAP + 1:GAP], 0.0), [],
-                [R(nm, c + z, c + z + 1, 32 * u, 32 * u + 32) for z in (0, GAP)], 64)
+        for p0, p1, c, step, n in [(0, 128, BEG[1], V + GAP, NR - 1), (0, 128, 0, 1, 1)] + [(32 * u, 32 * u + 32, OWN[NR - 1] + V - Q * u, GAP, 2) for u in range(4)]:
+            ap, wr = T[nm][p0:p1, c:c + step * (n - 1) + 1:step], [R(nm, c + z * step, c + z * step + 1, p0, p1) for z in range(n)]
+            if p1 - p0 < 128:
+                add("a", lambda q, ap=ap, z=R("ones", 0, n, p0, p1): q.activation(ap, AP(z), AF.Copy, scale=0.0), [ones], wr, 0.125)
+            else:
+                iota(wr, ap, [[0, n]])
     bl = R("bl", 0, 128)
     select(bl, ones, [[1, 128]], AL.is_gt, 0.0, 0, -1)
     select(bl, bl, [[-16, 8], [0, 16]], AL.is_ge, 0.0, 0, 1)
@@ -240,56 +242,44 @@ def build_ops(core, K, T, topo):
     for z in range(9):
         ts(R("bc", 128 * z, 128 * z + 128), R("f16", 0, 128), col(0), -float(z), AL.subtract, AL.is_equal, half=True)
 
-    exps, u = [], 0
-    for h, (x0, x1) in enumerate(START[K]):
-        via, eng = START_VIA[K][h], start_engines(K, h, len(far))
-        for dd in via + [d for d in (1, 2, 3) if d not in via]:
-            exps.append((h, dd))
+    order = [(h, dd) for call in CALLS[K] for dd, h, via in call]
     own = [(h, 0) for h in range(len(START[K]))]
-    exps = exps + own if K == NR - 1 else own + exps
-    line = []
-    for z, (h, dd) in enumerate(exps):
+    exps = []
+    for z, (h, dd) in enumerate(order + own if K >= OWN_LAST else own + order):
         (x0, x1), d, sem = START[K][h], (K + dd) % NR, newsem()
         raw, rf = R("raw", dd * Q + x0, dd * Q + x1), R("rawf", dd * Q + x0, dd * Q + x1)
-        ld = [dma("sa"[u % 2] if z < LOADS_A else "s", R("raw", raw[3], raw[4], 32 * u, 32 * u + 32), T.ends[32 * d:32 * d + 32, u * Q + x0:u * Q + x1], 128 * wd(raw), sem)
-              for u in range(4)]
         for u in range(4):
-            ld[u]["due"] = -59.0 + 0.1 * (4 * z + u)
-        line.append((ts(rf, raw, float(MID), None, AL.subtract),
-                     act(R("enc", raw[3], raw[4]) if dd else R("w0", OWN[K] + x0, OWN[K] + x1), rf, AF.Exp, PHASE, ALPHA)))
-        for y in range(2):
-            line[-1][y]["due"] = -45.0 + 0.1 * z
-    exps = [l[1] for l in line]
+            dma("sa"[u % 2] if z < LOADS_A else "s", R("raw", raw[3], raw[4], 32 * u, 32 * u + 32), T.ends[32 * d:32 * d + 32, u * Q + x0:u * Q + x1],
+                128 * wd(raw), sem)["due"] = -59.0 + 0.1 * (4 * z + u)
+        ts(rf, raw, float(MID), None, AL.subtract)["due"] = -45.0 + 0.1 * z
+        exps.append(act(R("enc", raw[3], raw[4]) if dd else R("w0", OWN[K] + x0, OWN[K] + x1), rf, AF.Exp, PHASE, ALPHA))
+        exps[-1]["due"] = -45.0 + 0.1 * z
     tile = lambda r, h: R("w0", OWN[r] + START[r][h][0], OWN[r] + START[r][h][1])
 
     def arrive(r, after):
         for h in range(len(START[r])):
-            arrival(tile(r, h), "as%d" % (2 * r + h), start_engines(r, h, len(far))[(K - r) % NR], after, 0.1, ARRIVE[r][h])
+            arrival(tile(r, h), "as%d" % (2 * r + h), start_engines(r, (K - r) % NR, h, len(far)), after, 0.1,
+                    ARRIVE[r][h] + (RELAY if ((K - r) % NR, h, 1) in sum(CALLS[r], []) else 0.0))
     for r in range(K + 1, NR):
         arrive(r, [first])
-    for h, (x0, x1) in enumerate(START[K]):
-        via, eng, xs, e0 = START_VIA[K][h], start_engines(K, h, len(far)), [], 0
-        for dd in (1, 2, 3):
-            src = R("enc", dd * Q + x0, dd * Q + x1)
-            if dd in via:
-                n = len(near) // len(via)
-                xs.append(to_helper(src, near[via.index(dd) * n:via.index(dd) * n + n]))
+    for z, call in enumerate(CALLS[K]):
+        xs, e0, n0 = [], 0, 0
+        for dd, h, via in call:
+            src = R("enc", dd * Q + START[K][h][0], dd * Q + START[K][h][1])
+            if via:
+                n = len(near) // len([x for x in call if x[2]])
+                xs.append(to_helper(src, near[n0:n0 + n]))
+                n0 += n
             else:
-                xs.append(([T.cores[(K + dd) % NR]], far[e0:e0 + eng[dd]], "as%d" % (2 * K + h), src, tile(K, h)))
-                e0 += eng[dd]
-        send(xs, [tile(START_AFTER[K], 0)] if START_AFTER[K] else [])["due"] = -40.0 + h
+                n = start_engines(K, dd, h, len(far))
+                xs.append(([T.cores[(K + dd) % NR]], far[e0:e0 + n], "as%d" % (2 * K + h), src, tile(K, h)))
+                e0 += n
+        send(xs)["due"] = -40.0 + z
     for r in range(K):
         arrive(r, sends[-1:])
 
     arrival(R("rta", 0, LB * NR), "ar", 3 * len(far), [first], RLAT)
     cp(R("rtb", 0, 12), R("rta", 0, 12))
-    def slot():
-        item[1] += 1
-        return PSUM[(item[1] - 1) % NSLOT]
-
-    def keep():
-        item[2] += 1
-        return PSUM[NSLOT + (item[2] - 1) % (len(PSUM) - NSLOT)]
     z = R(slot(), 0, 12)
     mm([(z, R("rep", 0, 128), R("rtb", 0, 12), True, True)])
     cp(R("rtc", 0, 12), z)
@@ -297,146 +287,136 @@ def build_ops(core, K, T, topo):
         for b in range(LB):
             ts(R("pt", 384 * r + 128 * b, 384 * r + 128 * b + 128), fio, col(1), R("rtc", LB * r + b, LB * r + b + 1), AL.subtract, AL.is_equal, half=True)
 
-    def permutation(r, bank, z):
-        mm([(R(bank, z + 128 * b, z + 128 * b + 128), R("pt", 384 * r + 128 * b, 384 * r + 128 * b + 128), negi, True, True) for b in range(LB)])
-        ts(R("pm", 384 * r, 384 * r + 384), R(bank, z, z + 384), -1.0 / BIG, None, AL.mult)
-    for r in range(NR - 1, NR - 1 - PERMS, -1):
-        permutation(r, slot(), 0)
+    def permutation(r, bank):
+        mm([(R(bank, 128 * b, 128 * b + 128), R("pt", 384 * r + 128 * b, 384 * r + 128 * b + 128), negi, True, True) for b in range(LB)])
+        ts(R("pm", 384 * r, 384 * r + 384), R(bank, 0, 384), -1.0 / BIG, None, AL.mult)
 
-    def spread(wn, k, first=False):
-        sem, c, n = newsem(), OWN[k], Q // 2 if first else Q
-        for j in (1, 2, 3):
-            dma("s", R(wn, c + j * Q, c + j * Q + n, 0, 128 - 32 * j), R(wn, c, c + n, 32 * j, 128), (128 - 32 * j) * n * 2, sem)
-        if first:
-            sem = newsem()
+    def spread(wn, k, x0=0, x1=Q, first=False):
+        sem, c, m = newsem(), OWN[k] + x0, x1 - x0
+        for h, (y0, y1) in enumerate(START[k] if first else [(0, m)]):
             for j in (1, 2, 3):
-                bank, z = slot(), 0
-                mm([(R(bank, z, z + n), R("negi", 32 * j, 32 * j + 128), R(wn, c + n, c + Q), True, True)])
-                to, z = R(wn, c + j * Q + n, c + j * Q + Q, 0, 128 - 32 * j), R(bank, z, z + n, 0, 128 - 32 * j)
-                if j == 1:
-                    act(to, z, AF.Copy, scale=-1.0 / BIG)
+                to, n = R(wn, c + j * Q + y0, c + j * Q + y1, 0, 128 - 32 * j), y1 - y0
+                if not first:
+                    dma("s", to, R(wn, c + y0, c + y1, 32 * j, 128), (128 - 32 * j) * n * 2, sem)
+                    continue
+                bank = keep() if h else slot()
+                mm([(R(bank, 0, n), R("negi", 32 * j, 32 * j + 128), R(wn, c + y0, c + y1), True, True)])
+                if (j + h) % 2:
+                    ts(to, R(bank, 0, n, 0, 128 - 32 * j), -1.0 / BIG, None, AL.mult)
                 else:
-                    ts(to, z, -1.0 / BIG, None, AL.mult)
+                    act(to, R(bank, 0, n, 0, 128 - 32 * j), AF.Copy, scale=-1.0 / BIG)
+                ops[-1]["due"] = ops[-2]["due"] = -27.0 + h + 0.1 * j
         if k:
+            sem = newsem() if first else sem
             for j in (1, 2, 3):
-                dma("s", R(wn, c - j * Q, c - j * Q + Q, 32 * j, 128), R(wn, c, c + Q, 0, 128 - 32 * j), (128 - 32 * j) * Q * 2, sem)
+                dma("s", R(wn, c - j * Q, c - j * Q + m, 32 * j, 128), R(wn, c, c + m, 0, 128 - 32 * j), (128 - 32 * j) * m * 2, sem)
 
-    nlist, lns = [0, 0], []
+    lns = []
 
-    def ln(out, src, rd, wr):
-        o = add("a", lambda q: q.activation(out, src, AF.Ln, scale=LNS), [rd], [wr], 384 * CY + 0.06)
+    def ln(out, src, scale):
+        o = act(out, src, AF.Ln, scale=scale)
         if not lns:
             o["dur"], o["due"] = o["dur"] + 1.5, -30.0
         o["after"] += exps + lns[:1]
         lns.append(o)
+    memset(col(7), math.exp(ALPHA * (0.5 - MID)))
+    ln(col(7), col(7), 1.0)
 
-    def first_lists(par):
-        n0, c = len(ops), CC // 2
-        for h in range(2):
-            c0, pc, z = OWN[NR - 1] + h * Q // 2, keep(), 0
-            mm([(T[pc][0:c, z + i:z + 384:16], T.w0[:, c0 + i:c0 + Q // 2:16], R("sel", 0, 24), True, True) for i in range(16)],
-               [R("w0", c0, c0 + Q // 2)], [R(pc, z, z + 384)], 16 * c)
-            lt = R("lt", 384 * par, 384 * par + 384, 64 * h, 64 * h + c)
-            ln(T.lt[64 * h:64 * h + c, LB * par:LB * par + LB, :], T[pc][0:c, z:z + 384], R(pc, z, z + 384), lt)
-            mm([(R(pc, z + b * c, z + (b + 1) * c), T.lt[64 * h:64 * h + c, LB * par + b, :], R("kid", 64 * h, 64 * h + c, 64 * h, 64 * h + c), True, True)
-                for b in range(LB)], [lt], None, 256 * LB)
-            xa = R("xa", h * LB * c, (h + 1) * LB * c)
-            act(xa, R(pc, z, z + LB * c), AF.Abs)
+    def left_rows(bank, wn, c0, n, i0, i1, p0=0):
+        mm([(T[bank][p0:p0 + n // 16, i:384:16], T[wn][:, c0 + i:c0 + n:16], R("sel", 0, 24), True, True) for i in range(i0, i1)],
+           [R(wn, c0, c0 + n)], [R(bank, 0, 384, p0, p0 + n // 16)], (i1 - i0) * n // 16)
+
+    def first_lists():
+        for h, (x0, x1) in enumerate(START[NR - 1]):
+            bank, p0, c, n0 = keep(), 64 * h, (x1 - x0) // 16, len(ops)
+            left_rows(bank, "w0", OWN[NR - 1] + x0, x1 - x0, 0, 16)
+            ln(R("lt", 0, 384, p0, p0 + c), R(bank, 0, 384, 0, c), LNS)
+            mm([(R(bank, b * c, (b + 1) * c), R("lt", 128 * b, 128 * b + 128, p0, p0 + c), R("kid", p0, p0 + c, p0, p0 + c), True, True) for b in range(LB)], cyc=256 * LB)
+            xa = R("xa", LB * x0 // 16, LB * x1 // 16)
+            act(xa, R(bank, 0, LB * c), AF.Abs)
             ts(R("off", (NR - 1) * NL + xa[3], (NR - 1) * NL + xa[4]), xa, col(6), None, AL.add)
-        for o in ops[n0:]:
-            o["chain"] = True
+            for o in ops[n0:]:
+                o["due"] = -28.0 + SPREAD1 * h
 
-    def lists(rnd, ks):
-        wn, par, n0 = w[rnd], nlist[0] % NLT, len(ops)
-        nlist[0] += 1
-        if rnd == 0 and ks == [NR - 1]:
-            return first_lists(par)
-        work = [keep() for k in ks]
-        banks = [keep() if REOPEN and k < NR - 1 else work[h] for h, k in enumerate(ks)]
-        tb, np_ = work[0], 64 * len(ks) - 16
-        for h, k in enumerate(ks):
-            c0 = OWN[k]
+    def counted_lists(rnd, k):
+        par, wb = turn("list", NLT), keep()
+        ks = [k, NR - 1] if PAIR and rnd and k == NR - 2 else [k]
+        lc, l0, top = 384 * par, 2 * NL * par, 64 * len(ks) - 16
+        if len(ks) > 1:
+            mm([(R(wb, 0, 384, 32, 64), R("ones", 0, 32), R("bc", 0, 384), True, True)])
+        for h, kk in enumerate(ks):
             for i0 in (0, 8):
-                mm([(T[tb][64 * h:64 * h + CC, i:384:16], T[wn][:, c0 + i:c0 + Q:16], R("sel", 0, 24), True, True) for i in range(i0, i0 + 8)],
-                   [R(wn, c0, c0 + Q)], [R(tb, 0, 384, 64 * h, 64 * h + CC)], 8 * CC)
-        lt = R("lt", 384 * par, 384 * par + 384)
-        ln(T.lt[0:np_, LB * par:LB * par + LB, :], T[tb][0:np_, 0:384], R(tb, 0, 384), lt)
-        X = lambda h, b: R(banks[h], b * CC, (b + 1) * CC)
-        back = lambda h, b: (T.lt[0:np_, LB * par + b, :], R("kid", 64 * h, 64 * h + CC, 0, np_))
+                left_rows(wb, w[rnd], OWN[kk], Q, i0, i0 + 8, 64 * h)
+        act(R("lc", lc, lc + 384, 0, top), R(wb, 0, 384, 0, top), AF.Copy)
         for h in range(len(ks)):
-            for b in range(LB):
-                mm([(R(work[h], b * CC, (b + 1) * CC),) + back(h, b) + (True, True)], [lt], None, 256)
-        for h, k in enumerate(ks):
-            xb = work[h]
-            off, xh = R("off", (rnd * NR + k) * NL, (rnd * NR + k + 1) * NL), R(banks[h], 0, NL)
-            if k < NR - 1:
-                cb, hb, rb, eb = k * NL, 3 * k * NL, 3 * (k % 2) * NL, 2 * k * CC
-                if "c" in ON_ACT:
-                    act(R("cls", cb, cb + NL), xh, AF.Identity, CB - 0.5 + (MID + 0.5) / V, 1.0 / V)
-                else:
-                    ts(R("cls", cb, cb + NL), R(xb, 0, NL), 1.0 / V, CB - 0.5 + (MID + 0.5) / V, AL.mult, AL.add)
-                for qq in range(k + 1, NR):
-                    ts(R("hh", hb + (qq - 1) * NL, hb + qq * NL), R("cls", cb, cb + NL), CB + qq, None, AL.is_equal, half=True)
-                if k == 0:
-                    vec(lambda q, h=h: q.tensor_scalar(T.fl[64 * h:64 * h + CC, :, 0:32], T.lt[64 * h:64 * h + CC, LB * par:LB * par + LB, 0:32], (0.5 - MID) / KI, None, AL.is_lt),
-                        [lt], [R("fl", 0, 384)], 96)
-                slots = [(qq, b) for qq in range(k + 1, NR) for b in range(LB)]
-                hq = lambda qq, b: R("hh", hb + (qq - 1) * NL + b * CC, hb + (qq - 1) * NL + (b + 1) * CC)
-                mm(group(R(xb, 400, 400 + CC), [(R("jc", 16 - z, 144 - z), hq(*s)) for z, s in enumerate(slots)]))
-                mm(group(R(xb, 400 + CC, 400 + 2 * CC), [(R("jw", 112 - z, 240 - z), hq(*s)) for z, s in enumerate(slots)]))
-                cs, eo, ex = R(xb, 400, 399 + 2 * CC), R("ee", eb, eb + 2 * CC - 1), R("ee", eb + CC - 1, eb + 2 * CC - 1)
-                vec(lambda q, eo=eo, cs=cs: q.tensor_tensor_scan(AP(eo), AP(cs), T.c256[:, 0:2 * CC - 1], 0.0, AL.add, AL.min), [cs, R("c256", 0, 2 * CC)], [eo], 2 * CC)
-                if REOPEN:
-                    mm([(xh, gapi, R("cls", cb, cb + NL), True, False)])
-                    for b in range(LB):
-                        mm([(X(h, b),) + back(h, b) + (False, False)], [lt], None, 256)
-                    if k == 0:
-                        mm([(X(h, b), T.fl[0:np_, b, :], R("negi", 64 * h, 64 * h + CC, 0, np_), False, False) for b in range(LB) if k == 0], [R("fl", 0, 384)] * (k == 0))
-                for z0 in range(0, len(slots), LB):
-                    if REOPEN:
-                        a = hq(*slots[z0])[3]
-                        mm([(R(xb, z0 * CC, z0 * CC + NL), bl, R("hh", a, a + NL), True, False)]
-                           + [(R(xb, z * CC, (z + 1) * CC), R("bc", 128 * z, 128 * z + 128), ex, False, z == z0 + LB - 1) for z in range(z0, z0 + LB)])
-                        continue
-                    mm([m for z in range(z0, z0 + LB) for m in group(R(xb, z * CC, (z + 1) * CC), [(bl, hq(*slots[z])), (R("bc", 128 * z, 128 * z + 128), ex)])])
-                if "r" in ON_ACT:
-                    act(R("rl", rb, rb + len(slots) * CC), R(xb, 0, len(slots) * CC), AF.Relu, -(CAP + 31.0))
-                else:
-                    ts(R("rl", rb, rb + len(slots) * CC), R(xb, 0, len(slots) * CC), CAP + 32.0, None, AL.is_ge)
-                if REOPEN:
-                    mm([(xh, negi, R("rl", rb + z * NL, rb + (z + 1) * NL), False, z == NR - 2 - k) for z in range(NR - 1 - k)])
-                for b in range(0 if REOPEN else LB):
-                    terms = [(gapi, R("cls", cb + b * CC, cb + (b + 1) * CC)), back(h, b)]
-                    terms += [(negi, R("rl", rb + z * CC, rb + (z + 1) * CC)) for z, s in enumerate(slots) if s[1] == b]
-                    if k == 0:
-                        terms.append((T.fl[0:np_, b, :], R("negi", 64 * h, 64 * h + CC, 0, np_)))
-                    mm(group(X(h, b), terms), [lt] + [R("fl", 0, 384)] * (k == 0), None, 64 * (len(terms) + 3))
-            ts(off, xh, col(2 + k), None, AL.add)
-        for o in ops[n0:]:
-            o["chain"] = True
+            mm([(R(wb, h * NL + b * CC, h * NL + (b + 1) * CC), R("lc", lc + 128 * b, lc + 128 * b + 128, 0, top), R("gapi", 64 * h, 64 * h + CC, 0, top), True, True)
+                for b in range(LB)])
+        ln(R("lv", l0, l0 + len(ks) * NL), R(wb, 0, len(ks) * NL), LNS / GAP)
+        lv, off = R("lv", l0, l0 + NL), R("off", (rnd * NR + k) * NL, (rnd * NR + k + 1) * NL)
+        if ks[-1] == NR - 1:
+            l1 = l0 + (len(ks) - 1) * NL
+            ts(R("off", (rnd * NR + NR - 1) * NL, (rnd + 1) * NR * NL), R("lv", l1, l1 + NL), KI, col(1 + NR), AL.mult, AL.add)
+            if k == NR - 1:
+                return
+        cl, hb, rb, eb, xh, nq = R("cls", k * NL, k * NL + NL), 3 * k * NL, 4 * (k % 2) * NL, 2 * k * CC, R(keep(), 0, NL), NR - 1 - k
+        ts(cl, lv, KI / V, CB - 0.5 + (MID + 0.5) / V, AL.mult, AL.add)
+        for z in range(nq):
+            ts(R("hh", hb + z * NL, hb + z * NL + NL), cl, CB + k + 1 + z, None, AL.is_equal, half=True)
+        hq = [R("hh", hb + z * CC, hb + z * CC + CC) for z in range(nq * LB)]
+        mm(group(R(wb, 400, 400 + CC), [(R("jc", 16 - z, 144 - z), s) for z, s in enumerate(hq)]))
+        mm(group(R(wb, 400 + CC, 400 + 2 * CC), [(R("jw", 112 - z, 240 - z), s) for z, s in enumerate(hq)]))
+        cs, eo, ex = R(wb, 400, 399 + 2 * CC), R("ee", eb, eb + 2 * CC - 1), R("ee", eb + CC - 1, eb + 2 * CC - 1)
+        vec(lambda q: q.tensor_tensor_scan(AP(eo), AP(cs), T.c256[:, 0:2 * CC - 1], 0.0, AL.add, AL.min), [cs, c256], [eo], 2 * CC)
+        mm([(xh, gapi, cl, True, False), (xh, kid, lv, False, False)], cyc=5 * NL)
+        if k == 0:
+            ts(R("rl", rb + nq * NL, rb + nq * NL + NL), lv, col(7), None, AL.is_lt)
+        for z0 in range(nq):
+            mm([(R(wb, z0 * NL, z0 * NL + NL), bl, R("hh", hb + z0 * NL, hb + z0 * NL + NL), True, False)]
+               + [(R(wb, z * CC, (z + 1) * CC), R("bc", 128 * z, 128 * z + 128), ex, False, z % LB == LB - 1) for z in range(z0 * LB, z0 * LB + LB)])
+        if "r" in ON_ACT:
+            act(R("rl", rb, rb + nq * NL), R(wb, 0, nq * NL), AF.Relu, -(CAP + 31.0))
+        else:
+            ts(R("rl", rb, rb + nq * NL), R(wb, 0, nq * NL), CAP + 32.0, None, AL.is_ge)
+        nq += k == 0
+        mm([(xh, negi, R("rl", rb + z * NL, rb + (z + 1) * NL), False, z == nq - 1) for z in range(nq)])
+        ts(off, xh, col(2 + k), None, AL.add)
 
+    def lists(rnd, k):
+        n0 = len(ops)
+        if rnd == 0 and k == NR - 1:
+            first_lists()
+        elif k < NR - 1 or not PAIR:
+            counted_lists(rnd, k)
+        for o in ops[n0:]:
+            o["chain"] = FIRST if rnd == 0 and k == NR - 1 else AHEAD0 if rnd == 0 else 1.0
+
+    early = [K] if OWN_LIST and K < NR - 1 else []
+    for k in early:
+        lists(0, k)
+    for r in SWEEP[K][:PERMS]:
+        permutation(r, keep() if PKEEP else slot())
     for k in range(NR - 1, -1, -1):
-        spread("w0", k, k == NR - 1)
-    for ks in sorted(BATCH[0], key=lambda ks: K not in ks or K == NR - 1):
-        lists(0, ks)
-    s_y, nd = newsem(), [0]
+        spread("w0", k, first=k == NR - 1)
+    for k in sorted(SWEEP[K], key=lambda k: (k != NR - 1, k != K)):
+        if k not in early:
+            lists(0, k)
+    s_y = newsem()
 
     def decode(src, r, x0, x1):
         a, e = r * Q + x0, r * Q + x1
-        way = "v" if e - a <= DIRECT else MIX[nd[0] % len(MIX)] if at[0] >= V else "p"
-        nd[0] += 1
-        bank, z0 = keep() if way == "p" else None, 0
         act(R("rawf", a, e), R(src, a, e), AF.Ln, scale=LNS)
-        if way != "p":
-            if way == "v":
-                ts(R("yf", a, e), R("rawf", a, e), KI, ROUND + MID, AL.mult, AL.add)
-            else:
-                act(R("yf", a, e), R("rawf", a, e), AF.Identity, ROUND + MID, KI)
+        if e - a <= DIRECT:
+            ts(R("yf", a, e), R("rawf", a, e), KI, ROUND + MID, AL.mult, AL.add)
             ts(R("yf", a, e), R("yf", a, e), ROUND, None, AL.subtract)
         else:
-            mm([(R(bank, z0, z0 + e - a), kid, R("rawf", a, e), True, True)], cyc=4 * (e - a))
-            ts(R("yf", a, e), R(bank, z0, z0 + e - a), ROUND + MID, ROUND, AL.add, AL.subtract)
+            z = R(keep(), 0, e - a)
+            mm([(z, kid, R("rawf", a, e), True, True)], cyc=4 * (e - a))
+            ts(R("yf", a, e), z, ROUND + MID, ROUND, AL.add, AL.subtract)
         ops[-1]["beat"] = DBEAT
+        if WHOLE and src == "land":
+            if turn("half%d" % r, 2) == 0:
+                return
+            x0, x1, a, e = 0, Q, r * Q, r * Q + Q
         for u in range(4):
             dma("s", T.y[32 * r:32 * r + 32, u * Q + x0:u * Q + x1], R("yf", a, e, 32 * u, 32 * u + 32), 128 * (e - a), s_y)
 
@@ -444,9 +424,8 @@ def build_ops(core, K, T, topo):
         ws, n, quick = w[rnd], x1 - x0, rnd == 0 and k == NR - 1
         win = R(ws, OWN[k] if quick else BEG[k], OWN[k] + V + 16 if k == NR - 1 else WW)
         dst = R("res", k * Q + x0, k * Q + x1) if rnd == RO - 1 else R(w[rnd + 1], OWN[k] + x0, OWN[k] + x1)
-        g0 = (item[0] % NG) * Q
-        item[0] += 1
-        nv = DVE_GATHER[rnd] * n // Q // 32 * 32 if b == DVE_B else 0
+        g0 = turn("gather", NG) * Q
+        nv = DVE_GATHER[rnd] * n // Q // 32 * 32 if b == 1 else 0
         for y0, y1, e in ((0, nv, "v"), (nv, n, "a")):
             if y1 > y0:
                 o0 = (rnd * NR + k) * NL + ((LB * x0 + b * n + y0) // 16 if quick else b * CC + (x0 + y0) // 16)
@@ -456,56 +435,46 @@ def build_ops(core, K, T, topo):
                 else:
                     add("a", lambda q, gt=gt, of=of: q.activation(AP(gt), AP(win).indirect(AP(of)), AF.Copy),
                         [win, of], [gt], (y1 - y0) * GA * CY + 0.065, cls=0)
-        for y0, y1 in ((0, n),) if n <= 512 else ((0, SPLIT), (SPLIT, n)):
+        for y0, y1 in ((0, n),) if n <= 512 else ((0, H), (H, n)):
             ps, to = R(slot(), 0, y1 - y0), R(dst[0], dst[3] + y0, dst[3] + y1)
             mm([(ps, R("pm", 384 * k + 128 * b, 384 * k + 128 * b + 128), R("gt", g0 + y0, g0 + y1), True, True)])
             tt(to, ps, R(ws, OWN[k] + x0 + y0, OWN[k] + x0 + y1) if b == 0 else to, AL.max)["beat"] = (y1 - y0) / Q
 
-    H, at = Q // 2, [0]
     coming = sorted((sum(p[2] - p[1] for p in last_round(r)[:i + 1]), via, r, h) for r in others for i, k, h, via in end_sends(r) if k == K)
-    late = []
+    late, at = [], [0]
 
     def done(rnd, k, x0, x1):
         if rnd < RO - 1:
+            spread(w[rnd + 1], k, x0, x1)
             if x1 == Q:
-                spread(w[rnd + 1], k)
-                for ks in BATCH[rnd + 1]:
-                    if ks[-1] == k:
-                        lists(rnd + 1, ks)
+                lists(rnd + 1, k)
             return
         at[0] += x1 - x0
         now = ops[-1]
         if k != K:
-            xs = [to_helper(R("res", k * Q + h * H, k * Q + h * H + H), near) if via else
+            send([to_helper(R("res", k * Q + h * H, k * Q + h * H + H), near) if via else
                   ([T.cores[k]], far, "ae%d" % (2 * K + h), R("res", k * Q + h * H, k * Q + h * H + H), R("land", K * Q + h * H, K * Q + h * H + H))
-                  for i, kk, h, via in end_sends(K) if kk == k and x0 <= h * H < x1]
-            for call in [xs] if END_VIA else [[x] for x in xs]:
-                send(call)
+                  for i, kk, h, via in end_sends(K) if kk == k and x0 <= h * H < x1])
         while coming and coming[0][0] <= at[0]:
             pos, via, r, h = coming.pop(0)
-            arrival(R("land", r * Q + h * H, r * Q + h * H + H), "ae%d" % (2 * r + h), len(far), [now], RCALL + RLAT * (1.7 if via else 1.0))
-            late.append((pos + LAG * (1.7 if via else 1.0), r, h * H, h * H + H))
+            arrival(R("land", r * Q + h * H, r * Q + h * H + H), "ae%d" % (2 * r + h), len(far), [now], RCALL + RLAT * (RVIA if via else 1.0))
+            late.append((pos + LAG * (RVIA if via else 1.0), r, h * H, h * H + H))
         late.sort()
         while late and late[0][0] <= at[0]:
             decode("land", *late.pop(0)[1:])
         if k == K:
             decode("res", K, x0, x1)
 
-    pieces = [(0, NR - 1, 0, H), (0, NR - 1, H, Q)] + [(rnd, k, 0, Q) for rnd in range(RO - 1) for k in range(NR - 1, -1, -1)][1:]
+    pieces = [(0, NR - 1) + p for p in START[NR - 1]] + [(rnd, k, 0, Q) for rnd in range(RO - 1) for k in SWEEP[K]][1:]
+    if HALVE and K % 2:
+        pieces[-1:] = [pieces[-1][:2] + (0, H), pieces[-1][:2] + (H, Q)]
     pieces += [(RO - 1,) + p for p in last_round(K)]
     for z, p in enumerate(pieces):
-        if p[0] == 0 and 0 < p[1] <= NR - PERMS and p[3] == Q:
-            permutation(p[1] - 1, slot(), 0)
-        if STAGGER:
-            grow(*p, 0)
-        if z:
-            grow(*pieces[z - 1], 2)
-            done(*pieces[z - 1])
-        if not STAGGER:
-            grow(*p, 0)
-        grow(*p, 1)
-    grow(*pieces[-1], 2)
-    done(*pieces[-1])
+        if PERMS <= z < NR:
+            permutation(SWEEP[K][z], slot())
+        for b in range(LB):
+            grow(*p, b)
+        done(*p)
     for d in late:
         decode("land", *d[1:])
     return ops
@@ -519,7 +488,7 @@ def depends(ops):
         for r, wr in mine:
             for q, qw, a in hist.get(r[0], ()):
                 if r[0] in PSUM and a["eng"] != o["eng"]:
-                    hit = q[3] // 512 <= (r[4] - 1) // 512 and r[3] // 512 <= (q[4] - 1) // 512
+                    hit = True
                 else:
                     hit = (wr or qw) and q[1] < r[2] and r[1] < q[2] and q[3] < r[4] and r[3] < q[4] and not a["eng"] == o["eng"] == "t"
                 if hit:
@@ -535,7 +504,7 @@ def depends(ops):
                 o["deps"].update(groups[ops[d]["sem"]])
         o["order"] = o["deps"] | set(a["n"] for a in o["after"])
         if o["eng"] == "t":
-            for bk in set((r[0], z) for r in o["wr"] for z in (r[3] // 512, (r[4] - 1) // 512)):
+            for bk in set(r[0] for r in o["wr"]):
                 if bk in lastt:
                     o["order"].add(lastt[bk])
                 lastt[bk] = o["n"]
@@ -544,12 +513,11 @@ def depends(ops):
 
 def schedule(ops):
     n = len(ops)
-    pred = [o["order"] | set(a["n"] for a in o.get("behind", ())) for o in ops]
     succ = [[] for _ in ops]
-    for i in range(n):
-        for d in pred[i]:
-            succ[d].append(i)
-    left = [len(p) for p in pred]
+    for o in ops:
+        for d in o["order"]:
+            succ[d].append(o["n"])
+    left = [len(o["order"]) for o in ops]
     line = [i for i in range(n) if not left[i]]
     for i in line:
         for s in succ[i]:
@@ -568,13 +536,12 @@ def schedule(ops):
         if o.get("due", 0.0) < 0.0:
             due[i] = o["due"]
     for i in range(n):
-        due[i] -= AHEAD[ops[i]["eng"]] if ops[i].get("chain") else 0.0
-    left, ready, free, dfree, seq = [len(p) for p in pred], {}, {}, 0.0, []
+        due[i] -= AHEAD.get(ops[i]["eng"], 0.0) * ops[i].get("chain", 0.0)
+    left, ready, free, dfree, seq = [len(o["order"]) for o in ops], {}, {}, 0.0, []
 
     def release(i):
         o = ops[i]
-        ready[i] = max([o.get("tmin", 0.0)] + [ops[d]["fin"] + o.get("lat", LAT if d in o["deps"] else 0.0) if d in o["order"] else ops[d]["st"]
-                                              for d in pred[i]])
+        ready[i] = max([o.get("tmin", 0.0)] + [ops[d]["fin"] + o.get("lat", LAT if d in o["deps"] else 0.0) for d in o["order"]])
     for i in range(n):
         if not left[i]:
             release(i)
@@ -585,7 +552,6 @@ def schedule(ops):
         o = ops[i]
         del ready[i]
         seq.append(i)
-        o["st"] = can[i]
         free[o["eng"]] = o["fin"] = can[i] + o["dur"]
         if o["kind"] == "d":
             dfree = o["fin"] = max(o["fin"] + DLAT, dfree) + o["nbytes"] / DBW + 0.05

import math
from concourse.bass import DstId, RemoteDMATransfer
from concourse.mybir import AluOpType as AL, ActivationFunctionType as AF

V, CAP, LB, RO, NR = 3072, 256, 3, 3, 4
ALPHA = math.log(2.0) / 98.0
PHASE = 0.00196
MID = 6144
KI = 1.0 / ALPHA
LNS = math.exp(0.0000192 - PHASE)
ROUND = 12582912.0
Q = V // 4
H = Q // 2
CC = Q // 16
NL = LB * CC
GAP = 3 * Q + 16
OWN = [16 + k * (V + GAP) for k in range(NR + 1)]
BEG = [0] + [c - GAP for c in OWN[1:]]
WW = OWN[NR] + 16
CB, BIG = 130.0, 32768.0
START = [[(0, Q)], [(0, Q)], [(0, H), (H, Q)], [(0, H), (H, Q)]]
CALLS = [[[(dd, 0, int(dd == 1))] for dd in (1, 2, 3)]] * 2 + [[[(dd, h, int(h == 0 and dd < 3))] for h in (0, 1) for dd in (1, 2, 3)]] * 2
SWEEP = [[3, 2, 1, 0], [3, 2, 0, 1], [3, 2, 1, 0], [3, 2, 0, 1]]
LAST = [[2, 1, 3], [3, 0, 2], [3, 1, 0], [2, 0, 1]]
CUTS = [0, 256, 512, Q]
END_VIA = 1
DVE_GATHER = [416, 416, 512]
LOADS_A = 3
PERMS = 4
NSLOT, NLT, NG = 3, 4, 6
LAG = 1200
DIRECT = 256
ON_ACT = ""
OWN_LAST = 0
FIRST, AHEAD0, SPREAD1 = 0.0, 1.0, 3.0
OWN_LIST = False
HALVE = False
PAIR = True
PKEEP = False
WHOLE = False

SB = lambda n, dt: ("sbuf", [128, n], dt)
F32, B16, I32, U16 = "float32", "bfloat16", "int32", "uint16"
SCRATCH = {
    "raw": SB(V, I32), "rawf": SB(V, F32), "rta": SB(16, I32), "rtb": SB(16, B16), "rtc": SB(16, F32), "enc": SB(V, B16), "land": SB(V, B16),
    "w0": SB(WW, B16), "w1": SB(WW, B16), "w2": SB(WW, B16), "res": SB(V, B16), "gt": SB(NG * Q, B16), "off": SB(RO * NR * NL, U16),
    "lt": SB(384, F32), "lc": SB(NLT * 384, B16), "lv": SB(2 * NLT * NL, F32), "cls": SB(3 * NL, B16), "hh": SB(9 * NL, B16),
    "rl": SB(8 * NL, B16), "ee": SB(6 * CC, B16), "xa": SB(NL, F32), "yf": SB(V, F32), "ones": SB(128, B16), "f16": SB(128, B16),
    "c256": SB(2 * CC, F32), "fio": SB(144, B16), "col": SB(8, F32), "pint": SB(8, I32), "sel": SB(24, B16), "rep": SB(128, B16),
    "jw": SB(240, B16), "jc": SB(144, B16), "bl": SB(128, B16), "bc": SB(9 * 128, B16), "negi": SB(224, B16), "gapi": SB(128, B16),
    "kid": SB(128, F32), "pt": SB(NR * 384, B16), "pm": SB(NR * 384, B16),
}
PSUM = ["p%d" % i for i in range(8)]
SCRATCH.update((p, ("psum", [128, 512], F32)) for p in PSUM)
SEMAPHORES = (["cp", "cv", "ca", "ct", "sent", "ar"] + ["d%d" % i for i in range(40)]
              + ["as%d" % i for i in range(8)] + ["ae%d" % i for i in range(8)] + ["h%d" % i for i in range(8)])

CY, PCY, GA = 0.00083 * 1.2, 0.00042 * 1.2, 1.75
LAT, DLAT, DBW, RLAT, RCALL, RVIA = 0.25, 1.9, 300e3, 4.5, 0.7, 1.7
ARRIVE, RELAY = [[14.0], [14.0], [11.0, 13.0], [10.0, 12.0]], 1.5
BEAT, DBEAT, HOP, LOOK, TAIL, AHEAD = 1.4, 0.2, 0.3, 0.1, 6.0, {"a": 1.5, "v": 1.5, "t": 1.5}


def last_round(K):
    a, b, c = LAST[K]
    return [(a, 0, Q), (b, 0, H), (b, H, Q), (c, 0, H), (c, H, Q)] + [(K, x0, x1) for x0, x1 in zip(CUTS, CUTS[1:])]


def end_sends(K):
    return [(i, k, h, h == 0 and i < END_VIA) for i, (k, x0, x1) in enumerate(last_round(K)) if k != K for h in range(x0 // H, x1 // H)]


def helpers_of(core, topo):
    return [c for c in topo.cores_of(core) if topo.die(c) != topo.die(core)]


def hand_ons(K):
    jobs = []
    for call in CALLS[K]:
        via = [c for c in call if c[2]]
        for dd, h, z in via:
            x0, x1 = START[K][h]
            jobs.append((z - 1, len(via), (K + dd) % NR, "as%d" % (2 * K + h), "enc", dd * Q + x0, dd * Q + x1, "w0", OWN[K] + x0))
    for i, k, h, via in end_sends(K):
        if via:
            jobs.append((0, 1, k, "ae%d" % (2 * K + h), "res", k * Q + h * H, k * Q + h * H + H, "land", K * Q + h * H))
    return [(j[0], "h%d" % n) + j[1:] for n, j in enumerate(jobs)]


def helper_program(g, core, owner, z, T, topo):
    K, n = T.rank_of(owner), 0
    far = set(topo.engines(owner, T.cores[(K + 1) % NR]))
    near = len([e for e in topo.engines(owner, core) if e not in far])
    for hz, hs, share, k, arr, src, c0, c1, dst, d0 in hand_ons(K):
        if hz == z:
            to = T.cores[k]
            g.wait_ge(T.sem[hs], near // share)
            g.remote_dma(T[dst][:, d0:d0 + c1 - c0], T[src][:, c0:c1], T.sem[arr], T.sem.sent, topo.addr(to)[1], topo.addr(to)[0], topo.mask(core, to))
            n += len(topo.engines(core, to))
    if n:
        g.wait_ge(T.sem.sent, n)


def start_engines(r, dd, h, nfar):
    call = [c for c in CALLS[r] if (dd, h, 0) in c]
    return nfar // len([x for x in call[0] if not x[2]]) if call else nfar


def build_ops(core, K, T, topo):
    ops, sends, count = [], [], {}

    def turn(name, n):
        count[name] = count.get(name, -1) + 1
        return count[name] % n

    newsem = lambda: "d%d" % turn("sem", 40)
    slot = lambda: PSUM[turn("slot", NSLOT)]
    keep = lambda: PSUM[NSLOT + turn("keep", len(PSUM) - NSLOT)]

    def R(name, c0, c1, p0=0, p1=128):
        return (name, p0, p1, c0, c1)

    def AP(r):
        return T[r[0]][r[1]:r[2], r[3]:r[4]] if isinstance(r, tuple) else r

    def add(eng, fn, rd, wr, dur, kind="c", **kw):
        o = dict(eng=eng, fn=fn, rd=[r for r in rd if isinstance(r, tuple)], wr=wr, dur=dur, kind=kind, n=len(ops), after=[], cls=-1)
        o.update(kw)
        ops.append(o)
        return o

    def wd(r):
        return r[4] - r[3]

    def vec(fn, rd, wr, cyc):
        return add("v", fn, rd, wr, max(64, cyc) * CY + 0.04)

    def act(out, src, func, bias=0.0, scale=1.0):
        return add("a", lambda q: q.activation(AP(out), AP(src), func, bias=AP(bias), scale=scale), [src, bias], [out], max(64, wd(src)) * CY + 0.06)

    def memset(r, val):
        return vec(lambda q: q.memset(AP(r), val), [], [r], wd(r) // 2)

    def ts(out, src, s1, s2, o0, o1=None, half=False):
        def fn(q):
            if o1 is None:
                return q.tensor_scalar(AP(out), AP(src), AP(s1), None, o0)
            return q.tensor_scalar(AP(out), AP(src), AP(s1), AP(s2), o0, o1)
        return vec(fn, [src, s1, s2], [out], wd(src) // 2 if half else wd(src))

    def tt(out, a, b, op):
        return vec(lambda q: q.tensor_tensor(AP(out), AP(a), AP(b), op), [a, b], [out], wd(a) * (1 if a[0] in PSUM else 2))

    def cp(out, src):
        return vec(lambda q: q.tensor_copy(AP(out), AP(src)), [src], [out], wd(src))

    def mm(items, rd=(), wr=None, cyc=None):
        def fn(q):
            return [q.matmul(AP(o), AP(l), AP(r), st, sp) for o, l, r, st, sp in items][-1]
        return add("t", fn, list(set([x for it in items for x in it[1:3] if isinstance(x, tuple)])) + list(rd),
                   wr or list(set(it[0] for it in items)), (cyc or sum(max(64, wd(it[0])) for it in items)) * PCY + 0.05, cls=1)

    def group(out, terms):
        return [(out, l, r, z == 0, z == len(terms) - 1) for z, (l, r) in enumerate(terms)]

    def iota(out, ap, pat):
        return add("p", lambda q: q.iota(ap, pat, 0, 0, allow_small_or_imprecise_dtypes=True), [], out, 0.13 + 2 * sum(wd(r) for r in out) * CY)

    def select(out, src, pat, op, fill, base, cm):
        return add("p", lambda q: q.affine_select(AP(out), AP(src), pat, op, fill, base, cm), [src], [out], 0.17 + 2 * wd(out) * CY)

    def dma(eng, out, src, nbytes, sem):
        return add(eng, lambda q: q.dma_start(AP(out), AP(src)), [src], [out] if isinstance(out, tuple) else [], 0.1, kind="d", sem=sem, nbytes=nbytes)

    hel = helpers_of(core, topo)
    far = topo.engines(core, T.cores[(K + 1) % NR])
    near = [e for e in topo.engines(core, hel[0]) if e not in set(far)]
    jobs = hand_ons(K)

    def send(xs):
        def fn(q):
            return q.remote_dma_fused([RemoteDMATransfer(dst_ids=[DstId(rid=topo.addr(c)[0], pnc=topo.addr(c)[1]) for c in to],
                                                         dma_engine_mask=sum(1 << e for e in engs), remote_sem=T.sem[sem],
                                                         srcs=[AP(src)], dsts=[AP(dst)] * len(to)) for to, engs, sem, src, dst in xs], local_sem=T.sem.sent)
        o = add("p", fn, [x[3] for x in xs], [], RCALL, kind="r", cnt=sum(len(x[1]) for x in xs))
        o["after"] += sends[-1:]
        sends.append(o)
        return o

    def arrival(dst, sem, cnt, after, lat, tmin=0.0):
        o = add("x" + sem, None, [], [dst], 0.01, kind="x", sem=sem, cnt=cnt, lat=lat, tmin=tmin)
        o["after"] += after

    def to_helper(src, engs):
        hz, hs = [j[:2] for j in jobs if (j[5], j[6]) == (src[0], src[3])][0]
        return ([hel[hz]], engs, hs, src, src)

    others = [(K + dd) % NR for dd in (1, 2, 3)]
    mine = R("rta", LB * K, LB * K + LB)
    dma("s", mine, T.rights[:, :], 2000, newsem())["due"] = -61.0
    first = send([([T.cores[k] for k in others], far, "ar", mine, mine)])
    first["due"] = -60.0

    col = lambda j: R("col", j, j + 1)
    ones, fio, negi, gapi, kid, w = R("ones", 0, 128), R("fio", 0, 128), R("negi", 0, 128), R("gapi", 0, 128), R("kid", 0, 128), ("w0", "w1", "w2")
    pi0, pi1, pi2, c256 = R("pint", 0, 1), R("pint", 1, 2), R("pint", 2, 3), R("c256", 0, 2 * CC)
    memset(ones, 1.0)
    memset(c256, 0.0)
    o = act(c256, c256, AF.Exp, math.log(CAP))
    o["dur"], o["due"] = o["dur"] + 1.3, -50.0
    add("p", lambda q: q.iota(AP(pi0), [[1, 1]], 0, 1), [], [pi0], 0.14)
    iota([R("fio", 0, 144)], T.fio[:, :], [[1, 144]])
    iota([R("f16", 0, 128)], T.f16[:, :], [[16, 8], [0, 16]])
    select(R("rep", 0, 128), ones, [[0, 4], [-1, 32]], AL.is_equal, 0.0, -32 * K, 1)
    select(R("sel", 0, 24), R("ones", 0, 24), [[-1, 3], [-16, 8]], AL.is_equal, 0.0, 0, 1)
    cp(col(0), pi0)
    ts(pi1, pi0, 112, None, AL.bitwise_and)
    ts(pi2, pi0, 96, None, AL.bitwise_and)
    cp(col(1), pi1)
    for k in range(NR):
        ts(col(2 + k), pi2, -Q / 32.0, MID + 16 - BEG[k] + (k * GAP if k == NR - 1 else -CB * GAP), AL.mult, AL.add)
    ts(col(6), pi2, -Q / 32.0, float(MID - 3 * V), AL.mult, AL.add)
    ts(negi, fio, col(0), -BIG, AL.is_equal, AL.mult, half=True)
    memset(R("negi", 128, 224), 0.0)
    ts(kid, fio, col(0), KI, AL.is_equal, AL.mult)
    ts(gapi, fio, col(0), float(GAP), AL.is_equal, AL.mult, half=True)
    memset(R("jw", 0, 96), 0.0)
    ts(R("jw", 96, 240), R("fio", 0, 144), col(1), 16.0, AL.subtract, AL.is_equal, half=True)
    tt(R("jc", 0, 144), R("jw", 64, 208), R("jw", 32, 176), AL.add)
    tt(R("jc", 0, 144), R("jc", 0, 144), R("jw", 0, 144), AL.add)
    for nm in w:
        for p0, p1, c, step, n in [(0, 128, BEG[1], V + GAP, NR - 1), (0, 128, 0, 1, 1)] + [(32 * u, 32 * u + 32, OWN[NR - 1] + V - Q * u, GAP, 2) for u in range(4)]:
            ap, wr = T[nm][p0:p1, c:c + step * (n - 1) + 1:step], [R(nm, c + z * step, c + z * step + 1, p0, p1) for z in range(n)]
            if p1 - p0 < 128:
                add("a", lambda q, ap=ap, z=R("ones", 0, n, p0, p1): q.activation(ap, AP(z), AF.Copy, scale=0.0), [ones], wr, 0.125)
            else:
                iota(wr, ap, [[0, n]])
    bl = R("bl", 0, 128)
    select(bl, ones, [[1, 128]], AL.is_gt, 0.0, 0, -1)
    select(bl, bl, [[-16, 8], [0, 16]], AL.is_ge, 0.0, 0, 1)
    select(bl, bl, [[1, 128]], AL.not_equal, 32.0, 0, -1)
    for z in range(9):
        ts(R("bc", 128 * z, 128 * z + 128), R("f16", 0, 128), col(0), -float(z), AL.subtract, AL.is_equal, half=True)

    order = [(h, dd) for call in CALLS[K] for dd, h, via in call]
    own = [(h, 0) for h in range(len(START[K]))]
    exps = []
    for z, (h, dd) in enumerate(order + own if K >= OWN_LAST else own + order):
        (x0, x1), d, sem = START[K][h], (K + dd) % NR, newsem()
        raw, rf = R("raw", dd * Q + x0, dd * Q + x1), R("rawf", dd * Q + x0, dd * Q + x1)
        for u in range(4):
            dma("sa"[u % 2] if z < LOADS_A else "s", R("raw", raw[3], raw[4], 32 * u, 32 * u + 32), T.ends[32 * d:32 * d + 32, u * Q + x0:u * Q + x1],
                128 * wd(raw), sem)["due"] = -59.0 + 0.1 * (4 * z + u)
        ts(rf, raw, float(MID), None, AL.subtract)["due"] = -45.0 + 0.1 * z
        exps.append(act(R("enc", raw[3], raw[4]) if dd else R("w0", OWN[K] + x0, OWN[K] + x1), rf, AF.Exp, PHASE, ALPHA))
        exps[-1]["due"] = -45.0 + 0.1 * z
    tile = lambda r, h: R("w0", OWN[r] + START[r][h][0], OWN[r] + START[r][h][1])

    def arrive(r, after):
        for h in range(len(START[r])):
            arrival(tile(r, h), "as%d" % (2 * r + h), start_engines(r, (K - r) % NR, h, len(far)), after, 0.1,
                    ARRIVE[r][h] + (RELAY if ((K - r) % NR, h, 1) in sum(CALLS[r], []) else 0.0))
    for r in range(K + 1, NR):
        arrive(r, [first])
    for z, call in enumerate(CALLS[K]):
        xs, e0, n0 = [], 0, 0
        for dd, h, via in call:
            src = R("enc", dd * Q + START[K][h][0], dd * Q + START[K][h][1])
            if via:
                n = len(near) // len([x for x in call if x[2]])
                xs.append(to_helper(src, near[n0:n0 + n]))
                n0 += n
            else:
                n = start_engines(K, dd, h, len(far))
                xs.append(([T.cores[(K + dd) % NR]], far[e0:e0 + n], "as%d" % (2 * K + h), src, tile(K, h)))
                e0 += n
        send(xs)["due"] = -40.0 + z
    for r in range(K):
        arrive(r, sends[-1:])

    arrival(R("rta", 0, LB * NR), "ar", 3 * len(far), [first], RLAT)
    cp(R("rtb", 0, 12), R("rta", 0, 12))
    z = R(slot(), 0, 12)
    mm([(z, R("rep", 0, 128), R("rtb", 0, 12), True, True)])
    cp(R("rtc", 0, 12), z)
    for r in range(NR - 1, -1, -1):
        for b in range(LB):
            ts(R("pt", 384 * r + 128 * b, 384 * r + 128 * b + 128), fio, col(1), R("rtc", LB * r + b, LB * r + b + 1), AL.subtract, AL.is_equal, half=True)

    def permutation(r, bank):
        mm([(R(bank, 128 * b, 128 * b + 128), R("pt", 384 * r + 128 * b, 384 * r + 128 * b + 128), negi, True, True) for b in range(LB)])
        ts(R("pm", 384 * r, 384 * r + 384), R(bank, 0, 384), -1.0 / BIG, None, AL.mult)

    def spread(wn, k, x0=0, x1=Q, first=False):
        sem, c, m = newsem(), OWN[k] + x0, x1 - x0
        for h, (y0, y1) in enumerate(START[k] if first else [(0, m)]):
            for j in (1, 2, 3):
                to, n = R(wn, c + j * Q + y0, c + j * Q + y1, 0, 128 - 32 * j), y1 - y0
                if not first:
                    dma("s", to, R(wn, c + y0, c + y1, 32 * j, 128), (128 - 32 * j) * n * 2, sem)
                    continue
                bank = keep() if h else slot()
                mm([(R(bank, 0, n), R("negi", 32 * j, 32 * j + 128), R(wn, c + y0, c + y1), True, True)])
                if (j + h) % 2:
                    ts(to, R(bank, 0, n, 0, 128 - 32 * j), -1.0 / BIG, None, AL.mult)
                else:
                    act(to, R(bank, 0, n, 0, 128 - 32 * j), AF.Copy, scale=-1.0 / BIG)
                ops[-1]["due"] = ops[-2]["due"] = -27.0 + h + 0.1 * j
        if k:
            sem = newsem() if first else sem
            for j in (1, 2, 3):
                dma("s", R(wn, c - j * Q, c - j * Q + m, 32 * j, 128), R(wn, c, c + m, 0, 128 - 32 * j), (128 - 32 * j) * m * 2, sem)

    lns = []

    def ln(out, src, scale):
        o = act(out, src, AF.Ln, scale=scale)
        if not lns:
            o["dur"], o["due"] = o["dur"] + 1.5, -30.0
        o["after"] += exps + lns[:1]
        lns.append(o)
    memset(col(7), math.exp(ALPHA * (0.5 - MID)))
    ln(col(7), col(7), 1.0)

    def left_rows(bank, wn, c0, n, i0, i1, p0=0):
        mm([(T[bank][p0:p0 + n // 16, i:384:16], T[wn][:, c0 + i:c0 + n:16], R("sel", 0, 24), True, True) for i in range(i0, i1)],
           [R(wn, c0, c0 + n)], [R(bank, 0, 384, p0, p0 + n // 16)], (i1 - i0) * n // 16)

    def first_lists():
        for h, (x0, x1) in enumerate(START[NR - 1]):
            bank, p0, c, n0 = keep(), 64 * h, (x1 - x0) // 16, len(ops)
            left_rows(bank, "w0", OWN[NR - 1] + x0, x1 - x0, 0, 16)
            ln(R("lt", 0, 384, p0, p0 + c), R(bank, 0, 384, 0, c), LNS)
            mm([(R(bank, b * c, (b + 1) * c), R("lt", 128 * b, 128 * b + 128, p0, p0 + c), R("kid", p0, p0 + c, p0, p0 + c), True, True) for b in range(LB)], cyc=256 * LB)
            xa = R("xa", LB * x0 // 16, LB * x1 // 16)
            act(xa, R(bank, 0, LB * c), AF.Abs)
            ts(R("off", (NR - 1) * NL + xa[3], (NR - 1) * NL + xa[4]), xa, col(6), None, AL.add)
            for o in ops[n0:]:
                o["due"] = -28.0 + SPREAD1 * h

    def counted_lists(rnd, k):
        par, wb = turn("list", NLT), keep()
        ks = [k, NR - 1] if PAIR and rnd and k == NR - 2 else [k]
        lc, l0, top = 384 * par, 2 * NL * par, 64 * len(ks) - 16
        if len(ks) > 1:
            mm([(R(wb, 0, 384, 32, 64), R("ones", 0, 32), R("bc", 0, 384), True, True)])
        for h, kk in enumerate(ks):
            for i0 in (0, 8):
                left_rows(wb, w[rnd], OWN[kk], Q, i0, i0 + 8, 64 * h)
        act(R("lc", lc, lc + 384, 0, top), R(wb, 0, 384, 0, top), AF.Copy)
        for h in range(len(ks)):
            mm([(R(wb, h * NL + b * CC, h * NL + (b + 1) * CC), R("lc", lc + 128 * b, lc + 128 * b + 128, 0, top), R("gapi", 64 * h, 64 * h + CC, 0, top), True, True)
                for b in range(LB)])
        ln(R("lv", l0, l0 + len(ks) * NL), R(wb, 0, len(ks) * NL), LNS / GAP)
        lv, off = R("lv", l0, l0 + NL), R("off", (rnd * NR + k) * NL, (rnd * NR + k + 1) * NL)
        if ks[-1] == NR - 1:
            l1 = l0 + (len(ks) - 1) * NL
            ts(R("off", (rnd * NR + NR - 1) * NL, (rnd + 1) * NR * NL), R("lv", l1, l1 + NL), KI, col(1 + NR), AL.mult, AL.add)
            if k == NR - 1:
                return
        cl, hb, rb, eb, xh, nq = R("cls", k * NL, k * NL + NL), 3 * k * NL, 4 * (k % 2) * NL, 2 * k * CC, R(keep(), 0, NL), NR - 1 - k
        ts(cl, lv, KI / V, CB - 0.5 + (MID + 0.5) / V, AL.mult, AL.add)
        for z in range(nq):
            ts(R("hh", hb + z * NL, hb + z * NL + NL), cl, CB + k + 1 + z, None, AL.is_equal, half=True)
        hq = [R("hh", hb + z * CC, hb + z * CC + CC) for z in range(nq * LB)]
        mm(group(R(wb, 400, 400 + CC), [(R("jc", 16 - z, 144 - z), s) for z, s in enumerate(hq)]))
        mm(group(R(wb, 400 + CC, 400 + 2 * CC), [(R("jw", 112 - z, 240 - z), s) for z, s in enumerate(hq)]))
        cs, eo, ex = R(wb, 400, 399 + 2 * CC), R("ee", eb, eb + 2 * CC - 1), R("ee", eb + CC - 1, eb + 2 * CC - 1)
        vec(lambda q: q.tensor_tensor_scan(AP(eo), AP(cs), T.c256[:, 0:2 * CC - 1], 0.0, AL.add, AL.min), [cs, c256], [eo], 2 * CC)
        mm([(xh, gapi, cl, True, False), (xh, kid, lv, False, False)], cyc=5 * NL)
        if k == 0:
            ts(R("rl", rb + nq * NL, rb + nq * NL + NL), lv, col(7), None, AL.is_lt)
        for z0 in range(nq):
            mm([(R(wb, z0 * NL, z0 * NL + NL), bl, R("hh", hb + z0 * NL, hb + z0 * NL + NL), True, False)]
               + [(R(wb, z * CC, (z + 1) * CC), R("bc", 128 * z, 128 * z + 128), ex, False, z % LB == LB - 1) for z in range(z0 * LB, z0 * LB + LB)])
        if "r" in ON_ACT:
            act(R("rl", rb, rb + nq * NL), R(wb, 0, nq * NL), AF.Relu, -(CAP + 31.0))
        else:
            ts(R("rl", rb, rb + nq * NL), R(wb, 0, nq * NL), CAP + 32.0, None, AL.is_ge)
        nq += k == 0
        mm([(xh, negi, R("rl", rb + z * NL, rb + (z + 1) * NL), False, z == nq - 1) for z in range(nq)])
        ts(off, xh, col(2 + k), None, AL.add)

    def lists(rnd, k):
        n0 = len(ops)
        if rnd == 0 and k == NR - 1:
            first_lists()
        elif k < NR - 1 or not PAIR:
            counted_lists(rnd, k)
        for o in ops[n0:]:
            o["chain"] = FIRST if rnd == 0 and k == NR - 1 else AHEAD0 if rnd == 0 else 1.0

    early = [K] if OWN_LIST and K < NR - 1 else []
    for k in early:
        lists(0, k)
    for r in SWEEP[K][:PERMS]:
        permutation(r, keep() if PKEEP else slot())
    for k in range(NR - 1, -1, -1):
        spread("w0", k, first=k == NR - 1)
    for k in sorted(SWEEP[K], key=lambda k: (k != NR - 1, k != K)):
        if k not in early:
            lists(0, k)
    s_y = newsem()

    def decode(src, r, x0, x1):
        a, e = r * Q + x0, r * Q + x1
        act(R("rawf", a, e), R(src, a, e), AF.Ln, scale=LNS)
        if e - a <= DIRECT:
            ts(R("yf", a, e), R("rawf", a, e), KI, ROUND + MID, AL.mult, AL.add)
            ts(R("yf", a, e), R("yf", a, e), ROUND, None, AL.subtract)
        else:
            z = R(keep(), 0, e - a)
            mm([(z, kid, R("rawf", a, e), True, True)], cyc=4 * (e - a))
            ts(R("yf", a, e), z, ROUND + MID, ROUND, AL.add, AL.subtract)
        ops[-1]["beat"] = DBEAT
        if WHOLE and src == "land":
            if turn("half%d" % r, 2) == 0:
                return
            x0, x1, a, e = 0, Q, r * Q, r * Q + Q
        for u in range(4):
            dma("s", T.y[32 * r:32 * r + 32, u * Q + x0:u * Q + x1], R("yf", a, e, 32 * u, 32 * u + 32), 128 * (e - a), s_y)

    def grow(rnd, k, x0, x1, b):
        ws, n, quick = w[rnd], x1 - x0, rnd == 0 and k == NR - 1
        win = R(ws, OWN[k] if quick else BEG[k], OWN[k] + V + 16 if k == NR - 1 else WW)
        dst = R("res", k * Q + x0, k * Q + x1) if rnd == RO - 1 else R(w[rnd + 1], OWN[k] + x0, OWN[k] + x1)
        g0 = turn("gather", NG) * Q
        nv = DVE_GATHER[rnd] * n // Q // 32 * 32 if b == 1 else 0
        for y0, y1, e in ((0, nv, "v"), (nv, n, "a")):
            if y1 > y0:
                o0 = (rnd * NR + k) * NL + ((LB * x0 + b * n + y0) // 16 if quick else b * CC + (x0 + y0) // 16)
                gt, of = R("gt", g0 + y0, g0 + y1), R("off", o0, o0 + (y1 - y0) // 16)
                if e == "v":
                    vec(lambda q, gt=gt, of=of: q.tensor_copy(AP(gt), AP(win).indirect(AP(of))), [win, of], [gt], (y1 - y0) * GA)["cls"] = 0
                else:
                    add("a", lambda q, gt=gt, of=of: q.activation(AP(gt), AP(win).indirect(AP(of)), AF.Copy),
                        [win, of], [gt], (y1 - y0) * GA * CY + 0.065, cls=0)
        for y0, y1 in ((0, n),) if n <= 512 else ((0, H), (H, n)):
            ps, to = R(slot(), 0, y1 - y0), R(dst[0], dst[3] + y0, dst[3] + y1)
            mm([(ps, R("pm", 384 * k + 128 * b, 384 * k + 128 * b + 128), R("gt", g0 + y0, g0 + y1), True, True)])
            tt(to, ps, R(ws, OWN[k] + x0 + y0, OWN[k] + x0 + y1) if b == 0 else to, AL.max)["beat"] = (y1 - y0) / Q

    coming = sorted((sum(p[2] - p[1] for p in last_round(r)[:i + 1]), via, r, h) for r in others for i, k, h, via in end_sends(r) if k == K)
    late, at = [], [0]

    def done(rnd, k, x0, x1):
        if rnd < RO - 1:
            spread(w[rnd + 1], k, x0, x1)
            if x1 == Q:
                lists(rnd + 1, k)
            return
        at[0] += x1 - x0
        now = ops[-1]
        if k != K:
            send([to_helper(R("res", k * Q + h * H, k * Q + h * H + H), near) if via else
                  ([T.cores[k]], far, "ae%d" % (2 * K + h), R("res", k * Q + h * H, k * Q + h * H + H), R("land", K * Q + h * H, K * Q + h * H + H))
                  for i, kk, h, via in end_sends(K) if kk == k and x0 <= h * H < x1])
        while coming and coming[0][0] <= at[0]:
            pos, via, r, h = coming.pop(0)
            arrival(R("land", r * Q + h * H, r * Q + h * H + H), "ae%d" % (2 * r + h), len(far), [now], RCALL + RLAT * (RVIA if via else 1.0))
            late.append((pos + LAG * (RVIA if via else 1.0), r, h * H, h * H + H))
        late.sort()
        while late and late[0][0] <= at[0]:
            decode("land", *late.pop(0)[1:])
        if k == K:
            decode("res", K, x0, x1)

    pieces = [(0, NR - 1) + p for p in START[NR - 1]] + [(rnd, k, 0, Q) for rnd in range(RO - 1) for k in SWEEP[K]][1:]
    if HALVE and K % 2:
        pieces[-1:] = [pieces[-1][:2] + (0, H), pieces[-1][:2] + (H, Q)]
    pieces += [(RO - 1,) + p for p in last_round(K)]
    for z, p in enumerate(pieces):
        if PERMS <= z < NR:
            permutation(SWEEP[K][z], slot())
        for b in range(LB):
            grow(*p, b)
        done(*p)
    for d in late:
        decode("land", *d[1:])
    return ops


def depends(ops):
    hist, groups, lastt = {}, {}, {}
    for o in ops:
        deps = set()
        mine = [(r, False) for r in o["rd"]] + [(r, True) for r in o["wr"]]
        for r, wr in mine:
            for q, qw, a in hist.get(r[0], ()):
                if r[0] in PSUM and a["eng"] != o["eng"]:
                    hit = True
                else:
                    hit = (wr or qw) and q[1] < r[2] and r[1] < q[2] and q[3] < r[4] and r[3] < q[4] and not a["eng"] == o["eng"] == "t"
                if hit:
                    deps.add(a["n"])
        for r, wr in mine:
            hist.setdefault(r[0], []).append((r, wr, o))
        o["deps"] = deps
        if o["kind"] == "d":
            groups.setdefault(o["sem"], []).append(o["n"])
    for o in ops:
        for d in list(o["deps"]):
            if ops[d]["kind"] == "d":
                o["deps"].update(groups[ops[d]["sem"]])
        o["order"] = o["deps"] | set(a["n"] for a in o["after"])
        if o["eng"] == "t":
            for bk in set(r[0] for r in o["wr"]):
                if bk in lastt:
                    o["order"].add(lastt[bk])
                lastt[bk] = o["n"]
    return groups


def schedule(ops):
    n = len(ops)
    succ = [[] for _ in ops]
    for o in ops:
        for d in o["order"]:
            succ[d].append(o["n"])
    left = [len(o["order"]) for o in ops]
    line = [i for i in range(n) if not left[i]]
    for i in line:
        for s in succ[i]:
            left[s] -= 1
            if not left[s]:
                line.append(s)
    t, due = 0.0, [0.0] * n
    for o in ops:
        if "beat" in o:
            t += o["beat"] * BEAT
            o["due"] = t
    for i in reversed(line):
        o = ops[i]
        e = min([due[s] - ops[s].get("lat", HOP if ops[s]["eng"] != o["eng"] else 0.0) for s in succ[i]] + [o.get("due", t + TAIL)])
        due[i] = e - o["dur"] - (DLAT + o["nbytes"] / DBW if o["kind"] == "d" else 0.0)
        if o.get("due", 0.0) < 0.0:
            due[i] = o["due"]
    for i in range(n):
        due[i] -= AHEAD.get(ops[i]["eng"], 0.0) * ops[i].get("chain", 0.0)
    left, ready, free, dfree, seq = [len(o["order"]) for o in ops], {}, {}, 0.0, []

    def release(i):
        o = ops[i]
        ready[i] = max([o.get("tmin", 0.0)] + [ops[d]["fin"] + o.get("lat", LAT if d in o["deps"] else 0.0) for d in o["order"]])
    for i in range(n):
        if not left[i]:
            release(i)
    while ready:
        can = dict((i, max(t, free.get(ops[i]["eng"], 0.0))) for i, t in ready.items())
        i0 = min(can, key=can.get)
        i = min((j for j in can if ops[j]["eng"] == ops[i0]["eng"] and can[j] <= can[i0] + LOOK), key=lambda j: due[j])
        o = ops[i]
        del ready[i]
        seq.append(i)
        free[o["eng"]] = o["fin"] = can[i] + o["dur"]
        if o["kind"] == "d":
            dfree = o["fin"] = max(o["fin"] + DLAT, dfree) + o["nbytes"] / DBW + 0.05
        for s in succ[i]:
            left[s] -= 1
            if not left[s]:
                release(s)
    return seq


def emit(g, T, ops, seq, groups):
    queue = {"p": g, "v": g.vector, "a": g.scalar, "t": g.tensor, "s": g.sync}
    need = set(d for o in ops for d in o["deps"])
    known = dict((e, {}) for e in queue)
    total = {}
    for i in seq:
        o = ops[i]
        if o["kind"] == "x":
            o["tok"], o["vc"] = (o["sem"], o["cnt"]), {}
            total[o["sem"]] = o["cnt"]
            continue
        q, kn, toks = queue[o["eng"]], known[o["eng"]], {}
        for d in o["deps"]:
            s, c = ops[d]["tok"]
            if c > toks.get(s, (0, 0))[0]:
                toks[s] = (c, d)
        for s, (c, d) in sorted(toks.items(), key=lambda kv: -ops[kv[1][1]]["fin"]):
            if kn.get(s, 0) < c:
                q.wait_ge(T.sem[s], c)
                kn[s] = c
                for m in (groups[s] if ops[d]["kind"] == "d" else [d]):
                    for s2, c2 in ops[m]["vc"].items():
                        kn[s2] = max(kn.get(s2, 0), c2)
        ins = o["fn"](q)
        o["vc"] = dict(kn)
        if o["kind"] == "d":
            ins.then_inc(T.sem[o["sem"]], 16)
            total[o["sem"]] = 16 * len(groups[o["sem"]])
            o["tok"] = (o["sem"], total[o["sem"]])
        elif o["kind"] == "r":
            total["sent"] = total.get("sent", 0) + o["cnt"]
        elif i in need:
            s = "c" + o["eng"]
            total[s] = total.get(s, 0) + 1
            ins.then_inc(T.sem[s], 1)
            o["tok"] = (s, total[s])
    for s, c in total.items():
        if max(kn.get(s, 0) for kn in known.values()) < c:
            g.wait_ge(T.sem[s], c)


def rank_program(g, core, T, topo):
    rank = T.rank_of(core)
    if rank is None:
        for owner in T.cores:
            if core in helpers_of(owner, topo):
                helper_program(g, core, owner, helpers_of(owner, topo).index(core), T, topo)
        return
    ops = build_ops(core, rank, T, topo)
    groups = depends(ops)
    emit(g, T, ops, schedule(ops), groups)
